import numpy as np
import ml_dtypes


def mxq(x, axis, fmt="e4m3"):
    dtype, down = {"e4m3": (ml_dtypes.float8_e4m3fn, 7), "e5m2": (ml_dtypes.float8_e5m2, 14)}[fmt]
    v = np.moveaxis(np.asarray(x, np.float32).astype(ml_dtypes.bfloat16).astype(np.float64), axis, -1)
    blocks = v.reshape(v.shape[:-1] + (-1, 32))
    amax = np.abs(blocks).max(-1, keepdims=True)
    byte = np.maximum(np.where(amax > 0, np.frexp(amax)[1] - 1 + 127, 0) - down, 1)
    scale = np.exp2(byte - 127.0)
    codes = (blocks / scale).astype(np.float32).astype(dtype).astype(np.float64)
    return np.moveaxis((codes * scale).reshape(v.shape), -1, axis)


WIDE = False


def mx_kscale(k):
    if not WIDE:
        return np.ones(k)
    levels = np.array([18, -18])
    if k % 512:
        return np.exp2(np.random.permutation(np.resize(levels, k // 32))).repeat(32)
    a = np.empty((k // 512, 16))
    for p in range(k // 512):
        a[p, :8] = np.random.permutation(np.resize(levels, 8))
        for g in range(8):
            far = levels[np.abs(levels - a[p, g]) >= 10]
            a[p, g + 8] = far[np.random.randint(len(far))]
    return np.exp2(a.ravel()).repeat(32)


def f64(x):
    return np.asarray(x).astype(np.float64)


def striped(idx):
    return np.tile(np.asarray(idx).reshape(-1, 16).T, (8, 1)).astype(np.uint16)


def unstriped(offs):
    return offs[:16].T.reshape(-1).astype(np.int64)

def planes(y):
    n, m = y.shape
    v = y.astype(np.float32).astype(ml_dtypes.bfloat16).astype(np.float64).reshape(n // 32, 32, m)
    top = np.abs(v).max(1)
    byte = np.clip(np.where(top > 0, np.frexp(top)[1] - 1 + 127 - 7, 1), 1, 254)
    codes = (v * np.exp2(127.0 - byte)[:, None, :]).reshape(n, m).astype(np.float32).astype(ml_dtypes.float8_e4m3fn).view(np.uint8)
    words = codes.reshape(n // 512, 128, 4, m).transpose(0, 1, 3, 2)
    return np.ascontiguousarray(words), np.ascontiguousarray(byte.astype(np.uint8).reshape(n // 512, 16, m))


def sig(x):
    return 1.0 / (1.0 + np.exp(-x))


def setup_inputs():
    n = np.random.standard_normal
    uni = np.random.uniform
    idx = np.random.permutation(1024)[:512]
    f_d = mx_kscale(512)
    f_f = mx_kscale(512)
    return {
        "xT": (n((512, 1024)) * f_d[:, None]).astype(np.float32),
        "dyT": (n((512, 1024)) / f_d[:, None]).astype(np.float32),
        "w1": (n((512, 512)) / np.sqrt(512) / f_d[:, None] * f_f[None, :]).astype(np.float32),
        "w2": (n((512, 512)) / np.sqrt(512) * f_d[:, None]).astype(np.float32),
        "cf": (uni(0.75, 1.3, (512, 1)) / f_f[:, None]).astype(np.float32),
        "gt": np.tile(uni(0.75, 1.3, 1024), (128, 1)).astype(np.float32),
        "tx": np.tile(uni(0.75, 1.3, 1024), (128, 1)).astype(np.float32),
        "c1": (uni(0.5, 1.5, (512, 1)) / np.sqrt(512)).astype(np.float32),
        "offs": striped(idx),
    }


def reference(xT, dyT, w1, w2, cf, gt, tx, c1, offs):
    idx = unstriped(offs)
    xT_i = f64(xT)[:, idx]
    dy = f64(dyT)[:, idx]
    gt_i = f64(gt)[:1][:, idx]
    tx_i = f64(tx)[:1][:, idx]
    a = mxq(f64(w1), 0, "e4m3").T @ mxq(xT_i, 0, "e4m3")
    dh = mxq(f64(w2), 0, "e4m3").T @ mxq(dy, 0, "e5m2")
    z = f64(cf) * tx_i * a
    da = f64(c1) * f64(cf) * tx_i * gt_i * dh * sig(z) * (1.0 + z * (1.0 - sig(z)))
    dx = mxq(f64(w1), 1, "e4m3") @ mxq(da, 0, "e5m2")
    nd = dy + dx
    out_0 = f64(dyT)
    out_0[:, idx] = nd
    return (out_0,) + planes(out_0)

@@ -1,0 +1,309 @@
+from contextlib import ExitStack
+
+import concourse.mybir as mybir
+from concourse.masks import make_identity
+
+F32 = mybir.dt.float32
+BF16 = mybir.dt.bfloat16
+I32 = mybir.dt.int32
+U32 = mybir.dt.uint32
+U16 = mybir.dt.uint16
+U8 = mybir.dt.uint8
+E4M3 = mybir.dt.float8_e4m3fn_x4
+E5M2 = mybir.dt.float8_e5m2_x4
+ALU = mybir.AluOpType
+ACT = mybir.ActivationFunctionType
+
+P = 128
+LANES = 4
+D = 512
+F = 512
+T = 1024
+N = 512
+CHUNKS = N // P
+SPLIT = 576
+FLOPS = 3 * 2 * 512 * 512 * 512
+
+
+def tile_attend_gdepth_sil_pl_kernel(tc, xT, dyT, w1, w2, cf, gt, tx, c1, offs, out_0, out_1, out_2):
+    nc = tc.nc
+    with ExitStack() as ctx:
+        keep = ctx.enter_context(tc.tile_pool(name="keep", bufs=1))
+        work = ctx.enter_context(tc.tile_pool(name="work", bufs=2))
+        psum = ctx.enter_context(tc.psum_pool(name="psum", bufs=2))
+
+        def held(name, shape, dtype):
+            return keep.tile(shape, dtype, name=name, align_bytes=64)
+
+        def bank(tag):
+            return psum.tile([P, 512], F32, name=tag, tag=tag)
+
+        offsets = keep.tile([P, N // 16], U16, name="offsets")
+        dy_rows = dyT.rearrange("(p t) n -> p t n", t=LANES)
+        x_rows = xT.rearrange("(p t) n -> p t n", t=LANES)
+        dy_pool = [held(f"dy_pool{t}", [P, T], F32) for t in range(LANES)]
+        out_plane = [held(f"out_plane{t}", [P, T], F32) for t in range(LANES)]
+        x_raw = [held(f"x_raw{u}", [P, 2, T], F32) for u in range(2)]
+        tx_pool = held("tx_pool", [P, T], F32)
+        gt_pool = held("gt_pool", [P, T], F32)
+        cf_col = held("cf_col", [P, LANES], F32)
+        c1_col = held("c1_col", [P, LANES], F32)
+        w1_raw = held("w1_raw", [P, LANES, F], F32)
+        w2_raw = held("w2_raw", [P, LANES, F], F32)
+
+        nc.sync.dma_start(offsets[:], offs)
+        nc.sync.dma_start(out=dy_pool[0][:], in_=dy_rows[:, 0, :])
+        nc.sync.dma_start(out=tx_pool[0:32, :], in_=tx[0:32, :])
+        nc.sync.dma_start(out=gt_pool[0:32, :], in_=gt[0:32, :])
+        nc.sync.dma_start(out=x_raw[0][:], in_=x_rows[:, 0:2, :])
+        nc.sync.dma_start(out=dy_pool[1][:], in_=dy_rows[:, 1, :])
+        nc.sync.dma_start(out=x_raw[1][:], in_=x_rows[:, 2:4, :])
+        nc.sync.dma_start(out=cf_col[:], in_=cf.rearrange("(p t) o -> p (t o)", t=LANES))
+        nc.sync.dma_start(out=c1_col[:], in_=c1.rearrange("(p t) o -> p (t o)", t=LANES))
+        nc.sync.dma_start(out=w1_raw[:], in_=w1.rearrange("(p j) f -> p j f", j=LANES))
+        nc.sync.dma_start(out=dy_pool[2][:], in_=dy_rows[:, 2, :])
+        nc.sync.dma_start(out=dy_pool[3][:], in_=dy_rows[:, 3, :])
+        nc.sync.dma_start(out=w2_raw[:], in_=w2.rearrange("(p j) f -> p j f", j=LANES))
+        for t in range(LANES):
+            nc.sync.dma_start(out=out_plane[t][:], in_=dy_rows[:, t, :])
+
+        ident = held("ident", [P, P], F32)
+        make_identity(nc, ident[:])
+        for pool_tile in (tx_pool, gt_pool):
+            nc.vector.memset(pool_tile[32:64, :], 0.0)
+            nc.vector.memset(pool_tile[64:128, :], 0.0)
+
+        dy_got = held("dy_got", [P, LANES, N], F32)
+
+        def gather_dy(t):
+            nc.vector.tensor_copy(out=dy_got[:, t, :], in_=dy_pool[t][:].indirect(offsets[:]))
+
+        x_words = held("x_words", [P, N * LANES], BF16)
+
+        def gather_x(u):
+            pairs = held(f"x_pairs{u}", [P, 2 * T], BF16)
+            nc.scalar.activation(
+                out=pairs[:].rearrange("p (c i e) -> p c e i", i=4, e=2),
+                in_=x_raw[u][:].rearrange("p e (c i) -> p c e i", i=4),
+                func=ACT.Copy,
+            )
+            nc.vector.tensor_copy(
+                out=x_words[:].bitcast(U32).rearrange("p (i u) -> p i u", u=2)[:, :, u],
+                in_=pairs[:].bitcast(U32).indirect(offsets[:]),
+            )
+
+        def quantize(name, values, fmt):
+            width = values.shape[1] // LANES
+            codes = held(name + "_codes", [P, width], U32)
+            scales = held(name + "_scales", [P, width], U8)
+            nc.vector.quantize_mx(out=codes[:].bitcast(fmt), scales=scales[:], in_=values)
+            return codes, scales
+
+        def round_weights(name, raw):
+            grouped = held(name, [P, F * LANES], BF16)
+            nc.scalar.copy(
+                out=grouped[:].rearrange("p (u m e j) -> p m j u e", u=2, e=2, j=LANES),
+                in_=raw[:].rearrange("p j (m u e) -> p m j u e", u=2, e=2),
+            )
+            return grouped
+
+        def token_columns(name, pool_tile):
+            got = held(name, [P, N], F32)
+            nc.vector.tensor_copy(out=got[:], in_=pool_tile[:].indirect(offsets[:]))
+            turned = bank("misc")
+            for c in range(CHUNKS):
+                nc.tensor.transpose(turned[:, c * P : (c + 1) * P], got[:, c * P : (c + 1) * P], ident[:])
+            return turned[:].rearrange("p (c r) -> p c r", r=P)[:, :, 0]
+
+        def spread_row(name, col):
+            turned = bank("misc")
+            for t in range(LANES):
+                nc.tensor.transpose(turned[:, t * P : (t + 1) * P], col[:, t : t + 1].to_broadcast([P, P]), ident[:])
+            row = held(name, [P, F], F32)
+            nc.scalar.copy(
+                out=row[:].rearrange("p (u m e) -> p u m e", u=2, e=2),
+                in_=turned[:].rearrange("p (u e m) -> p u m e", u=2, e=2),
+            )
+            return row
+
+        gather_dy(0)
+        tx_col = held("tx_col", [P, CHUNKS], F32)
+        w_col = held("w_col", [P, CHUNKS], F32)
+        nc.scalar.copy(out=tx_col[:], in_=token_columns("tx_got", tx_pool))
+        gt_turned = token_columns("gt_got", gt_pool)
+        nc.vector.tensor_tensor(out=w_col[:], in0=gt_turned, in1=tx_col[:], op=ALU.mult)
+        gather_x(0)
+        gather_dy(1)
+        gather_x(1)
+        c_col = held("c_col", [P, LANES], F32)
+        nc.vector.scalar_tensor_tensor(
+            out=c_col[:], in0=c1_col[:], scalar=-0.5, in1=cf_col[:], op0=ALU.mult, op1=ALU.mult
+        )
+        cf_row = spread_row("cf_row", cf_col)
+        c_row = spread_row("c_row", c_col)
+        x_codes, x_scales = quantize("x", x_words[:], E4M3)
+        w1_grouped = round_weights("w1_grouped", w1_raw)
+        gather_dy(2)
+        w1_codes, w1_scales = quantize("w1", w1_grouped[:], E4M3)
+        gather_dy(3)
+
+        slope = [held(f"slope{c}", [P, F], F32) for c in range(CHUNKS)]
+        dy_ops = []
+
+        def forward(c):
+            cols = slice(c * P, (c + 1) * P)
+            a_bank = bank("a")
+            nc.tensor.matmul_mx(
+                out=a_bank[:],
+                lhsT=x_codes[:, cols].bitcast(E4M3),
+                lhsT_scale=x_scales[:, cols],
+                rhs=w1_codes[:].bitcast(E4M3),
+                rhs_scale=w1_scales[:],
+                start=True,
+                stop=True,
+            )
+            z = work.tile([P, F], F32, name="z")
+            nc.vector.scalar_tensor_tensor(
+                out=z[:], in0=a_bank[:], scalar=tx_col[:, c : c + 1], in1=cf_row[:], op0=ALU.mult, op1=ALU.mult
+            )
+            silu_neg = work.tile([P, F], F32, name="silu_neg", bufs=4)
+            tanh_half = work.tile([P, F], F32, name="tanh_half", bufs=4)
+            nc.scalar.activation(out=silu_neg[:], in_=z[:], func=ACT.Silu, scale=-1.0)
+            nc.scalar.activation(out=tanh_half[:], in_=z[:], func=ACT.Tanh, scale=0.5)
+            return silu_neg, tanh_half
+
+        def make_slope(c, silu_neg, tanh_half):
+            part = work.tile([P, F], F32, name="part")
+            nc.vector.scalar_tensor_tensor(
+                out=part[:], in0=silu_neg[:], scalar=-1.0, in1=c_row[:], op0=ALU.add, op1=ALU.mult
+            )
+            nc.vector.scalar_tensor_tensor(
+                out=slope[c][:], in0=tanh_half[:], scalar=1.0, in1=part[:], op0=ALU.add, op1=ALU.mult
+            )
+
+        def quantize_dy(c):
+            grouped = work.tile([P, P * LANES], BF16, name="dy_grouped", align_bytes=64)
+            nc.scalar.copy(
+                out=grouped[:].rearrange("p (c i t) -> p c t i", i=4, t=LANES),
+                in_=dy_got[:, :, c * P : (c + 1) * P].rearrange("p t (c i) -> p c t i", i=4),
+            )
+            dy_ops.append(quantize(f"dy{c}", grouped[:], E5M2))
+
+        acts = [forward(c) for c in range(CHUNKS)]
+        w2_grouped = round_weights("w2_grouped", w2_raw)
+        quantize_dy(0)
+        make_slope(0, *acts[0])
+        w2_codes, w2_scales = quantize("w2", w2_grouped[:], E4M3)
+
+        w1t_grouped = held("w1t_grouped", [P, D * LANES], BF16)
+        w1_words = w1_grouped[:].bitcast(F32).rearrange("p (u m e h) -> p h u e m", u=2, e=2, h=2)
+        for h in range(2):
+            turned = bank("misc")
+            for t in range(LANES):
+                nc.tensor.transpose(turned[:, t * P : (t + 1) * P], w1_words[:, h, t // 2, t % 2, :], ident[:])
+            nc.scalar.copy(
+                out=w1t_grouped[:, h * 1024 : (h + 1) * 1024].rearrange("p (b q t) -> p q t b", b=2, t=LANES),
+                in_=turned[:].bitcast(BF16).rearrange("p (t q b) -> p q t b", t=LANES, b=2),
+            )
+        for c in range(1, CHUNKS):
+            quantize_dy(c)
+        w1t_codes, w1t_scales = quantize("w1t", w1t_grouped[:], E4M3)
+
+        dx_got = held("dx_got", [P, LANES, N], F32)
+
+        def backward(c):
+            dy_codes, dy_scales = dy_ops[c]
+            dh_bank = bank("dh")
+            nc.tensor.matmul_mx(
+                out=dh_bank[:],
+                lhsT=dy_codes[:].bitcast(E5M2),
+                lhsT_scale=dy_scales[:],
+                rhs=w2_codes[:].bitcast(E4M3),
+                rhs_scale=w2_scales[:],
+                start=True,
+                stop=True,
+            )
+            da = work.tile([P, F], BF16, name="da", align_bytes=64)
+            nc.vector.scalar_tensor_tensor(
+                out=da[:], in0=dh_bank[:], scalar=w_col[:, c : c + 1], in1=slope[c][:], op0=ALU.mult, op1=ALU.mult
+            )
+            da_words = da[:].bitcast(F32)
+            turned = bank("misc")
+            for u in range(2):
+                nc.tensor.transpose(turned[:, u * P : (u + 1) * P], da_words[:, u * P : (u + 1) * P], ident[:])
+            grouped = work.tile([P, P * LANES], BF16, name="da_grouped", align_bytes=64)
+            nc.scalar.copy(
+                out=grouped[:].bitcast(F32).rearrange("p (i u) -> p i u", u=2),
+                in_=turned[:, 0 : 2 * P].rearrange("p (u i) -> p i u", u=2),
+            )
+            return grouped
+
+        def input_gradient(c, grouped):
+            da_codes, da_scales = quantize(f"da{c}", grouped[:], E5M2)
+            dx_bank = bank("a")
+            nc.tensor.matmul_mx(
+                out=dx_bank[:],
+                lhsT=da_codes[:].bitcast(E5M2),
+                lhsT_scale=da_scales[:],
+                rhs=w1t_codes[:].bitcast(E4M3),
+                rhs_scale=w1t_scales[:],
+                start=True,
+                stop=True,
+            )
+            dx_slots = work.tile([P, D], F32, name="dx_slots")
+            nc.scalar.copy(out=dx_slots[:], in_=dx_bank[:])
+            turned = bank("dx")
+            for j in range(LANES):
+                nc.tensor.transpose(turned[:, j * P : (j + 1) * P], dx_slots[:, j * P : (j + 1) * P], ident[:])
+            nc.scalar.copy(
+                out=dx_got[:, :, c * P : (c + 1) * P], in_=turned[:].rearrange("p (j i) -> p j i", j=LANES)
+            )
+
+        def scatter(t, first, last):
+            nc.vector.tensor_tensor(
+                out=out_plane[t][:].indirect(offsets[:, first // 16 : last // 16]),
+                in0=dx_got[:, t, first:last],
+                in1=dy_got[:, t, first:last],
+                op=ALU.add,
+            )
+
+        pending = None
+        for c in range(CHUNKS):
+            if c > 0:
+                make_slope(c, *acts[c])
+            if pending is not None:
+                input_gradient(c - 1, pending)
+            pending = backward(c)
+        for t in range(2):
+            scatter(t, 0, P)
+        input_gradient(CHUNKS - 1, pending)
+        for t in range(2, LANES):
+            scatter(t, 0, P)
+
+        y_grouped = held("y_grouped", [P, T * LANES], BF16)
+        y_lanes = y_grouped[:].rearrange("p (n t) -> p n t", t=LANES)
+        out_rows = out_0.rearrange("(p t) n -> p t n", t=LANES)
+        for t in range(LANES):
+            scatter(t, P, N)
+            nc.sync.dma_start(out=out_rows[:, t, :], in_=out_plane[t][:])
+            first = 0 if t < 2 else SPLIT
+            nc.scalar.copy(out=y_lanes[:, first:, t], in_=out_plane[t][:, first:])
+        for t in range(2, LANES):
+            nc.vector.tensor_copy(out=y_lanes[:, :SPLIT, t], in_=out_plane[t][:, :SPLIT])
+
+        y_codes = held("y_codes", [P, T], U32)
+        y_scales = held("y_scales", [P, T], U8)
+        words_out = out_1[0].rearrange("p n l -> p (n l)").bitcast(I32)
+        for h in range(2):
+            cols = slice(h * 512, (h + 1) * 512)
+            nc.vector.quantize_mx(
+                out=y_codes[:, cols].bitcast(E4M3),
+                scales=y_scales[:, cols],
+                in_=y_grouped[:, h * 2048 : (h + 1) * 2048],
+            )
+            nc.sync.dma_start(out=words_out[:, cols], in_=y_codes[:, cols].bitcast(I32))
+        scales_out = out_2[0].bitcast(I32)
+        for q in range(4):
+            nc.scalar.dma_start(
+                out=scales_out[4 * q : 4 * q + 4, :], in_=y_scales[32 * q : 32 * q + 4, :].bitcast(I32)
+            )

@@ -21,8 +21,15 @@ F = 512
 T = 1024
 N = 512
 CHUNKS = N // P
-SPLIT = 576
-FLOPS = 3 * 2 * 512 * 512 * 512
+QUAD = 32
+RUN = 4
+LAST = P - 1
+X_CAST_SCALAR = 512
+W2_SCALAR = 64
+W2_PIECE = 32
+OUT_VECTOR = 576
+HALF = T // 2
+FLOPS = 3 * 2 * D * F * N
 
 
 def tile_attend_gdepth_sil_pl_kernel(tc, xT, dyT, w1, w2, cf, gt, tx, c1, offs, out_0, out_1, out_2):
@@ -38,59 +45,8 @@ def tile_attend_gdepth_sil_pl_kernel(tc, xT, dyT, w1, w2, cf, gt, tx, c1, offs, 
         def bank(tag):
             return psum.tile([P, 512], F32, name=tag, tag=tag)
 
-        offsets = keep.tile([P, N // 16], U16, name="offsets")
-        dy_rows = dyT.rearrange("(p t) n -> p t n", t=LANES)
-        x_rows = xT.rearrange("(p t) n -> p t n", t=LANES)
-        dy_pool = [held(f"dy_pool{t}", [P, T], F32) for t in range(LANES)]
-        out_plane = [held(f"out_plane{t}", [P, T], F32) for t in range(LANES)]
-        x_raw = [held(f"x_raw{u}", [P, 2, T], F32) for u in range(2)]
-        tx_pool = held("tx_pool", [P, T], F32)
-        gt_pool = held("gt_pool", [P, T], F32)
-        cf_col = held("cf_col", [P, LANES], F32)
-        c1_col = held("c1_col", [P, LANES], F32)
-        w1_raw = held("w1_raw", [P, LANES, F], F32)
-        w2_raw = held("w2_raw", [P, LANES, F], F32)
-
-        nc.sync.dma_start(offsets[:], offs)
-        nc.sync.dma_start(out=dy_pool[0][:], in_=dy_rows[:, 0, :])
-        nc.sync.dma_start(out=tx_pool[0:32, :], in_=tx[0:32, :])
-        nc.sync.dma_start(out=gt_pool[0:32, :], in_=gt[0:32, :])
-        nc.sync.dma_start(out=x_raw[0][:], in_=x_rows[:, 0:2, :])
-        nc.sync.dma_start(out=dy_pool[1][:], in_=dy_rows[:, 1, :])
-        nc.sync.dma_start(out=x_raw[1][:], in_=x_rows[:, 2:4, :])
-        nc.sync.dma_start(out=cf_col[:], in_=cf.rearrange("(p t) o -> p (t o)", t=LANES))
-        nc.sync.dma_start(out=c1_col[:], in_=c1.rearrange("(p t) o -> p (t o)", t=LANES))
-        nc.sync.dma_start(out=w1_raw[:], in_=w1.rearrange("(p j) f -> p j f", j=LANES))
-        nc.sync.dma_start(out=dy_pool[2][:], in_=dy_rows[:, 2, :])
-        nc.sync.dma_start(out=dy_pool[3][:], in_=dy_rows[:, 3, :])
-        nc.sync.dma_start(out=w2_raw[:], in_=w2.rearrange("(p j) f -> p j f", j=LANES))
-        for t in range(LANES):
-            nc.sync.dma_start(out=out_plane[t][:], in_=dy_rows[:, t, :])
-
-        ident = held("ident", [P, P], F32)
-        make_identity(nc, ident[:])
-        for pool_tile in (tx_pool, gt_pool):
-            nc.vector.memset(pool_tile[32:64, :], 0.0)
-            nc.vector.memset(pool_tile[64:128, :], 0.0)
-
-        dy_got = held("dy_got", [P, LANES, N], F32)
-
-        def gather_dy(t):
-            nc.vector.tensor_copy(out=dy_got[:, t, :], in_=dy_pool[t][:].indirect(offsets[:]))
-
-        x_words = held("x_words", [P, N * LANES], BF16)
-
-        def gather_x(u):
-            pairs = held(f"x_pairs{u}", [P, 2 * T], BF16)
-            nc.scalar.activation(
-                out=pairs[:].rearrange("p (c i e) -> p c e i", i=4, e=2),
-                in_=x_raw[u][:].rearrange("p e (c i) -> p c e i", i=4),
-                func=ACT.Copy,
-            )
-            nc.vector.tensor_copy(
-                out=x_words[:].bitcast(U32).rearrange("p (i u) -> p i u", u=2)[:, :, u],
-                in_=pairs[:].bitcast(U32).indirect(offsets[:]),
-            )
+        def block(n):
+            return slice(n * P, (n + 1) * P)
 
         def quantize(name, values, fmt):
             width = values.shape[1] // LANES
@@ -99,211 +55,258 @@ def tile_attend_gdepth_sil_pl_kernel(tc, xT, dyT, w1, w2, cf, gt, tx, c1, offs, 
             nc.vector.quantize_mx(out=codes[:].bitcast(fmt), scales=scales[:], in_=values)
             return codes, scales
 
-        def round_weights(name, raw):
-            grouped = held(name, [P, F * LANES], BF16)
-            nc.scalar.copy(
-                out=grouped[:].rearrange("p (u m e j) -> p m j u e", u=2, e=2, j=LANES),
-                in_=raw[:].rearrange("p j (m u e) -> p m j u e", u=2, e=2),
-            )
-            return grouped
-
-        def token_columns(name, pool_tile):
-            got = held(name, [P, N], F32)
-            nc.vector.tensor_copy(out=got[:], in_=pool_tile[:].indirect(offsets[:]))
-            turned = bank("misc")
-            for c in range(CHUNKS):
-                nc.tensor.transpose(turned[:, c * P : (c + 1) * P], got[:, c * P : (c + 1) * P], ident[:])
-            return turned[:].rearrange("p (c r) -> p c r", r=P)[:, :, 0]
-
-        def spread_row(name, col):
-            turned = bank("misc")
-            for t in range(LANES):
-                nc.tensor.transpose(turned[:, t * P : (t + 1) * P], col[:, t : t + 1].to_broadcast([P, P]), ident[:])
-            row = held(name, [P, F], F32)
-            nc.scalar.copy(
-                out=row[:].rearrange("p (u m e) -> p u m e", u=2, e=2),
-                in_=turned[:].rearrange("p (u e m) -> p u m e", u=2, e=2),
-            )
-            return row
-
-        gather_dy(0)
-        tx_col = held("tx_col", [P, CHUNKS], F32)
-        w_col = held("w_col", [P, CHUNKS], F32)
-        nc.scalar.copy(out=tx_col[:], in_=token_columns("tx_got", tx_pool))
-        gt_turned = token_columns("gt_got", gt_pool)
-        nc.vector.tensor_tensor(out=w_col[:], in0=gt_turned, in1=tx_col[:], op=ALU.mult)
-        gather_x(0)
-        gather_dy(1)
-        gather_x(1)
-        c_col = held("c_col", [P, LANES], F32)
-        nc.vector.scalar_tensor_tensor(
-            out=c_col[:], in0=c1_col[:], scalar=-0.5, in1=cf_col[:], op0=ALU.mult, op1=ALU.mult
-        )
-        cf_row = spread_row("cf_row", cf_col)
-        c_row = spread_row("c_row", c_col)
-        x_codes, x_scales = quantize("x", x_words[:], E4M3)
-        w1_grouped = round_weights("w1_grouped", w1_raw)
-        gather_dy(2)
-        w1_codes, w1_scales = quantize("w1", w1_grouped[:], E4M3)
-        gather_dy(3)
-
-        slope = [held(f"slope{c}", [P, F], F32) for c in range(CHUNKS)]
-        dy_ops = []
-
-        def forward(c):
-            cols = slice(c * P, (c + 1) * P)
-            a_bank = bank("a")
+        def product(out, still, still_fmt, cols, moving, moving_fmt):
             nc.tensor.matmul_mx(
-                out=a_bank[:],
-                lhsT=x_codes[:, cols].bitcast(E4M3),
-                lhsT_scale=x_scales[:, cols],
-                rhs=w1_codes[:].bitcast(E4M3),
-                rhs_scale=w1_scales[:],
+                out=out[:],
+                lhsT=still[0][:, cols].bitcast(still_fmt),
+                lhsT_scale=still[1][:, cols],
+                rhs=moving[0][:].bitcast(moving_fmt),
+                rhs_scale=moving[1][:],
                 start=True,
                 stop=True,
             )
-            z = work.tile([P, F], F32, name="z")
-            nc.vector.scalar_tensor_tensor(
-                out=z[:], in0=a_bank[:], scalar=tx_col[:, c : c + 1], in1=cf_row[:], op0=ALU.mult, op1=ALU.mult
-            )
-            silu_neg = work.tile([P, F], F32, name="silu_neg", bufs=4)
-            tanh_half = work.tile([P, F], F32, name="tanh_half", bufs=4)
-            nc.scalar.activation(out=silu_neg[:], in_=z[:], func=ACT.Silu, scale=-1.0)
-            nc.scalar.activation(out=tanh_half[:], in_=z[:], func=ACT.Tanh, scale=0.5)
-            return silu_neg, tanh_half
 
-        def make_slope(c, silu_neg, tanh_half):
-            part = work.tile([P, F], F32, name="part")
-            nc.vector.scalar_tensor_tensor(
-                out=part[:], in0=silu_neg[:], scalar=-1.0, in1=c_row[:], op0=ALU.add, op1=ALU.mult
-            )
-            nc.vector.scalar_tensor_tensor(
-                out=slope[c][:], in0=tanh_half[:], scalar=1.0, in1=part[:], op0=ALU.add, op1=ALU.mult
-            )
+        offsets = keep.tile([P, N // 16], U16, name="offsets")
+        cf_col = held("cf_col", [P, LANES], F32)
+        c1_col = held("c1_col", [P, LANES], F32)
+        tx_pool = held("tx_pool", [P, T], F32)
+        gt_pool = held("gt_pool", [P, T], F32)
+        x_raw = [held(f"x_raw{u}", [P, 2, T], F32) for u in range(2)]
+        w1_raw = held("w1_raw", [P, LANES, F], F32)
+        w2_raw = held("w2_raw", [P, LANES, F], F32)
+        dy_pool = [held(f"dy_pool{t}", [P, T], F32) for t in range(LANES)]
+        out_plane = [held(f"out_plane{t}", [P, T], F32) for t in range(LANES)]
+        x_rows = xT.rearrange("(p t) n -> p t n", t=LANES)
+        dy_rows = dyT.rearrange("(p t) n -> p t n", t=LANES)
+
+        nc.sync.dma_start(offsets[:], offs)
+        nc.sync.dma_start(out=cf_col[:], in_=cf.rearrange("(m t) o -> m (t o)", t=LANES))
+        nc.sync.dma_start(out=c1_col[:], in_=c1.rearrange("(m t) o -> m (t o)", t=LANES))
+        nc.sync.dma_start(out=tx_pool[LAST:, :], in_=tx[LAST:, :])
+        nc.sync.dma_start(out=gt_pool[LAST:, :], in_=gt[LAST:, :])
+        for u in range(2):
+            nc.sync.dma_start(out=x_raw[u][:], in_=x_rows[:, 2 * u : 2 * u + 2, :])
+        nc.sync.dma_start(out=w1_raw[:], in_=w1.rearrange("(p j) f -> p j f", j=LANES))
+        nc.sync.dma_start(out=w2_raw[:], in_=w2.rearrange("(p j) f -> p j f", j=LANES))
+        for t in range(LANES):
+            nc.sync.dma_start(out=dy_pool[t][:], in_=dy_rows[:, t, :])
+        for t in range(LANES):
+            nc.sync.dma_start(out=out_plane[t][:], in_=dy_rows[:, t, :])
+
+        ident = held("ident", [P, P], F32)
+        make_identity(nc, ident[:])
+        for pool_tile in (tx_pool, gt_pool):
+            nc.vector.memset(pool_tile[:LAST, :], 0.0)
+
+        c_col = held("c_col", [P, LANES], F32)
+        nc.gpsimd.tensor_tensor(out=c_col[:], in0=c1_col[:], in1=cf_col[:], op=ALU.mult)
+        c_turned = bank("small")
+        for t in range(LANES):
+            nc.tensor.transpose(c_turned[:, block(t)], c_col[:, t : t + 1].to_broadcast([P, P]), ident[:])
+        c_row = held("c_row", [P, F], F32)
+        nc.scalar.copy(
+            out=c_row[:].rearrange("p (u m e) -> p u m e", u=2, e=2),
+            in_=c_turned[:].rearrange("p (u e m) -> p u m e", u=2, e=2),
+        )
+
+        def slot_columns(name, pool_tile):
+            got = held(name, [P, N], F32)
+            nc.vector.tensor_copy(out=got[:], in_=pool_tile[:].indirect(offsets[:]))
+            turned = bank("small")
+            for c in range(CHUNKS):
+                nc.tensor.transpose(turned[:, block(c)], got[:, block(c)], ident[:])
+            return turned[:].rearrange("p (c r) -> p c r", r=P)[:, :, LAST]
+
+        tx_neg = held("tx_neg", [P, CHUNKS], F32)
+        tx_half = held("tx_half", [P, CHUNKS], F32)
+        gt_neg = held("gt_neg", [P, CHUNKS], F32)
+        slot_factor = held("slot_factor", [P, CHUNKS], F32)
+        tx_cols = slot_columns("tx_got", tx_pool)
+        nc.scalar.activation(out=tx_neg[:], in_=tx_cols, func=ACT.Copy, scale=-1.0)
+        nc.scalar.activation(out=tx_half[:], in_=tx_cols, func=ACT.Copy, scale=0.5)
+        nc.scalar.activation(out=gt_neg[:], in_=slot_columns("gt_got", gt_pool), func=ACT.Copy, scale=-1.0)
+        nc.gpsimd.tensor_tensor(out=slot_factor[:], in0=gt_neg[:], in1=tx_half[:], op=ALU.mult)
+
+        x_got = held("x_got", [P, 2, N], U32)
+        for u in range(2):
+            pairs = held(f"x_pairs{u}", [P, 2 * T], BF16)
+            dst = pairs[:].rearrange("p (c i e) -> p c e i", i=RUN, e=2)
+            src = x_raw[u][:].rearrange("p e (c i) -> p c e i", i=RUN)
+            cut = u * X_CAST_SCALAR // RUN
+            if cut:
+                nc.scalar.activation(out=dst[:, :cut], in_=src[:, :cut], func=ACT.Copy)
+            nc.vector.tensor_copy(out=dst[:, cut:], in_=src[:, cut:])
+            nc.vector.tensor_copy(out=x_got[:, u, :], in_=pairs[:].bitcast(U32).indirect(offsets[:]))
+        x_grouped = held("x_grouped", [P, N * LANES], BF16)
+        nc.vector.tensor_copy(
+            out=x_grouped[:].bitcast(I32).rearrange("p (i u) -> p i u", u=2),
+            in_=x_got[:].bitcast(I32).rearrange("p u i -> p i u"),
+        )
+        x_mx = quantize("x", x_grouped[:], E4M3)
+
+        w1_grouped = held("w1_grouped", [P, F * LANES], BF16)
+        nc.scalar.copy(
+            out=w1_grouped[:].rearrange("p (t m j) -> p m j t", t=LANES, j=LANES),
+            in_=w1_raw[:].rearrange("p j (m t) -> p m j t", t=LANES),
+        )
+        w1_mx = quantize("w1", w1_grouped[:], E4M3)
+
+        dy_got = held("dy_got", [P, LANES, N], F32)
+        for t in range(LANES):
+            nc.vector.tensor_copy(out=dy_got[:, t, :], in_=dy_pool[t][:].indirect(offsets[:]))
+
+        a_scaled = held("a_scaled", [P, LANES, N], F32)
+        for t in range(LANES):
+            a_bank = bank(("product", "dh")[t % 2])
+            product(a_bank, w1_mx, E4M3, block(t), x_mx, E4M3)
+            nc.scalar.activation(out=a_scaled[:, t, :], in_=a_bank[:], func=ACT.Copy, scale=cf_col[:, t : t + 1])
+
+        w2_grouped = held("w2_grouped", [P, F * LANES], BF16)
+        w2_dst = w2_grouped[:].rearrange("p (u m e j) -> p m j u e", u=2, e=2, j=LANES)
+        w2_src = w2_raw[:].rearrange("p j (m u e) -> p m j u e", u=2, e=2)
+        for m0 in range(0, W2_SCALAR, W2_PIECE):
+            nc.scalar.copy(out=w2_dst[:, m0 : m0 + W2_PIECE], in_=w2_src[:, m0 : m0 + W2_PIECE])
+        nc.vector.tensor_copy(out=w2_dst[:, W2_SCALAR:], in_=w2_src[:, W2_SCALAR:])
+        w2_mx = quantize("w2", w2_grouped[:], E4M3)
+
+        silu_neg = [held(f"silu_neg{c}", [P, F], F32) for c in range(CHUNKS)]
+        tanh_half = [held(f"tanh_half{c}", [P, F], F32) for c in range(CHUNKS)]
+
+        def activations(c):
+            turned = bank("turned")
+            for t in range(LANES):
+                nc.tensor.transpose(turned[:, block(t)], a_scaled[:, t, block(c)], ident[:])
+            in_pair_order = turned[:].rearrange("p (u e m) -> p u m e", u=2, e=2)
+            for dst, func, scale in ((silu_neg, ACT.Silu, tx_neg), (tanh_half, ACT.Tanh, tx_half)):
+                nc.scalar.activation(
+                    out=dst[c][:].rearrange("p (u m e) -> p u m e", u=2, e=2),
+                    in_=in_pair_order,
+                    func=func,
+                    scale=scale[:, c : c + 1],
+                )
 
         def quantize_dy(c):
             grouped = work.tile([P, P * LANES], BF16, name="dy_grouped", align_bytes=64)
             nc.scalar.copy(
-                out=grouped[:].rearrange("p (c i t) -> p c t i", i=4, t=LANES),
-                in_=dy_got[:, :, c * P : (c + 1) * P].rearrange("p t (c i) -> p c t i", i=4),
+                out=grouped[:].rearrange("p (c i t) -> p c t i", i=RUN, t=LANES),
+                in_=dy_got[:, :, block(c)].rearrange("p t (c i) -> p c t i", i=RUN),
             )
-            dy_ops.append(quantize(f"dy{c}", grouped[:], E5M2))
+            return quantize(f"dy{c}", grouped[:], E5M2)
 
-        acts = [forward(c) for c in range(CHUNKS)]
-        w2_grouped = round_weights("w2_grouped", w2_raw)
-        quantize_dy(0)
-        make_slope(0, *acts[0])
-        w2_codes, w2_scales = quantize("w2", w2_grouped[:], E4M3)
+        dy_mx = []
+        for first in range(0, CHUNKS, 2):
+            activations(first)
+            activations(first + 1)
+            dy_mx.append(quantize_dy(first))
+            dy_mx.append(quantize_dy(first + 1))
 
         w1t_grouped = held("w1t_grouped", [P, D * LANES], BF16)
-        w1_words = w1_grouped[:].bitcast(F32).rearrange("p (u m e h) -> p h u e m", u=2, e=2, h=2)
+        w1_words = w1_grouped[:].bitcast(F32).rearrange("p (t m h) -> p h t m", t=LANES, h=2)
         for h in range(2):
-            turned = bank("misc")
+            turned = bank("small")
             for t in range(LANES):
-                nc.tensor.transpose(turned[:, t * P : (t + 1) * P], w1_words[:, h, t // 2, t % 2, :], ident[:])
+                nc.tensor.transpose(turned[:, block(t)], w1_words[:, h, t, :], ident[:])
             nc.scalar.copy(
                 out=w1t_grouped[:, h * 1024 : (h + 1) * 1024].rearrange("p (b q t) -> p q t b", b=2, t=LANES),
                 in_=turned[:].bitcast(BF16).rearrange("p (t q b) -> p q t b", t=LANES, b=2),
             )
-        for c in range(1, CHUNKS):
-            quantize_dy(c)
-        w1t_codes, w1t_scales = quantize("w1t", w1t_grouped[:], E4M3)
+        w1t_mx = quantize("w1t", w1t_grouped[:], E4M3)
 
-        dx_got = held("dx_got", [P, LANES, N], F32)
+        slope = [held(f"slope{c}", [P, F], F32) for c in range(CHUNKS)]
+        da_mx = (held("da_codes", [P, N], U32), held("da_scales", [P, N], U8))
+        da_grouped = {}
 
-        def backward(c):
-            dy_codes, dy_scales = dy_ops[c]
-            dh_bank = bank("dh")
-            nc.tensor.matmul_mx(
-                out=dh_bank[:],
-                lhsT=dy_codes[:].bitcast(E5M2),
-                lhsT_scale=dy_scales[:],
-                rhs=w2_codes[:].bitcast(E4M3),
-                rhs_scale=w2_scales[:],
-                start=True,
-                stop=True,
+        def make_slope(c):
+            part = work.tile([P, F], F32, name="part")
+            nc.vector.scalar_tensor_tensor(
+                out=part[:], in0=silu_neg[c][:], scalar=-1.0, in1=c_row[:], op0=ALU.add, op1=ALU.mult
             )
+            nc.vector.scalar_tensor_tensor(
+                out=slope[c][:], in0=tanh_half[c][:], scalar=1.0, in1=part[:], op0=ALU.add, op1=ALU.mult
+            )
+
+        def make_da(c):
+            dh_bank = bank("dh")
+            product(dh_bank, dy_mx[c], E5M2, slice(0, P), w2_mx, E4M3)
             da = work.tile([P, F], BF16, name="da", align_bytes=64)
             nc.vector.scalar_tensor_tensor(
-                out=da[:], in0=dh_bank[:], scalar=w_col[:, c : c + 1], in1=slope[c][:], op0=ALU.mult, op1=ALU.mult
+                out=da[:],
+                in0=dh_bank[:],
+                scalar=slot_factor[:, c : c + 1],
+                in1=slope[c][:],
+                op0=ALU.mult,
+                op1=ALU.mult,
             )
-            da_words = da[:].bitcast(F32)
-            turned = bank("misc")
+            turned = bank("small")
             for u in range(2):
-                nc.tensor.transpose(turned[:, u * P : (u + 1) * P], da_words[:, u * P : (u + 1) * P], ident[:])
-            grouped = work.tile([P, P * LANES], BF16, name="da_grouped", align_bytes=64)
+                nc.tensor.transpose(turned[:, block(u)], da[:].bitcast(F32)[:, block(u)], ident[:])
+            da_grouped[c] = work.tile([P, P * LANES], BF16, name="da_grouped", align_bytes=64)
             nc.scalar.copy(
-                out=grouped[:].bitcast(F32).rearrange("p (i u) -> p i u", u=2),
+                out=da_grouped[c][:].bitcast(F32).rearrange("p (i u) -> p i u", u=2),
                 in_=turned[:, 0 : 2 * P].rearrange("p (u i) -> p i u", u=2),
             )
-            return grouped
 
-        def input_gradient(c, grouped):
-            da_codes, da_scales = quantize(f"da{c}", grouped[:], E5M2)
-            dx_bank = bank("a")
-            nc.tensor.matmul_mx(
-                out=dx_bank[:],
-                lhsT=da_codes[:].bitcast(E5M2),
-                lhsT_scale=da_scales[:],
-                rhs=w1t_codes[:].bitcast(E4M3),
-                rhs_scale=w1t_scales[:],
-                start=True,
-                stop=True,
-            )
-            dx_slots = work.tile([P, D], F32, name="dx_slots")
-            nc.scalar.copy(out=dx_slots[:], in_=dx_bank[:])
-            turned = bank("dx")
-            for j in range(LANES):
-                nc.tensor.transpose(turned[:, j * P : (j + 1) * P], dx_slots[:, j * P : (j + 1) * P], ident[:])
-            nc.scalar.copy(
-                out=dx_got[:, :, c * P : (c + 1) * P], in_=turned[:].rearrange("p (j i) -> p j i", j=LANES)
-            )
+        dx_first = held("dx_first", [P, D], F32)
 
-        def scatter(t, first, last):
+        def quantize_da(c):
+            nc.vector.quantize_mx(
+                out=da_mx[0][:, block(c)].bitcast(E5M2), scales=da_mx[1][:, block(c)], in_=da_grouped[c][:]
+            )
+            if c == 0:
+                dx_bank = bank("product")
+                product(dx_bank, da_mx, E5M2, block(0), w1t_mx, E4M3)
+                dx_slots = held("dx_slots", [P, D], F32)
+                nc.scalar.copy(out=dx_slots[:], in_=dx_bank[:])
+                turned = bank("turned")
+                for j in range(LANES):
+                    nc.tensor.transpose(turned[:, block(j)], dx_slots[:, block(j)], ident[:])
+                nc.scalar.copy(out=dx_first[:], in_=turned[:])
+
+        for step in range(CHUNKS + 2):
+            for lag, stage in enumerate((make_slope, make_da, quantize_da)):
+                if 0 <= step - lag < CHUNKS:
+                    stage(step - lag)
+
+        def scatter(t, first, last, dx):
             nc.vector.tensor_tensor(
                 out=out_plane[t][:].indirect(offsets[:, first // 16 : last // 16]),
-                in0=dx_got[:, t, first:last],
+                in0=dx,
                 in1=dy_got[:, t, first:last],
                 op=ALU.add,
             )
 
-        pending = None
-        for c in range(CHUNKS):
-            if c > 0:
-                make_slope(c, *acts[c])
-            if pending is not None:
-                input_gradient(c - 1, pending)
-            pending = backward(c)
-        for t in range(2):
-            scatter(t, 0, P)
-        input_gradient(CHUNKS - 1, pending)
-        for t in range(2, LANES):
-            scatter(t, 0, P)
+        for t in range(LANES):
+            scatter(t, 0, P, dx_first[:, block(t)])
 
-        y_grouped = held("y_grouped", [P, T * LANES], BF16)
-        y_lanes = y_grouped[:].rearrange("p (n t) -> p n t", t=LANES)
+        dx_rest = held("dx_rest", [P, LANES, N - P], F32)
+        for j in range(LANES):
+            dx_bank = bank("product")
+            product(dx_bank, w1t_mx, E4M3, block(j), da_mx, E5M2)
+            nc.scalar.copy(out=dx_rest[:, j, :], in_=dx_bank[:, P:])
+
+        out_grouped = held("out_grouped", [P, T * LANES], BF16)
+        out_lanes = out_grouped[:].rearrange("p (n t) -> p n t", t=LANES)
         out_rows = out_0.rearrange("(p t) n -> p t n", t=LANES)
         for t in range(LANES):
-            scatter(t, P, N)
+            scatter(t, P, N, dx_rest[:, t, :])
             nc.sync.dma_start(out=out_rows[:, t, :], in_=out_plane[t][:])
-            first = 0 if t < 2 else SPLIT
-            nc.scalar.copy(out=y_lanes[:, first:, t], in_=out_plane[t][:, first:])
+            first = 0 if t < 2 else OUT_VECTOR
+            nc.scalar.copy(out=out_lanes[:, first:, t], in_=out_plane[t][:, first:])
         for t in range(2, LANES):
-            nc.vector.tensor_copy(out=y_lanes[:, :SPLIT, t], in_=out_plane[t][:, :SPLIT])
+            nc.vector.tensor_copy(out=out_lanes[:, :OUT_VECTOR, t], in_=out_plane[t][:, :OUT_VECTOR])
 
-        y_codes = held("y_codes", [P, T], U32)
-        y_scales = held("y_scales", [P, T], U8)
-        words_out = out_1[0].rearrange("p n l -> p (n l)").bitcast(I32)
-        for h in range(2):
-            cols = slice(h * 512, (h + 1) * 512)
+        out_codes = held("out_codes", [P, T], U32)
+        out_scales = held("out_scales", [P, T], U8)
+        words_hbm = out_1[0].rearrange("p n l -> p (n l)").bitcast(I32)
+        for first in range(0, T, HALF):
+            cols = slice(first, first + HALF)
             nc.vector.quantize_mx(
-                out=y_codes[:, cols].bitcast(E4M3),
-                scales=y_scales[:, cols],
-                in_=y_grouped[:, h * 2048 : (h + 1) * 2048],
+                out=out_codes[:, cols].bitcast(E4M3),
+                scales=out_scales[:, cols],
+                in_=out_grouped[:, first * LANES : (first + HALF) * LANES],
             )
-            nc.sync.dma_start(out=words_out[:, cols], in_=y_codes[:, cols].bitcast(I32))
-        scales_out = out_2[0].bitcast(I32)
+            nc.sync.dma_start(out=words_hbm[:, cols], in_=out_codes[:, cols].bitcast(I32))
+        scales_hbm = out_2[0].bitcast(I32)
         for q in range(4):
-            nc.scalar.dma_start(
-                out=scales_out[4 * q : 4 * q + 4, :], in_=y_scales[32 * q : 32 * q + 4, :].bitcast(I32)
-            )
+            queue = (nc.scalar, nc.sync)[q % 2]
+            queue.dma_start(out=scales_hbm[4 * q : 4 * q + 4, :], in_=out_scales[QUAD * q : QUAD * q + 4, :].bitcast(I32))

@@ -186,8 +186,8 @@ def tile_attend_gdepth_sil_pl_kernel(tc, xT, dyT, w1, w2, cf, gt, tx, c1, offs, 
                 )
 
         def quantize_dy(c):
-            grouped = work.tile([P, P * LANES], BF16, name="dy_grouped", align_bytes=64)
-            nc.scalar.copy(
+            grouped = held(f"dy_grouped{c}", [P, P * LANES], BF16)
+            nc.vector.tensor_copy(
                 out=grouped[:].rearrange("p (c i t) -> p c t i", i=RUN, t=LANES),
                 in_=dy_got[:, :, block(c)].rearrange("p t (c i) -> p c t i", i=RUN),
             )
@@ -240,13 +240,13 @@ def tile_attend_gdepth_sil_pl_kernel(tc, xT, dyT, w1, w2, cf, gt, tx, c1, offs, 
             turned = bank("small")
             for u in range(2):
                 nc.tensor.transpose(turned[:, block(u)], da[:].bitcast(F32)[:, block(u)], ident[:])
-            da_grouped[c] = work.tile([P, P * LANES], BF16, name="da_grouped", align_bytes=64)
+            da_grouped[c] = held(f"da_grouped{c}", [P, P * LANES], BF16)
             nc.scalar.copy(
                 out=da_grouped[c][:].bitcast(F32).rearrange("p (i u) -> p i u", u=2),
                 in_=turned[:, 0 : 2 * P].rearrange("p (u i) -> p i u", u=2),
             )
 
-        dx_first = held("dx_first", [P, D], F32)
+        first_turned = []
 
         def quantize_da(c):
             nc.vector.quantize_mx(
@@ -257,10 +257,9 @@ def tile_attend_gdepth_sil_pl_kernel(tc, xT, dyT, w1, w2, cf, gt, tx, c1, offs, 
                 product(dx_bank, da_mx, E5M2, block(0), w1t_mx, E4M3)
                 dx_slots = held("dx_slots", [P, D], F32)
                 nc.scalar.copy(out=dx_slots[:], in_=dx_bank[:])
-                turned = bank("turned")
+                first_turned.append(bank("turned"))
                 for j in range(LANES):
-                    nc.tensor.transpose(turned[:, block(j)], dx_slots[:, block(j)], ident[:])
-                nc.scalar.copy(out=dx_first[:], in_=turned[:])
+                    nc.tensor.transpose(first_turned[0][:, block(j)], dx_slots[:, block(j)], ident[:])
 
         for step in range(CHUNKS + 2):
             for lag, stage in enumerate((make_slope, make_da, quantize_da)):
@@ -275,16 +274,19 @@ def tile_attend_gdepth_sil_pl_kernel(tc, xT, dyT, w1, w2, cf, gt, tx, c1, offs, 
                 op=ALU.add,
             )
 
-        for t in range(LANES):
-            scatter(t, 0, P, dx_first[:, block(t)])
+        for half, tag in enumerate(("dx_early", f"da_grouped{CHUNKS - 1}")):
+            dx_half = keep.tile([P, 2 * P], F32, name=f"dx_half{half}", tag=tag, align_bytes=64)
+            nc.scalar.copy(out=dx_half[:], in_=first_turned[0][:, half * 2 * P : (half + 1) * 2 * P])
+            for e in range(2):
+                scatter(2 * half + e, 0, P, dx_half[:, block(e)])
 
         dx_rest = held("dx_rest", [P, LANES, N - P], F32)
         for j in range(LANES):
-            dx_bank = bank("product")
+            dx_bank = bank(("product", "dh")[j % 2])
             product(dx_bank, w1t_mx, E4M3, block(j), da_mx, E5M2)
             nc.scalar.copy(out=dx_rest[:, j, :], in_=dx_bank[:, P:])
 
-        out_grouped = held("out_grouped", [P, T * LANES], BF16)
+        out_grouped = keep.tile([P, T * LANES], BF16, name="out_grouped", tag="w1t_codes", align_bytes=64)
         out_lanes = out_grouped[:].rearrange("p (n t) -> p n t", t=LANES)
         out_rows = out_0.rearrange("(p t) n -> p t n", t=LANES)
         for t in range(LANES):

@@ -24,9 +24,11 @@ CHUNKS = N // P
 QUAD = 32
 RUN = 4
 LAST = P - 1
-X_CAST_SCALAR = 512
-W2_SCALAR = 64
+X_PIECE = 512
+W1_SCALAR = 64
+W2_SCALAR = 0
 W2_PIECE = 32
+DY_VECTOR = 2
 OUT_VECTOR = 576
 HALF = T // 2
 FLOPS = 3 * 2 * D * F * N
@@ -36,14 +38,13 @@ def tile_attend_gdepth_sil_pl_kernel(tc, xT, dyT, w1, w2, cf, gt, tx, c1, offs, 
     nc = tc.nc
     with ExitStack() as ctx:
         keep = ctx.enter_context(tc.tile_pool(name="keep", bufs=1))
-        work = ctx.enter_context(tc.tile_pool(name="work", bufs=2))
-        psum = ctx.enter_context(tc.psum_pool(name="psum", bufs=2))
+        psum = ctx.enter_context(tc.psum_pool(name="psum", bufs=1))
 
         def held(name, shape, dtype):
             return keep.tile(shape, dtype, name=name, align_bytes=64)
 
-        def bank(tag):
-            return psum.tile([P, 512], F32, name=tag, tag=tag)
+        def bank(n):
+            return psum.tile([P, 512], F32, name=f"bank{n}", tag=f"bank{n}")
 
         def block(n):
             return slice(n * P, (n + 1) * P)
@@ -71,7 +72,7 @@ def tile_attend_gdepth_sil_pl_kernel(tc, xT, dyT, w1, w2, cf, gt, tx, c1, offs, 
         c1_col = held("c1_col", [P, LANES], F32)
         tx_pool = held("tx_pool", [P, T], F32)
         gt_pool = held("gt_pool", [P, T], F32)
-        x_raw = [held(f"x_raw{u}", [P, 2, T], F32) for u in range(2)]
+        x_raw = [[held(f"x_raw{u}{h}", [P, 2, X_PIECE], F32) for h in range(T // X_PIECE)] for u in range(2)]
         w1_raw = held("w1_raw", [P, LANES, F], F32)
         w2_raw = held("w2_raw", [P, LANES, F], F32)
         dy_pool = [held(f"dy_pool{t}", [P, T], F32) for t in range(LANES)]
@@ -80,12 +81,13 @@ def tile_attend_gdepth_sil_pl_kernel(tc, xT, dyT, w1, w2, cf, gt, tx, c1, offs, 
         dy_rows = dyT.rearrange("(p t) n -> p t n", t=LANES)
 
         nc.sync.dma_start(offsets[:], offs)
-        nc.sync.dma_start(out=cf_col[:], in_=cf.rearrange("(m t) o -> m (t o)", t=LANES))
-        nc.sync.dma_start(out=c1_col[:], in_=c1.rearrange("(m t) o -> m (t o)", t=LANES))
         nc.sync.dma_start(out=tx_pool[LAST:, :], in_=tx[LAST:, :])
         nc.sync.dma_start(out=gt_pool[LAST:, :], in_=gt[LAST:, :])
+        nc.scalar.dma_start(out=cf_col[:], in_=cf.rearrange("(m t) o -> m (t o)", t=LANES))
+        nc.scalar.dma_start(out=c1_col[:], in_=c1.rearrange("(m t) o -> m (t o)", t=LANES))
         for u in range(2):
-            nc.sync.dma_start(out=x_raw[u][:], in_=x_rows[:, 2 * u : 2 * u + 2, :])
+            for h, piece in enumerate(x_raw[u]):
+                nc.sync.dma_start(out=piece[:], in_=x_rows[:, 2 * u : 2 * u + 2, h * X_PIECE : (h + 1) * X_PIECE])
         nc.sync.dma_start(out=w1_raw[:], in_=w1.rearrange("(p j) f -> p j f", j=LANES))
         nc.sync.dma_start(out=w2_raw[:], in_=w2.rearrange("(p j) f -> p j f", j=LANES))
         for t in range(LANES):
@@ -98,44 +100,27 @@ def tile_attend_gdepth_sil_pl_kernel(tc, xT, dyT, w1, w2, cf, gt, tx, c1, offs, 
         for pool_tile in (tx_pool, gt_pool):
             nc.vector.memset(pool_tile[:LAST, :], 0.0)
 
-        c_col = held("c_col", [P, LANES], F32)
-        nc.gpsimd.tensor_tensor(out=c_col[:], in0=c1_col[:], in1=cf_col[:], op=ALU.mult)
-        c_turned = bank("small")
-        for t in range(LANES):
-            nc.tensor.transpose(c_turned[:, block(t)], c_col[:, t : t + 1].to_broadcast([P, P]), ident[:])
-        c_row = held("c_row", [P, F], F32)
-        nc.scalar.copy(
-            out=c_row[:].rearrange("p (u m e) -> p u m e", u=2, e=2),
-            in_=c_turned[:].rearrange("p (u e m) -> p u m e", u=2, e=2),
-        )
-
-        def slot_columns(name, pool_tile):
+        warm = held("warm", [P, 1], F32)
+        nc.scalar.activation(out=warm[:], in_=ident[:, 0:1], func=ACT.Silu)
+        def slot_columns(name, pool_tile, n):
             got = held(name, [P, N], F32)
             nc.vector.tensor_copy(out=got[:], in_=pool_tile[:].indirect(offsets[:]))
-            turned = bank("small")
+            turned = bank(n)
             for c in range(CHUNKS):
                 nc.tensor.transpose(turned[:, block(c)], got[:, block(c)], ident[:])
             return turned[:].rearrange("p (c r) -> p c r", r=P)[:, :, LAST]
 
-        tx_neg = held("tx_neg", [P, CHUNKS], F32)
-        tx_half = held("tx_half", [P, CHUNKS], F32)
-        gt_neg = held("gt_neg", [P, CHUNKS], F32)
-        slot_factor = held("slot_factor", [P, CHUNKS], F32)
-        tx_cols = slot_columns("tx_got", tx_pool)
-        nc.scalar.activation(out=tx_neg[:], in_=tx_cols, func=ACT.Copy, scale=-1.0)
-        nc.scalar.activation(out=tx_half[:], in_=tx_cols, func=ACT.Copy, scale=0.5)
-        nc.scalar.activation(out=gt_neg[:], in_=slot_columns("gt_got", gt_pool), func=ACT.Copy, scale=-1.0)
-        nc.gpsimd.tensor_tensor(out=slot_factor[:], in0=gt_neg[:], in1=tx_half[:], op=ALU.mult)
+        tx_cols = slot_columns("tx_got", tx_pool, 0)
+        gt_cols = slot_columns("gt_got", gt_pool, 1)
 
         x_got = held("x_got", [P, 2, N], U32)
         for u in range(2):
             pairs = held(f"x_pairs{u}", [P, 2 * T], BF16)
             dst = pairs[:].rearrange("p (c i e) -> p c e i", i=RUN, e=2)
-            src = x_raw[u][:].rearrange("p e (c i) -> p c e i", i=RUN)
-            cut = u * X_CAST_SCALAR // RUN
-            if cut:
-                nc.scalar.activation(out=dst[:, :cut], in_=src[:, :cut], func=ACT.Copy)
-            nc.vector.tensor_copy(out=dst[:, cut:], in_=src[:, cut:])
+            src = [piece[:].rearrange("p e (c i) -> p c e i", i=RUN) for piece in x_raw[u]]
+            runs = X_PIECE // RUN
+            nc.scalar.activation(out=dst[:, :runs], in_=src[0], func=ACT.Copy)
+            nc.vector.tensor_copy(out=dst[:, runs:], in_=src[1])
             nc.vector.tensor_copy(out=x_got[:, u, :], in_=pairs[:].bitcast(U32).indirect(offsets[:]))
         x_grouped = held("x_grouped", [P, N * LANES], BF16)
         nc.vector.tensor_copy(
@@ -144,20 +129,47 @@ def tile_attend_gdepth_sil_pl_kernel(tc, xT, dyT, w1, w2, cf, gt, tx, c1, offs, 
         )
         x_mx = quantize("x", x_grouped[:], E4M3)
 
+        c_col = held("c_col", [P, LANES], F32)
+        nc.gpsimd.tensor_tensor(out=c_col[:], in0=c1_col[:], in1=cf_col[:], op=ALU.mult)
+        c_turned = bank(2)
+        c_lanes = c_turned[:].rearrange("p (u m e) -> p u e m", u=2, e=2)
+        for t in range(LANES):
+            nc.tensor.transpose(c_lanes[:, t // 2, t % 2, :], c_col[:, t : t + 1].to_broadcast([P, P]), ident[:])
+        c_row = c_turned
+
         w1_grouped = held("w1_grouped", [P, F * LANES], BF16)
-        nc.scalar.copy(
-            out=w1_grouped[:].rearrange("p (t m j) -> p m j t", t=LANES, j=LANES),
-            in_=w1_raw[:].rearrange("p j (m t) -> p m j t", t=LANES),
-        )
+        w1_dst = w1_grouped[:].rearrange("p (t m j) -> p m j t", t=LANES, j=LANES)
+        w1_src = w1_raw[:].rearrange("p j (m t) -> p m j t", t=LANES)
+        nc.scalar.copy(out=w1_dst[:, :, :, :2], in_=w1_src[:, :, :, :2])
+        nc.vector.tensor_copy(out=w1_dst[:, :, :, 2:], in_=w1_src[:, :, :, 2:])
         w1_mx = quantize("w1", w1_grouped[:], E4M3)
 
-        dy_got = held("dy_got", [P, LANES, N], F32)
-        for t in range(LANES):
-            nc.vector.tensor_copy(out=dy_got[:, t, :], in_=dy_pool[t][:].indirect(offsets[:]))
+        factors = keep.tile([P, 3, CHUNKS], F32, name="factors", tag="w1_raw", align_bytes=64)
+        tx_neg, tx_half, gt_neg = (factors[:, k, :] for k in range(3))
+        slot_factor = held("slot_factor", [P, CHUNKS], F32)
+        nc.scalar.activation(out=tx_neg[:], in_=tx_cols, func=ACT.Copy, scale=-1.0)
+        nc.scalar.activation(out=tx_half[:], in_=tx_cols, func=ACT.Copy, scale=0.5)
+        nc.scalar.activation(out=gt_neg[:], in_=gt_cols, func=ACT.Copy, scale=-1.0)
+        nc.gpsimd.tensor_tensor(out=slot_factor[:], in0=gt_neg[:], in1=tx_half[:], op=ALU.mult)
+
+        w1t_grouped = held("w1t_grouped", [P, D * LANES], BF16)
+        w1_words = w1_grouped[:].bitcast(F32).rearrange("p (t m h) -> p h t m", t=LANES, h=2)
+
+        def turn_w1(h, n):
+            turned = bank(n)
+            for t in range(LANES):
+                nc.tensor.transpose(turned[:, block(t)], w1_words[:, h, t, :], ident[:])
+            nc.scalar.copy(
+                out=w1t_grouped[:, h * 1024 : (h + 1) * 1024].rearrange("p (b q t) -> p q t b", b=2, t=LANES),
+                in_=turned[:].bitcast(BF16).rearrange("p (t q b) -> p q t b", t=LANES, b=2),
+            )
+
+
+        turn_w1(0, 4)
 
         a_scaled = held("a_scaled", [P, LANES, N], F32)
         for t in range(LANES):
-            a_bank = bank(("product", "dh")[t % 2])
+            a_bank = bank((5 + t) % 8)
             product(a_bank, w1_mx, E4M3, block(t), x_mx, E4M3)
             nc.scalar.activation(out=a_scaled[:, t, :], in_=a_bank[:], func=ACT.Copy, scale=cf_col[:, t : t + 1])
 
@@ -166,17 +178,23 @@ def tile_attend_gdepth_sil_pl_kernel(tc, xT, dyT, w1, w2, cf, gt, tx, c1, offs, 
         w2_src = w2_raw[:].rearrange("p j (m u e) -> p m j u e", u=2, e=2)
         for m0 in range(0, W2_SCALAR, W2_PIECE):
             nc.scalar.copy(out=w2_dst[:, m0 : m0 + W2_PIECE], in_=w2_src[:, m0 : m0 + W2_PIECE])
-        nc.vector.tensor_copy(out=w2_dst[:, W2_SCALAR:], in_=w2_src[:, W2_SCALAR:])
+        if W2_SCALAR < P:
+            nc.vector.tensor_copy(out=w2_dst[:, W2_SCALAR:], in_=w2_src[:, W2_SCALAR:])
         w2_mx = quantize("w2", w2_grouped[:], E4M3)
+
 
         silu_neg = [held(f"silu_neg{c}", [P, F], F32) for c in range(CHUNKS)]
         tanh_half = [held(f"tanh_half{c}", [P, F], F32) for c in range(CHUNKS)]
 
-        def activations(c):
-            turned = bank("turned")
+        a_turned = []
+
+        def turn_a(c):
+            a_turned.append(bank((1, 3, 4, 0)[c]))
             for t in range(LANES):
-                nc.tensor.transpose(turned[:, block(t)], a_scaled[:, t, block(c)], ident[:])
-            in_pair_order = turned[:].rearrange("p (u e m) -> p u m e", u=2, e=2)
+                nc.tensor.transpose(a_turned[c][:, block(t)], a_scaled[:, t, block(c)], ident[:])
+
+        def activations(c):
+            in_pair_order = a_turned[c][:].rearrange("p (u e m) -> p u m e", u=2, e=2)
             for dst, func, scale in ((silu_neg, ACT.Silu, tx_neg), (tanh_half, ACT.Tanh, tx_half)):
                 nc.scalar.activation(
                     out=dst[c][:].rearrange("p (u m e) -> p u m e", u=2, e=2),
@@ -187,37 +205,37 @@ def tile_attend_gdepth_sil_pl_kernel(tc, xT, dyT, w1, w2, cf, gt, tx, c1, offs, 
 
         def quantize_dy(c):
             grouped = held(f"dy_grouped{c}", [P, P * LANES], BF16)
-            nc.vector.tensor_copy(
+            rounding_copy = nc.vector.tensor_copy if c < DY_VECTOR else nc.scalar.copy
+            rounding_copy(
                 out=grouped[:].rearrange("p (c i t) -> p c t i", i=RUN, t=LANES),
                 in_=dy_got[:, :, block(c)].rearrange("p t (c i) -> p c t i", i=RUN),
             )
             return quantize(f"dy{c}", grouped[:], E5M2)
 
-        dy_mx = []
-        for first in range(0, CHUNKS, 2):
-            activations(first)
-            activations(first + 1)
-            dy_mx.append(quantize_dy(first))
-            dy_mx.append(quantize_dy(first + 1))
+        turn_a(0)
+        activations(0)
+        turn_a(1)
+        turn_w1(1, 5)
+        activations(1)
+        turn_a(2)
+        turn_a(3)
+        dy_got = held("dy_got", [P, LANES, N], F32)
+        for t in range(LANES):
+            nc.vector.tensor_copy(out=dy_got[:, t, :], in_=dy_pool[t][:].indirect(offsets[:]))
 
-        w1t_grouped = held("w1t_grouped", [P, D * LANES], BF16)
-        w1_words = w1_grouped[:].bitcast(F32).rearrange("p (t m h) -> p h t m", t=LANES, h=2)
-        for h in range(2):
-            turned = bank("small")
-            for t in range(LANES):
-                nc.tensor.transpose(turned[:, block(t)], w1_words[:, h, t, :], ident[:])
-            nc.scalar.copy(
-                out=w1t_grouped[:, h * 1024 : (h + 1) * 1024].rearrange("p (b q t) -> p q t b", b=2, t=LANES),
-                in_=turned[:].bitcast(BF16).rearrange("p (t q b) -> p q t b", t=LANES, b=2),
-            )
+        dh_banks = []
+        for c in range(CHUNKS):
+            dh_banks.append(bank((6, 7, 5, 6)[c]))
+            product(dh_banks[c], quantize_dy(c), E5M2, slice(0, P), w2_mx, E4M3)
         w1t_mx = quantize("w1t", w1t_grouped[:], E4M3)
-
         slope = [held(f"slope{c}", [P, F], F32) for c in range(CHUNKS)]
         da_mx = (held("da_codes", [P, N], U32), held("da_scales", [P, N], U8))
         da_grouped = {}
 
+        first_turned = []
+
         def make_slope(c):
-            part = work.tile([P, F], F32, name="part")
+            part = held(f"part{c}", [P, F], F32)
             nc.vector.scalar_tensor_tensor(
                 out=part[:], in0=silu_neg[c][:], scalar=-1.0, in1=c_row[:], op0=ALU.add, op1=ALU.mult
             )
@@ -226,18 +244,16 @@ def tile_attend_gdepth_sil_pl_kernel(tc, xT, dyT, w1, w2, cf, gt, tx, c1, offs, 
             )
 
         def make_da(c):
-            dh_bank = bank("dh")
-            product(dh_bank, dy_mx[c], E5M2, slice(0, P), w2_mx, E4M3)
-            da = work.tile([P, F], BF16, name="da", align_bytes=64)
+            da = keep.tile([P, F], BF16, name=f"da{c}", tag=f"da{c % 2}", align_bytes=64)
             nc.vector.scalar_tensor_tensor(
                 out=da[:],
-                in0=dh_bank[:],
+                in0=dh_banks[c][:],
                 scalar=slot_factor[:, c : c + 1],
                 in1=slope[c][:],
                 op0=ALU.mult,
                 op1=ALU.mult,
             )
-            turned = bank("small")
+            turned = first_turned[1] if c == CHUNKS - 1 else bank((1, 3, 4)[c])
             for u in range(2):
                 nc.tensor.transpose(turned[:, block(u)], da[:].bitcast(F32)[:, block(u)], ident[:])
             da_grouped[c] = held(f"da_grouped{c}", [P, P * LANES], BF16)
@@ -246,25 +262,33 @@ def tile_attend_gdepth_sil_pl_kernel(tc, xT, dyT, w1, w2, cf, gt, tx, c1, offs, 
                 in_=turned[:, 0 : 2 * P].rearrange("p (u i) -> p i u", u=2),
             )
 
-        first_turned = []
-
         def quantize_da(c):
             nc.vector.quantize_mx(
                 out=da_mx[0][:, block(c)].bitcast(E5M2), scales=da_mx[1][:, block(c)], in_=da_grouped[c][:]
             )
             if c == 0:
-                dx_bank = bank("product")
+                dx_bank = bank(7)
                 product(dx_bank, da_mx, E5M2, block(0), w1t_mx, E4M3)
                 dx_slots = held("dx_slots", [P, D], F32)
                 nc.scalar.copy(out=dx_slots[:], in_=dx_bank[:])
-                first_turned.append(bank("turned"))
+                first_turned.extend((bank(1), bank(7)))
                 for j in range(LANES):
-                    nc.tensor.transpose(first_turned[0][:, block(j)], dx_slots[:, block(j)], ident[:])
+                    nc.tensor.transpose(first_turned[j // 2][:, block(j)], dx_slots[:, block(j)], ident[:])
 
-        for step in range(CHUNKS + 2):
-            for lag, stage in enumerate((make_slope, make_da, quantize_da)):
-                if 0 <= step - lag < CHUNKS:
-                    stage(step - lag)
+        make_slope(0)
+        make_da(0)
+        make_slope(1)
+        quantize_da(0)
+        make_da(1)
+        activations(2)
+        make_slope(2)
+        quantize_da(1)
+        make_da(2)
+        activations(3)
+        make_slope(3)
+        make_da(3)
+        quantize_da(2)
+        quantize_da(3)
 
         def scatter(t, first, last, dx):
             nc.vector.tensor_tensor(
@@ -274,15 +298,15 @@ def tile_attend_gdepth_sil_pl_kernel(tc, xT, dyT, w1, w2, cf, gt, tx, c1, offs, 
                 op=ALU.add,
             )
 
-        for half, tag in enumerate(("dx_early", f"da_grouped{CHUNKS - 1}")):
-            dx_half = keep.tile([P, 2 * P], F32, name=f"dx_half{half}", tag=tag, align_bytes=64)
-            nc.scalar.copy(out=dx_half[:], in_=first_turned[0][:, half * 2 * P : (half + 1) * 2 * P])
+        for half in range(2):
+            dx_half = keep.tile([P, 2 * P], F32, name=f"dx_half{half}", tag=(f"part{CHUNKS - 1}", "dx_late")[half], align_bytes=64)
+            nc.scalar.copy(out=dx_half[:], in_=first_turned[half][:, half * 2 * P : (half + 1) * 2 * P])
             for e in range(2):
                 scatter(2 * half + e, 0, P, dx_half[:, block(e)])
 
         dx_rest = held("dx_rest", [P, LANES, N - P], F32)
         for j in range(LANES):
-            dx_bank = bank(("product", "dh")[j % 2])
+            dx_bank = bank((0, 5, 2, 3)[j])
             product(dx_bank, w1t_mx, E4M3, block(j), da_mx, E5M2)
             nc.scalar.copy(out=dx_rest[:, j, :], in_=dx_bank[:, P:])
 

@@ -25,11 +25,9 @@ QUAD = 32
 RUN = 4
 LAST = P - 1
 X_PIECE = 512
-W1_SCALAR = 64
-W2_SCALAR = 0
-W2_PIECE = 32
-DY_VECTOR = 2
-OUT_VECTOR = 576
+OUT_VECTOR = 704
+WEAVE_VECTOR = 640
+PLANE_ORDER = (2, 0, 1, 3)
 HALF = T // 2
 FLOPS = 3 * 2 * D * F * N
 
@@ -89,9 +87,9 @@ def tile_attend_gdepth_sil_pl_kernel(tc, xT, dyT, w1, w2, cf, gt, tx, c1, offs, 
             for h, piece in enumerate(x_raw[u]):
                 nc.sync.dma_start(out=piece[:], in_=x_rows[:, 2 * u : 2 * u + 2, h * X_PIECE : (h + 1) * X_PIECE])
         nc.sync.dma_start(out=w1_raw[:], in_=w1.rearrange("(p j) f -> p j f", j=LANES))
-        nc.sync.dma_start(out=w2_raw[:], in_=w2.rearrange("(p j) f -> p j f", j=LANES))
         for t in range(LANES):
             nc.sync.dma_start(out=dy_pool[t][:], in_=dy_rows[:, t, :])
+        nc.sync.dma_start(out=w2_raw[:], in_=w2.rearrange("(p j) f -> p j f", j=LANES))
         for t in range(LANES):
             nc.sync.dma_start(out=out_plane[t][:], in_=dy_rows[:, t, :])
 
@@ -101,7 +99,7 @@ def tile_attend_gdepth_sil_pl_kernel(tc, xT, dyT, w1, w2, cf, gt, tx, c1, offs, 
             nc.vector.memset(pool_tile[:LAST, :], 0.0)
 
         warm = held("warm", [P, 1], F32)
-        nc.scalar.activation(out=warm[:], in_=ident[:, 0:1], func=ACT.Silu)
+        nc.scalar.activation(out=warm[:QUAD, :], in_=tx_pool[:QUAD, 0:1], func=ACT.Silu)
         def slot_columns(name, pool_tile, n):
             got = held(name, [P, N], F32)
             nc.vector.tensor_copy(out=got[:], in_=pool_tile[:].indirect(offsets[:]))
@@ -140,8 +138,7 @@ def tile_attend_gdepth_sil_pl_kernel(tc, xT, dyT, w1, w2, cf, gt, tx, c1, offs, 
         w1_grouped = held("w1_grouped", [P, F * LANES], BF16)
         w1_dst = w1_grouped[:].rearrange("p (t m j) -> p m j t", t=LANES, j=LANES)
         w1_src = w1_raw[:].rearrange("p j (m t) -> p m j t", t=LANES)
-        nc.scalar.copy(out=w1_dst[:, :, :, :2], in_=w1_src[:, :, :, :2])
-        nc.vector.tensor_copy(out=w1_dst[:, :, :, 2:], in_=w1_src[:, :, :, 2:])
+        nc.scalar.copy(out=w1_dst, in_=w1_src)
         w1_mx = quantize("w1", w1_grouped[:], E4M3)
 
         factors = keep.tile([P, 3, CHUNKS], F32, name="factors", tag="w1_raw", align_bytes=64)
@@ -173,16 +170,6 @@ def tile_attend_gdepth_sil_pl_kernel(tc, xT, dyT, w1, w2, cf, gt, tx, c1, offs, 
             product(a_bank, w1_mx, E4M3, block(t), x_mx, E4M3)
             nc.scalar.activation(out=a_scaled[:, t, :], in_=a_bank[:], func=ACT.Copy, scale=cf_col[:, t : t + 1])
 
-        w2_grouped = held("w2_grouped", [P, F * LANES], BF16)
-        w2_dst = w2_grouped[:].rearrange("p (u m e j) -> p m j u e", u=2, e=2, j=LANES)
-        w2_src = w2_raw[:].rearrange("p j (m u e) -> p m j u e", u=2, e=2)
-        for m0 in range(0, W2_SCALAR, W2_PIECE):
-            nc.scalar.copy(out=w2_dst[:, m0 : m0 + W2_PIECE], in_=w2_src[:, m0 : m0 + W2_PIECE])
-        if W2_SCALAR < P:
-            nc.vector.tensor_copy(out=w2_dst[:, W2_SCALAR:], in_=w2_src[:, W2_SCALAR:])
-        w2_mx = quantize("w2", w2_grouped[:], E4M3)
-
-
         silu_neg = [held(f"silu_neg{c}", [P, F], F32) for c in range(CHUNKS)]
         tanh_half = [held(f"tanh_half{c}", [P, F], F32) for c in range(CHUNKS)]
 
@@ -203,30 +190,36 @@ def tile_attend_gdepth_sil_pl_kernel(tc, xT, dyT, w1, w2, cf, gt, tx, c1, offs, 
                     scale=scale[:, c : c + 1],
                 )
 
-        def quantize_dy(c):
-            grouped = held(f"dy_grouped{c}", [P, P * LANES], BF16)
-            rounding_copy = nc.vector.tensor_copy if c < DY_VECTOR else nc.scalar.copy
-            rounding_copy(
+        def quantize_dy(h):
+            grouped = held(f"dy_grouped{h}", [P, 2 * P * LANES], BF16)
+            nc.vector.tensor_copy(
                 out=grouped[:].rearrange("p (c i t) -> p c t i", i=RUN, t=LANES),
-                in_=dy_got[:, :, block(c)].rearrange("p t (c i) -> p c t i", i=RUN),
+                in_=dy_got[:, :, 2 * P * h : 2 * P * (h + 1)].rearrange("p t (c i) -> p c t i", i=RUN),
             )
-            return quantize(f"dy{c}", grouped[:], E5M2)
+            return quantize(f"dy{h}", grouped[:], E5M2)
 
         turn_a(0)
         activations(0)
-        turn_a(1)
-        turn_w1(1, 5)
+        for c in range(1, CHUNKS):
+            turn_a(c)
+        w2_grouped = held("w2_grouped", [P, F * LANES], BF16)
+        w2_dst = w2_grouped[:].rearrange("p (u m e j) -> p m j u e", u=2, e=2, j=LANES)
+        w2_src = w2_raw[:].rearrange("p j (m u e) -> p m j u e", u=2, e=2)
+        nc.scalar.copy(out=w2_dst, in_=w2_src)
+        w2_mx = quantize("w2", w2_grouped[:], E4M3)
+
+
         activations(1)
-        turn_a(2)
-        turn_a(3)
+        turn_w1(1, 1)
         dy_got = held("dy_got", [P, LANES, N], F32)
         for t in range(LANES):
             nc.vector.tensor_copy(out=dy_got[:, t, :], in_=dy_pool[t][:].indirect(offsets[:]))
 
         dh_banks = []
+        dy_mx = [quantize_dy(h) for h in range(2)]
         for c in range(CHUNKS):
             dh_banks.append(bank((6, 7, 5, 6)[c]))
-            product(dh_banks[c], quantize_dy(c), E5M2, slice(0, P), w2_mx, E4M3)
+            product(dh_banks[c], dy_mx[c // 2], E5M2, block(c % 2), w2_mx, E4M3)
         w1t_mx = quantize("w1t", w1t_grouped[:], E4M3)
         slope = [held(f"slope{c}", [P, F], F32) for c in range(CHUNKS)]
         da_mx = (held("da_codes", [P, N], U32), held("da_scales", [P, N], U8))
@@ -304,32 +297,49 @@ def tile_attend_gdepth_sil_pl_kernel(tc, xT, dyT, w1, w2, cf, gt, tx, c1, offs, 
             for e in range(2):
                 scatter(2 * half + e, 0, P, dx_half[:, block(e)])
 
-        dx_rest = held("dx_rest", [P, LANES, N - P], F32)
-        for j in range(LANES):
-            dx_bank = bank((0, 5, 2, 3)[j])
-            product(dx_bank, w1t_mx, E4M3, block(j), da_mx, E5M2)
-            nc.scalar.copy(out=dx_rest[:, j, :], in_=dx_bank[:, P:])
+        dx_banks = {}
+        for j, n in zip(PLANE_ORDER, (0, 5, 2, 3)):
+            dx_banks[j] = bank(n)
+            product(dx_banks[j], w1t_mx, E4M3, block(j), da_mx, E5M2)
 
-        out_grouped = keep.tile([P, T * LANES], BF16, name="out_grouped", tag="w1t_codes", align_bytes=64)
-        out_lanes = out_grouped[:].rearrange("p (n t) -> p n t", t=LANES)
+        def fetch_dx(j, tag):
+            dx = keep.tile([P, N - P], F32, name=f"dx_rest{j}", tag=tag, align_bytes=64)
+            nc.scalar.copy(out=dx[:], in_=dx_banks[j][:, P:])
+            return dx
+
+        dx_rest = {j: fetch_dx(j, f"dx_rest{j}") for j in PLANE_ORDER[:-1]}
+
+        out_pairs = keep.tile([P, 2, 2 * T], BF16, name="out_pairs", tag="dy_pool0", align_bytes=64)
+        out_lane = [out_pairs[:, t // 2, :].rearrange("p (n e) -> p n e", e=2)[:, :, t % 2] for t in range(LANES)]
         out_rows = out_0.rearrange("(p t) n -> p t n", t=LANES)
-        for t in range(LANES):
-            scatter(t, P, N, dx_rest[:, t, :])
+        final = PLANE_ORDER[-1]
+        for t in PLANE_ORDER:
+            scatter(t, P, N, dx_rest[t][:])
             nc.sync.dma_start(out=out_rows[:, t, :], in_=out_plane[t][:])
-            first = 0 if t < 2 else OUT_VECTOR
-            nc.scalar.copy(out=out_lanes[:, first:, t], in_=out_plane[t][:, first:])
-        for t in range(2, LANES):
-            nc.vector.tensor_copy(out=out_lanes[:, :OUT_VECTOR, t], in_=out_plane[t][:, :OUT_VECTOR])
+            if t != final:
+                nc.scalar.copy(out=out_lane[t], in_=out_plane[t][:])
+            if t == PLANE_ORDER[0]:
+                dx_rest[final] = fetch_dx(final, f"dx_rest{t}")
+        nc.scalar.copy(out=out_lane[final][:, OUT_VECTOR:], in_=out_plane[final][:, OUT_VECTOR:])
+        for cols in (slice(0, HALF), slice(HALF, OUT_VECTOR)):
+            nc.vector.tensor_copy(out=out_lane[final][:, cols], in_=out_plane[final][:, cols])
+
+        out_grouped = held("out_grouped", [P, T * LANES], BF16)
+        woven = out_grouped[:].bitcast(U32).rearrange("p (n u) -> p n u", u=2)
+        pair_words = out_pairs[:].bitcast(U32).rearrange("p u n -> p n u")
+        nc.scalar.copy(out=woven[:, WEAVE_VECTOR:], in_=pair_words[:, WEAVE_VECTOR:])
+        for cols in (slice(0, HALF), slice(HALF, WEAVE_VECTOR)):
+            nc.vector.tensor_copy(out=woven[:, cols].bitcast(I32), in_=pair_words[:, cols].bitcast(I32))
 
         out_codes = held("out_codes", [P, T], U32)
         out_scales = held("out_scales", [P, T], U8)
         words_hbm = out_1[0].rearrange("p n l -> p (n l)").bitcast(I32)
-        for first in range(0, T, HALF):
-            cols = slice(first, first + HALF)
+        for first, last in ((0, HALF), (HALF, 3 * T // 4), (3 * T // 4, T)):
+            cols = slice(first, last)
             nc.vector.quantize_mx(
                 out=out_codes[:, cols].bitcast(E4M3),
                 scales=out_scales[:, cols],
-                in_=out_grouped[:, first * LANES : (first + HALF) * LANES],
+                in_=out_grouped[:, first * LANES : last * LANES],
             )
             nc.sync.dma_start(out=words_hbm[:, cols], in_=out_codes[:, cols].bitcast(I32))
         scales_hbm = out_2[0].bitcast(I32)

@@ -28,6 +28,7 @@ X_PIECE = 512
 OUT_VECTOR = 704
 WEAVE_VECTOR = 640
 PLANE_ORDER = (2, 0, 1, 3)
+W1_VECTOR = 56
 HALF = T // 2
 FLOPS = 3 * 2 * D * F * N
 
@@ -70,7 +71,8 @@ def tile_attend_gdepth_sil_pl_kernel(tc, xT, dyT, w1, w2, cf, gt, tx, c1, offs, 
         c1_col = held("c1_col", [P, LANES], F32)
         tx_pool = held("tx_pool", [P, T], F32)
         gt_pool = held("gt_pool", [P, T], F32)
-        x_raw = [[held(f"x_raw{u}{h}", [P, 2, X_PIECE], F32) for h in range(T // X_PIECE)] for u in range(2)]
+        x_raw = [held(f"x_raw{h}", [P, 2, X_PIECE], F32) for h in range(T // X_PIECE)]
+        x_plane = {t: held(f"x_plane{t}", [P, T], F32) for t in (2, 3)}
         w1_raw = held("w1_raw", [P, LANES, F], F32)
         w2_raw = held("w2_raw", [P, LANES, F], F32)
         dy_pool = [held(f"dy_pool{t}", [P, T], F32) for t in range(LANES)]
@@ -83,9 +85,10 @@ def tile_attend_gdepth_sil_pl_kernel(tc, xT, dyT, w1, w2, cf, gt, tx, c1, offs, 
         nc.sync.dma_start(out=gt_pool[LAST:, :], in_=gt[LAST:, :])
         nc.scalar.dma_start(out=cf_col[:], in_=cf.rearrange("(m t) o -> m (t o)", t=LANES))
         nc.scalar.dma_start(out=c1_col[:], in_=c1.rearrange("(m t) o -> m (t o)", t=LANES))
-        for u in range(2):
-            for h, piece in enumerate(x_raw[u]):
-                nc.sync.dma_start(out=piece[:], in_=x_rows[:, 2 * u : 2 * u + 2, h * X_PIECE : (h + 1) * X_PIECE])
+        for t in (2, 3):
+            nc.sync.dma_start(out=x_plane[t][:], in_=x_rows[:, t, :])
+        for h, piece in enumerate(x_raw):
+            nc.sync.dma_start(out=piece[:], in_=x_rows[:, 0:2, h * X_PIECE : (h + 1) * X_PIECE])
         nc.sync.dma_start(out=w1_raw[:], in_=w1.rearrange("(p j) f -> p j f", j=LANES))
         for t in range(LANES):
             nc.sync.dma_start(out=dy_pool[t][:], in_=dy_rows[:, t, :])
@@ -111,19 +114,22 @@ def tile_attend_gdepth_sil_pl_kernel(tc, xT, dyT, w1, w2, cf, gt, tx, c1, offs, 
         tx_cols = slot_columns("tx_got", tx_pool, 0)
         gt_cols = slot_columns("gt_got", gt_pool, 1)
 
-        x_got = held("x_got", [P, 2, N], U32)
-        for u in range(2):
-            pairs = held(f"x_pairs{u}", [P, 2 * T], BF16)
-            dst = pairs[:].rearrange("p (c i e) -> p c e i", i=RUN, e=2)
-            src = [piece[:].rearrange("p e (c i) -> p c e i", i=RUN) for piece in x_raw[u]]
-            runs = X_PIECE // RUN
-            nc.scalar.activation(out=dst[:, :runs], in_=src[0], func=ACT.Copy)
-            nc.vector.tensor_copy(out=dst[:, runs:], in_=src[1])
-            nc.vector.tensor_copy(out=x_got[:, u, :], in_=pairs[:].bitcast(U32).indirect(offsets[:]))
         x_grouped = held("x_grouped", [P, N * LANES], BF16)
+        x_lanes = x_grouped[:].rearrange("p (i t) -> p i t", t=LANES)
+        x_rounded = {t: held(f"x_rounded{t}", [P, T], BF16) for t in x_plane}
+        nc.scalar.activation(out=x_rounded[2][:], in_=x_plane[2][:], func=ACT.Copy)
+        nc.vector.tensor_copy(out=x_rounded[3][:], in_=x_plane[3][:])
+        for t in (2, 3):
+            nc.scalar.activation(out=x_lanes[:, :, t], in_=x_rounded[t][:].indirect(offsets[:]), func=ACT.Copy)
+        pairs = held("x_pairs", [P, 2 * T], BF16)
+        dst = pairs[:].rearrange("p (c i e) -> p c e i", i=RUN, e=2)
+        src = [piece[:].rearrange("p e (c i) -> p c e i", i=RUN) for piece in x_raw]
+        runs = X_PIECE // RUN
+        for h in range(T // X_PIECE):
+            nc.vector.tensor_copy(out=dst[:, h * runs : (h + 1) * runs], in_=src[h])
         nc.vector.tensor_copy(
-            out=x_grouped[:].bitcast(I32).rearrange("p (i u) -> p i u", u=2),
-            in_=x_got[:].bitcast(I32).rearrange("p u i -> p i u"),
+            out=x_grouped[:].bitcast(U32).rearrange("p (i u) -> p i u", u=2)[:, :, 0],
+            in_=pairs[:].bitcast(U32).indirect(offsets[:]),
         )
         x_mx = quantize("x", x_grouped[:], E4M3)
 
@@ -138,10 +144,11 @@ def tile_attend_gdepth_sil_pl_kernel(tc, xT, dyT, w1, w2, cf, gt, tx, c1, offs, 
         w1_grouped = held("w1_grouped", [P, F * LANES], BF16)
         w1_dst = w1_grouped[:].rearrange("p (t m j) -> p m j t", t=LANES, j=LANES)
         w1_src = w1_raw[:].rearrange("p j (m t) -> p m j t", t=LANES)
-        nc.scalar.copy(out=w1_dst, in_=w1_src)
+        nc.vector.tensor_copy(out=w1_dst[:, :W1_VECTOR], in_=w1_src[:, :W1_VECTOR])
+        nc.scalar.copy(out=w1_dst[:, W1_VECTOR:], in_=w1_src[:, W1_VECTOR:])
         w1_mx = quantize("w1", w1_grouped[:], E4M3)
 
-        factors = keep.tile([P, 3, CHUNKS], F32, name="factors", tag="w1_raw", align_bytes=64)
+        factors = keep.tile([P, 3, CHUNKS], F32, name="factors", tag="x_raw1", align_bytes=64)
         tx_neg, tx_half, gt_neg = (factors[:, k, :] for k in range(3))
         slot_factor = held("slot_factor", [P, CHUNKS], F32)
         nc.scalar.activation(out=tx_neg[:], in_=tx_cols, func=ACT.Copy, scale=-1.0)
@@ -211,7 +218,7 @@ def tile_attend_gdepth_sil_pl_kernel(tc, xT, dyT, w1, w2, cf, gt, tx, c1, offs, 
 
         activations(1)
         turn_w1(1, 1)
-        dy_got = held("dy_got", [P, LANES, N], F32)
+        dy_got = keep.tile([P, LANES, N], F32, name="dy_got", tag="w1_raw", align_bytes=64)
         for t in range(LANES):
             nc.vector.tensor_copy(out=dy_got[:, t, :], in_=dy_pool[t][:].indirect(offsets[:]))
 
@@ -223,9 +230,9 @@ def tile_attend_gdepth_sil_pl_kernel(tc, xT, dyT, w1, w2, cf, gt, tx, c1, offs, 
         w1t_mx = quantize("w1t", w1t_grouped[:], E4M3)
         slope = [held(f"slope{c}", [P, F], F32) for c in range(CHUNKS)]
         da_mx = (held("da_codes", [P, N], U32), held("da_scales", [P, N], U8))
-        da_grouped = {}
-
-        first_turned = []
+        nc.gpsimd.memset(da_mx[0][:, N // 2 :].bitcast(I32), 0)
+        nc.gpsimd.memset(da_mx[1][:, N // 2 :].bitcast(I32), 0)
+        da_grouped = held("da_grouped", [P, N * LANES], BF16)
 
         def make_slope(c):
             part = held(f"part{c}", [P, F], F32)
@@ -236,7 +243,7 @@ def tile_attend_gdepth_sil_pl_kernel(tc, xT, dyT, w1, w2, cf, gt, tx, c1, offs, 
                 out=slope[c][:], in0=tanh_half[c][:], scalar=1.0, in1=part[:], op0=ALU.add, op1=ALU.mult
             )
 
-        def make_da(c):
+        def make_da(c, turned):
             da = keep.tile([P, F], BF16, name=f"da{c}", tag=f"da{c % 2}", align_bytes=64)
             nc.vector.scalar_tensor_tensor(
                 out=da[:],
@@ -246,42 +253,45 @@ def tile_attend_gdepth_sil_pl_kernel(tc, xT, dyT, w1, w2, cf, gt, tx, c1, offs, 
                 op0=ALU.mult,
                 op1=ALU.mult,
             )
-            turned = first_turned[1] if c == CHUNKS - 1 else bank((1, 3, 4)[c])
             for u in range(2):
                 nc.tensor.transpose(turned[:, block(u)], da[:].bitcast(F32)[:, block(u)], ident[:])
-            da_grouped[c] = held(f"da_grouped{c}", [P, P * LANES], BF16)
+
+        def fetch_da(first, count, turned):
             nc.scalar.copy(
-                out=da_grouped[c][:].bitcast(F32).rearrange("p (i u) -> p i u", u=2),
-                in_=turned[:, 0 : 2 * P].rearrange("p (u i) -> p i u", u=2),
+                out=da_grouped[:].bitcast(F32)[:, first * 2 * P : (first + count) * 2 * P].rearrange(
+                    "p (c i u) -> p c i u", c=count, u=2
+                ),
+                in_=turned.rearrange("p (c u i) -> p c i u", c=count, u=2),
             )
 
-        def quantize_da(c):
+        def quantize_da(h):
+            slots = slice(h * N // 2, (h + 1) * N // 2)
             nc.vector.quantize_mx(
-                out=da_mx[0][:, block(c)].bitcast(E5M2), scales=da_mx[1][:, block(c)], in_=da_grouped[c][:]
+                out=da_mx[0][:, slots].bitcast(E5M2),
+                scales=da_mx[1][:, slots],
+                in_=da_grouped[:, h * N // 2 * LANES : (h + 1) * N // 2 * LANES],
             )
-            if c == 0:
-                dx_bank = bank(7)
-                product(dx_bank, da_mx, E5M2, block(0), w1t_mx, E4M3)
-                dx_slots = held("dx_slots", [P, D], F32)
-                nc.scalar.copy(out=dx_slots[:], in_=dx_bank[:])
-                first_turned.extend((bank(1), bank(7)))
-                for j in range(LANES):
-                    nc.tensor.transpose(first_turned[j // 2][:, block(j)], dx_slots[:, block(j)], ident[:])
 
         make_slope(0)
-        make_da(0)
+        first_bank = bank(1)
+        make_da(0, first_bank[:, : 2 * P])
         make_slope(1)
+        make_da(1, first_bank[:, 2 * P :])
+        fetch_da(0, 2, first_bank[:])
         quantize_da(0)
-        make_da(1)
         activations(2)
+        early_banks = [bank(7), bank(4)]
+        for j, early_bank in zip(PLANE_ORDER, early_banks):
+            product(early_bank, w1t_mx, E4M3, block(j), da_mx, E5M2)
         make_slope(2)
-        quantize_da(1)
-        make_da(2)
+        third_bank = bank(3)
+        make_da(2, third_bank[:, : 2 * P])
+        fetch_da(2, 1, third_bank[:, : 2 * P])
         activations(3)
         make_slope(3)
-        make_da(3)
-        quantize_da(2)
-        quantize_da(3)
+        make_da(3, early_banks[1][:, 2 * P :])
+        fetch_da(3, 1, early_banks[1][:, 2 * P :])
+        quantize_da(1)
 
         def scatter(t, first, last, dx):
             nc.vector.tensor_tensor(
@@ -291,20 +301,20 @@ def tile_attend_gdepth_sil_pl_kernel(tc, xT, dyT, w1, w2, cf, gt, tx, c1, offs, 
                 op=ALU.add,
             )
 
-        for half in range(2):
-            dx_half = keep.tile([P, 2 * P], F32, name=f"dx_half{half}", tag=(f"part{CHUNKS - 1}", "dx_late")[half], align_bytes=64)
-            nc.scalar.copy(out=dx_half[:], in_=first_turned[half][:, half * 2 * P : (half + 1) * 2 * P])
-            for e in range(2):
-                scatter(2 * half + e, 0, P, dx_half[:, block(e)])
+        for j, early_bank, tag in zip(PLANE_ORDER, early_banks, (f"part{CHUNKS - 1}", "dx_early")):
+            dx_early = keep.tile([P, N // 2], F32, name=f"dx_early{j}", tag=tag, align_bytes=64)
+            nc.scalar.copy(out=dx_early[:], in_=early_bank[:, : N // 2])
+            scatter(j, 0, N // 2, dx_early[:])
 
         dx_banks = {}
+        done = {j: N // 2 if j in PLANE_ORDER[:2] else 0 for j in PLANE_ORDER}
         for j, n in zip(PLANE_ORDER, (0, 5, 2, 3)):
             dx_banks[j] = bank(n)
             product(dx_banks[j], w1t_mx, E4M3, block(j), da_mx, E5M2)
 
         def fetch_dx(j, tag):
-            dx = keep.tile([P, N - P], F32, name=f"dx_rest{j}", tag=tag, align_bytes=64)
-            nc.scalar.copy(out=dx[:], in_=dx_banks[j][:, P:])
+            dx = keep.tile([P, N - done[j]], F32, name=f"dx_rest{j}", tag=tag, align_bytes=64)
+            nc.scalar.copy(out=dx[:], in_=dx_banks[j][:, done[j] :])
             return dx
 
         dx_rest = {j: fetch_dx(j, f"dx_rest{j}") for j in PLANE_ORDER[:-1]}
@@ -314,7 +324,7 @@ def tile_attend_gdepth_sil_pl_kernel(tc, xT, dyT, w1, w2, cf, gt, tx, c1, offs, 
         out_rows = out_0.rearrange("(p t) n -> p t n", t=LANES)
         final = PLANE_ORDER[-1]
         for t in PLANE_ORDER:
-            scatter(t, P, N, dx_rest[t][:])
+            scatter(t, done[t], N, dx_rest[t][:])
             nc.sync.dma_start(out=out_rows[:, t, :], in_=out_plane[t][:])
             if t != final:
                 nc.scalar.copy(out=out_lane[t], in_=out_plane[t][:])

@@ -24,7 +24,6 @@ CHUNKS = N // P
 QUAD = 32
 RUN = 4
 LAST = P - 1
-X_PIECE = 512
 OUT_VECTOR = 704
 WEAVE_VECTOR = 640
 PLANE_ORDER = (2, 0, 1, 3)
@@ -48,9 +47,9 @@ def tile_attend_gdepth_sil_pl_kernel(tc, xT, dyT, w1, w2, cf, gt, tx, c1, offs, 
         def block(n):
             return slice(n * P, (n + 1) * P)
 
-        def quantize(name, values, fmt):
+        def quantize(name, values, fmt, tag=""):
             width = values.shape[1] // LANES
-            codes = held(name + "_codes", [P, width], U32)
+            codes = keep.tile([P, width], U32, name=name + "_codes", tag=tag or name + "_codes", align_bytes=64)
             scales = held(name + "_scales", [P, width], U8)
             nc.vector.quantize_mx(out=codes[:].bitcast(fmt), scales=scales[:], in_=values)
             return codes, scales
@@ -71,8 +70,7 @@ def tile_attend_gdepth_sil_pl_kernel(tc, xT, dyT, w1, w2, cf, gt, tx, c1, offs, 
         c1_col = held("c1_col", [P, LANES], F32)
         tx_pool = held("tx_pool", [P, T], F32)
         gt_pool = held("gt_pool", [P, T], F32)
-        x_raw = [held(f"x_raw{h}", [P, 2, X_PIECE], F32) for h in range(T // X_PIECE)]
-        x_plane = {t: held(f"x_plane{t}", [P, T], F32) for t in (2, 3)}
+        x_plane = {t: held(f"x_plane{t}", [P, T], F32) for t in range(LANES)}
         w1_raw = held("w1_raw", [P, LANES, F], F32)
         w2_raw = held("w2_raw", [P, LANES, F], F32)
         dy_pool = [held(f"dy_pool{t}", [P, T], F32) for t in range(LANES)]
@@ -85,10 +83,8 @@ def tile_attend_gdepth_sil_pl_kernel(tc, xT, dyT, w1, w2, cf, gt, tx, c1, offs, 
         nc.sync.dma_start(out=gt_pool[LAST:, :], in_=gt[LAST:, :])
         nc.scalar.dma_start(out=cf_col[:], in_=cf.rearrange("(m t) o -> m (t o)", t=LANES))
         nc.scalar.dma_start(out=c1_col[:], in_=c1.rearrange("(m t) o -> m (t o)", t=LANES))
-        for t in (2, 3):
+        for t in (2, 3, 0, 1):
             nc.sync.dma_start(out=x_plane[t][:], in_=x_rows[:, t, :])
-        for h, piece in enumerate(x_raw):
-            nc.sync.dma_start(out=piece[:], in_=x_rows[:, 0:2, h * X_PIECE : (h + 1) * X_PIECE])
         nc.sync.dma_start(out=w1_raw[:], in_=w1.rearrange("(p j) f -> p j f", j=LANES))
         for t in range(LANES):
             nc.sync.dma_start(out=dy_pool[t][:], in_=dy_rows[:, t, :])
@@ -116,21 +112,13 @@ def tile_attend_gdepth_sil_pl_kernel(tc, xT, dyT, w1, w2, cf, gt, tx, c1, offs, 
 
         x_grouped = held("x_grouped", [P, N * LANES], BF16)
         x_lanes = x_grouped[:].rearrange("p (i t) -> p i t", t=LANES)
-        x_rounded = {t: held(f"x_rounded{t}", [P, T], BF16) for t in x_plane}
+        x_rounded = {t: held(f"x_rounded{t}", [P, T], BF16) for t in (2, 3)}
         nc.scalar.activation(out=x_rounded[2][:], in_=x_plane[2][:], func=ACT.Copy)
         nc.vector.tensor_copy(out=x_rounded[3][:], in_=x_plane[3][:])
         for t in (2, 3):
             nc.scalar.activation(out=x_lanes[:, :, t], in_=x_rounded[t][:].indirect(offsets[:]), func=ACT.Copy)
-        pairs = held("x_pairs", [P, 2 * T], BF16)
-        dst = pairs[:].rearrange("p (c i e) -> p c e i", i=RUN, e=2)
-        src = [piece[:].rearrange("p e (c i) -> p c e i", i=RUN) for piece in x_raw]
-        runs = X_PIECE // RUN
-        for h in range(T // X_PIECE):
-            nc.vector.tensor_copy(out=dst[:, h * runs : (h + 1) * runs], in_=src[h])
-        nc.vector.tensor_copy(
-            out=x_grouped[:].bitcast(U32).rearrange("p (i u) -> p i u", u=2)[:, :, 0],
-            in_=pairs[:].bitcast(U32).indirect(offsets[:]),
-        )
+        for t in (0, 1):
+            nc.vector.tensor_copy(out=x_lanes[:, :, t], in_=x_plane[t][:].indirect(offsets[:]))
         x_mx = quantize("x", x_grouped[:], E4M3)
 
         c_col = held("c_col", [P, LANES], F32)
@@ -148,7 +136,7 @@ def tile_attend_gdepth_sil_pl_kernel(tc, xT, dyT, w1, w2, cf, gt, tx, c1, offs, 
         nc.scalar.copy(out=w1_dst[:, W1_VECTOR:], in_=w1_src[:, W1_VECTOR:])
         w1_mx = quantize("w1", w1_grouped[:], E4M3)
 
-        factors = keep.tile([P, 3, CHUNKS], F32, name="factors", tag="x_raw1", align_bytes=64)
+        factors = keep.tile([P, 3, CHUNKS], F32, name="factors", tag="x_plane0", align_bytes=64)
         tx_neg, tx_half, gt_neg = (factors[:, k, :] for k in range(3))
         slot_factor = held("slot_factor", [P, CHUNKS], F32)
         nc.scalar.activation(out=tx_neg[:], in_=tx_cols, func=ACT.Copy, scale=-1.0)
@@ -180,16 +168,16 @@ def tile_attend_gdepth_sil_pl_kernel(tc, xT, dyT, w1, w2, cf, gt, tx, c1, offs, 
         silu_neg = [held(f"silu_neg{c}", [P, F], F32) for c in range(CHUNKS)]
         tanh_half = [held(f"tanh_half{c}", [P, F], F32) for c in range(CHUNKS)]
 
-        a_turned = []
+        a_turned = {}
 
         def turn_a(c):
-            a_turned.append(bank((1, 3, 4, 0)[c]))
+            a_turned[c] = bank((1, 3, 4, 0)[c])
             for t in range(LANES):
                 nc.tensor.transpose(a_turned[c][:, block(t)], a_scaled[:, t, block(c)], ident[:])
 
-        def activations(c):
+        def activations(c, which):
             in_pair_order = a_turned[c][:].rearrange("p (u e m) -> p u m e", u=2, e=2)
-            for dst, func, scale in ((silu_neg, ACT.Silu, tx_neg), (tanh_half, ACT.Tanh, tx_half)):
+            for dst, func, scale in (((silu_neg, ACT.Silu, tx_neg), (tanh_half, ACT.Tanh, tx_half))[k] for k in which):
                 nc.scalar.activation(
                     out=dst[c][:].rearrange("p (u m e) -> p u m e", u=2, e=2),
                     in_=in_pair_order,
@@ -198,36 +186,65 @@ def tile_attend_gdepth_sil_pl_kernel(tc, xT, dyT, w1, w2, cf, gt, tx, c1, offs, 
                 )
 
         def quantize_dy(h):
-            grouped = held(f"dy_grouped{h}", [P, 2 * P * LANES], BF16)
-            nc.vector.tensor_copy(
+            tag, rounding_copy = (("dy_grouped", nc.vector.tensor_copy), ("w2_grouped", nc.scalar.copy))[h]
+            grouped = keep.tile([P, 2 * P * LANES], BF16, name=f"dy_grouped{h}", tag=tag, align_bytes=64)
+            rounding_copy(
                 out=grouped[:].rearrange("p (c i t) -> p c t i", i=RUN, t=LANES),
                 in_=dy_got[:, :, 2 * P * h : 2 * P * (h + 1)].rearrange("p t (c i) -> p c t i", i=RUN),
             )
-            return quantize(f"dy{h}", grouped[:], E5M2)
+            return grouped
 
+        turn_w1(1, 5)
         turn_a(0)
-        activations(0)
-        for c in range(1, CHUNKS):
+        activations(0, (0,))
+        for c in (2, 3, 1):
             turn_a(c)
+        for c in (2, 3):
+            nc.scalar.activation(out=tanh_half[c][:], in_=a_turned[c][:], func=ACT.Tanh, scale=tx_half[:, c : c + 1])
+        activations(0, (1,))
+        activations(1, (0, 1))
+        lifted = held("lifted", [P, LANES, 2 * P], F32)
+        for u, n in ((0, 5), (1, 1)):
+            by_unit = bank(n)
+            for e in range(2):
+                t = 2 * u + e
+                for c in (2, 3):
+                    nc.tensor.transpose(by_unit[:, block(2 * e + c - 2)], tanh_half[c][:, block(t)], ident[:])
+            for e in range(2):
+                t = 2 * u + e
+                nc.scalar.activation(
+                    out=lifted[:, t, :],
+                    in_=by_unit[:, e * 2 * P : (e + 1) * 2 * P],
+                    func=ACT.Identity,
+                    scale=c_col[:, t : t + 1],
+                    bias=c_col[:, t : t + 1],
+                )
+        dy_got = keep.tile([P, LANES, N], F32, name="dy_got", tag="w1_raw", align_bytes=64)
+        for t in range(LANES - 1):
+            nc.vector.tensor_copy(out=dy_got[:, t, :], in_=dy_pool[t][:].indirect(offsets[:]))
+        for first in (0, N // 2):
+            nc.vector.tensor_copy(
+                out=dy_got[:, LANES - 1, first : first + N // 2],
+                in_=dy_pool[LANES - 1][:].indirect(offsets[:, first // 16 : (first + N // 2) // 16]),
+            )
+
+        dh_banks = []
+
+        def make_dh(dy_mx, banks):
+            for e, n in enumerate(banks):
+                dh_banks.append(bank(n))
+                product(dh_banks[-1], dy_mx, E5M2, block(e), w2_mx, E4M3)
+
+        dy_first = quantize_dy(0)
         w2_grouped = held("w2_grouped", [P, F * LANES], BF16)
         w2_dst = w2_grouped[:].rearrange("p (u m e j) -> p m j u e", u=2, e=2, j=LANES)
         w2_src = w2_raw[:].rearrange("p j (m u e) -> p m j u e", u=2, e=2)
-        nc.scalar.copy(out=w2_dst, in_=w2_src)
+        nc.vector.tensor_copy(out=w2_dst, in_=w2_src)
+        dy_first = quantize("dy0", dy_first[:], E5M2, tag="w2_raw")
         w2_mx = quantize("w2", w2_grouped[:], E4M3)
 
 
-        activations(1)
-        turn_w1(1, 1)
-        dy_got = keep.tile([P, LANES, N], F32, name="dy_got", tag="w1_raw", align_bytes=64)
-        for t in range(LANES):
-            nc.vector.tensor_copy(out=dy_got[:, t, :], in_=dy_pool[t][:].indirect(offsets[:]))
-
-        dh_banks = []
-        dy_mx = [quantize_dy(h) for h in range(2)]
-        for c in range(CHUNKS):
-            dh_banks.append(bank((6, 7, 5, 6)[c]))
-            product(dh_banks[c], dy_mx[c // 2], E5M2, block(c % 2), w2_mx, E4M3)
-        w1t_mx = quantize("w1t", w1t_grouped[:], E4M3)
+        make_dh(dy_first, (6, 7))
         slope = [held(f"slope{c}", [P, F], F32) for c in range(CHUNKS)]
         da_mx = (held("da_codes", [P, N], U32), held("da_scales", [P, N], U8))
         nc.gpsimd.memset(da_mx[0][:, N // 2 :].bitcast(I32), 0)
@@ -272,25 +289,44 @@ def tile_attend_gdepth_sil_pl_kernel(tc, xT, dyT, w1, w2, cf, gt, tx, c1, offs, 
                 in_=da_grouped[:, h * N // 2 * LANES : (h + 1) * N // 2 * LANES],
             )
 
+        def silu_only(c):
+            nc.scalar.activation(
+                out=silu_neg[c][:].rearrange("p (u m e) -> p u m e", u=2, e=2),
+                in_=a_turned[c][:].rearrange("p (u e m) -> p u m e", u=2, e=2),
+                func=ACT.Silu,
+                scale=tx_neg[:, c : c + 1],
+            )
+
+        def lifted_slope(c, n):
+            by_slot = bank(n)
+            lanes = by_slot[:].rearrange("p (u m e) -> p u e m", u=2, e=2)
+            for t in range(LANES):
+                nc.tensor.transpose(lanes[:, t // 2, t % 2, :], lifted[:, t, block(c - 2)], ident[:])
+            nc.vector.scalar_tensor_tensor(
+                out=slope[c][:], in0=silu_neg[c][:], scalar=-1.0, in1=by_slot[:], op0=ALU.add, op1=ALU.mult
+            )
+
         make_slope(0)
-        first_bank = bank(1)
-        make_da(0, first_bank[:, : 2 * P])
         make_slope(1)
+        first_bank = bank(3)
+        make_da(0, first_bank[:, : 2 * P])
         make_da(1, first_bank[:, 2 * P :])
+        w1t_mx = quantize("w1t", w1t_grouped[:], E4M3, tag="slope1")
+        make_dh(quantize("dy1", quantize_dy(1)[:], E5M2), (2, 6))
+        silu_only(2)
         fetch_da(0, 2, first_bank[:])
         quantize_da(0)
-        activations(2)
-        early_banks = [bank(7), bank(4)]
-        for j, early_bank in zip(PLANE_ORDER, early_banks):
-            product(early_bank, w1t_mx, E4M3, block(j), da_mx, E5M2)
-        make_slope(2)
-        third_bank = bank(3)
-        make_da(2, third_bank[:, : 2 * P])
-        fetch_da(2, 1, third_bank[:, : 2 * P])
-        activations(3)
-        make_slope(3)
-        make_da(3, early_banks[1][:, 2 * P :])
-        fetch_da(3, 1, early_banks[1][:, 2 * P :])
+        early_banks = [bank(7)]
+        product(early_banks[0], w1t_mx, E4M3, block(PLANE_ORDER[0]), da_mx, E5M2)
+        silu_only(3)
+        lifted_slope(2, 5)
+        lifted_slope(3, 1)
+        second_bank = bank(3)
+        make_da(2, second_bank[:, : 2 * P])
+        make_da(3, second_bank[:, 2 * P :])
+        fetch_da(2, 2, second_bank[:])
+        early_banks.append(bank(6))
+        product(early_banks[1], w1t_mx, E4M3, block(PLANE_ORDER[1]), da_mx, E5M2)
         quantize_da(1)
 
         def scatter(t, first, last, dx):
@@ -301,14 +337,14 @@ def tile_attend_gdepth_sil_pl_kernel(tc, xT, dyT, w1, w2, cf, gt, tx, c1, offs, 
                 op=ALU.add,
             )
 
-        for j, early_bank, tag in zip(PLANE_ORDER, early_banks, (f"part{CHUNKS - 1}", "dx_early")):
+        for j, early_bank, tag in zip(PLANE_ORDER, early_banks, ("slope2", "dx_early")):
             dx_early = keep.tile([P, N // 2], F32, name=f"dx_early{j}", tag=tag, align_bytes=64)
             nc.scalar.copy(out=dx_early[:], in_=early_bank[:, : N // 2])
             scatter(j, 0, N // 2, dx_early[:])
 
         dx_banks = {}
         done = {j: N // 2 if j in PLANE_ORDER[:2] else 0 for j in PLANE_ORDER}
-        for j, n in zip(PLANE_ORDER, (0, 5, 2, 3)):
+        for j, n in zip(PLANE_ORDER, (4, 0, 5, 1)):
             dx_banks[j] = bank(n)
             product(dx_banks[j], w1t_mx, E4M3, block(j), da_mx, E5M2)
 

@@ -24,8 +24,8 @@ CHUNKS = N // P
 QUAD = 32
 RUN = 4
 LAST = P - 1
-OUT_VECTOR = 704
-WEAVE_VECTOR = 640
+OUT_VECTOR = 640
+WEAVE_VECTOR = 576
 PLANE_ORDER = (2, 0, 1, 3)
 W1_VECTOR = 56
 HALF = T // 2
@@ -72,7 +72,7 @@ def tile_attend_gdepth_sil_pl_kernel(tc, xT, dyT, w1, w2, cf, gt, tx, c1, offs, 
         gt_pool = held("gt_pool", [P, T], F32)
         x_plane = {t: held(f"x_plane{t}", [P, T], F32) for t in range(LANES)}
         w1_raw = held("w1_raw", [P, LANES, F], F32)
-        w2_raw = held("w2_raw", [P, LANES, F], F32)
+        w2_raw = [held(f"w2_raw{h}", [P, LANES, F // 2], F32) for h in range(2)]
         dy_pool = [held(f"dy_pool{t}", [P, T], F32) for t in range(LANES)]
         out_plane = [held(f"out_plane{t}", [P, T], F32) for t in range(LANES)]
         x_rows = xT.rearrange("(p t) n -> p t n", t=LANES)
@@ -86,9 +86,11 @@ def tile_attend_gdepth_sil_pl_kernel(tc, xT, dyT, w1, w2, cf, gt, tx, c1, offs, 
         for t in (2, 3, 0, 1):
             nc.sync.dma_start(out=x_plane[t][:], in_=x_rows[:, t, :])
         nc.sync.dma_start(out=w1_raw[:], in_=w1.rearrange("(p j) f -> p j f", j=LANES))
+        w2_rows = w2.rearrange("(p j) (h f) -> h p j f", j=LANES, h=2)
+        nc.sync.dma_start(out=w2_raw[0][:], in_=w2_rows[0])
         for t in range(LANES):
             nc.sync.dma_start(out=dy_pool[t][:], in_=dy_rows[:, t, :])
-        nc.sync.dma_start(out=w2_raw[:], in_=w2.rearrange("(p j) f -> p j f", j=LANES))
+        nc.sync.dma_start(out=w2_raw[1][:], in_=w2_rows[1])
         for t in range(LANES):
             nc.sync.dma_start(out=out_plane[t][:], in_=dy_rows[:, t, :])
 
@@ -135,6 +137,11 @@ def tile_attend_gdepth_sil_pl_kernel(tc, xT, dyT, w1, w2, cf, gt, tx, c1, offs, 
         nc.vector.tensor_copy(out=w1_dst[:, :W1_VECTOR], in_=w1_src[:, :W1_VECTOR])
         nc.scalar.copy(out=w1_dst[:, W1_VECTOR:], in_=w1_src[:, W1_VECTOR:])
         w1_mx = quantize("w1", w1_grouped[:], E4M3)
+
+        w2_grouped = held("w2_grouped", [P, F * LANES], BF16)
+        w2_dst = w2_grouped[:].rearrange("p (u m e j) -> p m j u e", u=2, e=2, j=LANES)
+        w2_src = [half[:].rearrange("p j (m u e) -> p m j u e", u=2, e=2) for half in w2_raw]
+        nc.scalar.copy(out=w2_dst[:, : P // 2], in_=w2_src[0])
 
         factors = keep.tile([P, 3, CHUNKS], F32, name="factors", tag="x_plane0", align_bytes=64)
         tx_neg, tx_half, gt_neg = (factors[:, k, :] for k in range(3))
@@ -236,11 +243,8 @@ def tile_attend_gdepth_sil_pl_kernel(tc, xT, dyT, w1, w2, cf, gt, tx, c1, offs, 
                 product(dh_banks[-1], dy_mx, E5M2, block(e), w2_mx, E4M3)
 
         dy_first = quantize_dy(0)
-        w2_grouped = held("w2_grouped", [P, F * LANES], BF16)
-        w2_dst = w2_grouped[:].rearrange("p (u m e j) -> p m j u e", u=2, e=2, j=LANES)
-        w2_src = w2_raw[:].rearrange("p j (m u e) -> p m j u e", u=2, e=2)
-        nc.vector.tensor_copy(out=w2_dst, in_=w2_src)
-        dy_first = quantize("dy0", dy_first[:], E5M2, tag="w2_raw")
+        nc.vector.tensor_copy(out=w2_dst[:, P // 2 :], in_=w2_src[1])
+        dy_first = quantize("dy0", dy_first[:], E5M2, tag="w2_raw1")
         w2_mx = quantize("w2", w2_grouped[:], E4M3)
 
 
@@ -337,7 +341,7 @@ def tile_attend_gdepth_sil_pl_kernel(tc, xT, dyT, w1, w2, cf, gt, tx, c1, offs, 
                 op=ALU.add,
             )
 
-        for j, early_bank, tag in zip(PLANE_ORDER, early_banks, ("slope2", "dx_early")):
+        for j, early_bank, tag in zip(PLANE_ORDER, early_banks, ("silu_neg3", "dx_early")):
             dx_early = keep.tile([P, N // 2], F32, name=f"dx_early{j}", tag=tag, align_bytes=64)
             nc.scalar.copy(out=dx_early[:], in_=early_bank[:, : N // 2])
             scatter(j, 0, N // 2, dx_early[:])

@@ -21,14 +21,15 @@ F = 512
 T = 1024
 N = 512
 CHUNKS = N // P
+HALF = N // 2
+BAND = 16
 QUAD = 32
 RUN = 4
 LAST = P - 1
-OUT_VECTOR = 640
+W1_VECTOR = 56
+LAST_VECTOR = 640
 WEAVE_VECTOR = 576
 PLANE_ORDER = (2, 0, 1, 3)
-W1_VECTOR = 56
-HALF = T // 2
 FLOPS = 3 * 2 * D * F * N
 
 
@@ -37,19 +38,34 @@ def tile_attend_gdepth_sil_pl_kernel(tc, xT, dyT, w1, w2, cf, gt, tx, c1, offs, 
     with ExitStack() as ctx:
         keep = ctx.enter_context(tc.tile_pool(name="keep", bufs=1))
         psum = ctx.enter_context(tc.psum_pool(name="psum", bufs=1))
+        place = {}
 
-        def held(name, shape, dtype):
-            return keep.tile(shape, dtype, name=name, align_bytes=64)
+        def held(name, shape, dtype, replaces=""):
+            place[name] = place.get(replaces, name)
+            return keep.tile(shape, dtype, name=name, tag=place[name], align_bytes=64)
 
-        def bank(n):
-            return psum.tile([P, 512], F32, name=f"bank{n}", tag=f"bank{n}")
+        def bank(name, replaces=""):
+            place[name] = place.get(replaces, name)
+            return psum.tile([P, 512], F32, name=name, tag=place[name])
 
         def block(n):
             return slice(n * P, (n + 1) * P)
 
-        def quantize(name, values, fmt, tag=""):
+        def half(h):
+            return slice(h * HALF, (h + 1) * HALF)
+
+        def entries(first, last):
+            return offsets[:, first // BAND : last // BAND]
+
+        def in_pair_order(lane_ordered):
+            return lane_ordered.rearrange("p (u e m) -> p u m e", u=2, e=2)
+
+        def pair_places(pair_ordered):
+            return pair_ordered.rearrange("p (u m e) -> p u e m", u=2, e=2)
+
+        def quantize(name, values, fmt, replaces=""):
             width = values.shape[1] // LANES
-            codes = keep.tile([P, width], U32, name=name + "_codes", tag=tag or name + "_codes", align_bytes=64)
+            codes = held(name + "_codes", [P, width], U32, replaces)
             scales = held(name + "_scales", [P, width], U8)
             nc.vector.quantize_mx(out=codes[:].bitcast(fmt), scales=scales[:], in_=values)
             return codes, scales
@@ -65,28 +81,29 @@ def tile_attend_gdepth_sil_pl_kernel(tc, xT, dyT, w1, w2, cf, gt, tx, c1, offs, 
                 stop=True,
             )
 
-        offsets = keep.tile([P, N // 16], U16, name="offsets")
+        offsets = keep.tile([P, N // BAND], U16, name="offsets")
         cf_col = held("cf_col", [P, LANES], F32)
         c1_col = held("c1_col", [P, LANES], F32)
         tx_pool = held("tx_pool", [P, T], F32)
         gt_pool = held("gt_pool", [P, T], F32)
-        x_plane = {t: held(f"x_plane{t}", [P, T], F32) for t in range(LANES)}
+        x_plane = [held(f"x_plane{t}", [P, T], F32) for t in range(LANES)]
         w1_raw = held("w1_raw", [P, LANES, F], F32)
         w2_raw = [held(f"w2_raw{h}", [P, LANES, F // 2], F32) for h in range(2)]
         dy_pool = [held(f"dy_pool{t}", [P, T], F32) for t in range(LANES)]
         out_plane = [held(f"out_plane{t}", [P, T], F32) for t in range(LANES)]
         x_rows = xT.rearrange("(p t) n -> p t n", t=LANES)
         dy_rows = dyT.rearrange("(p t) n -> p t n", t=LANES)
+        w2_rows = w2.rearrange("(p j) (h f) -> h p j f", j=LANES, h=2)
+        scalar_lanes, vector_lanes = (2, 3), (0, 1)
 
         nc.sync.dma_start(offsets[:], offs)
         nc.sync.dma_start(out=tx_pool[LAST:, :], in_=tx[LAST:, :])
         nc.sync.dma_start(out=gt_pool[LAST:, :], in_=gt[LAST:, :])
         nc.scalar.dma_start(out=cf_col[:], in_=cf.rearrange("(m t) o -> m (t o)", t=LANES))
         nc.scalar.dma_start(out=c1_col[:], in_=c1.rearrange("(m t) o -> m (t o)", t=LANES))
-        for t in (2, 3, 0, 1):
+        for t in scalar_lanes + vector_lanes:
             nc.sync.dma_start(out=x_plane[t][:], in_=x_rows[:, t, :])
         nc.sync.dma_start(out=w1_raw[:], in_=w1.rearrange("(p j) f -> p j f", j=LANES))
-        w2_rows = w2.rearrange("(p j) (h f) -> h p j f", j=LANES, h=2)
         nc.sync.dma_start(out=w2_raw[0][:], in_=w2_rows[0])
         for t in range(LANES):
             nc.sync.dma_start(out=dy_pool[t][:], in_=dy_rows[:, t, :])
@@ -101,35 +118,35 @@ def tile_attend_gdepth_sil_pl_kernel(tc, xT, dyT, w1, w2, cf, gt, tx, c1, offs, 
 
         warm = held("warm", [P, 1], F32)
         nc.scalar.activation(out=warm[:QUAD, :], in_=tx_pool[:QUAD, 0:1], func=ACT.Silu)
-        def slot_columns(name, pool_tile, n):
-            got = held(name, [P, N], F32)
+
+        def slot_columns(name, pool_tile):
+            got = held(name + "_got", [P, N], F32)
             nc.vector.tensor_copy(out=got[:], in_=pool_tile[:].indirect(offsets[:]))
-            turned = bank(n)
+            turned = bank(name + "_turned")
             for c in range(CHUNKS):
                 nc.tensor.transpose(turned[:, block(c)], got[:, block(c)], ident[:])
             return turned[:].rearrange("p (c r) -> p c r", r=P)[:, :, LAST]
 
-        tx_cols = slot_columns("tx_got", tx_pool, 0)
-        gt_cols = slot_columns("gt_got", gt_pool, 1)
+        tx_cols = slot_columns("tx", tx_pool)
+        gt_cols = slot_columns("gt", gt_pool)
 
         x_grouped = held("x_grouped", [P, N * LANES], BF16)
         x_lanes = x_grouped[:].rearrange("p (i t) -> p i t", t=LANES)
-        x_rounded = {t: held(f"x_rounded{t}", [P, T], BF16) for t in (2, 3)}
+        x_rounded = {t: held(f"x_rounded{t}", [P, T], BF16) for t in scalar_lanes}
         nc.scalar.activation(out=x_rounded[2][:], in_=x_plane[2][:], func=ACT.Copy)
         nc.vector.tensor_copy(out=x_rounded[3][:], in_=x_plane[3][:])
-        for t in (2, 3):
+        for t in scalar_lanes:
             nc.scalar.activation(out=x_lanes[:, :, t], in_=x_rounded[t][:].indirect(offsets[:]), func=ACT.Copy)
-        for t in (0, 1):
+        for t in vector_lanes:
             nc.vector.tensor_copy(out=x_lanes[:, :, t], in_=x_plane[t][:].indirect(offsets[:]))
         x_mx = quantize("x", x_grouped[:], E4M3)
 
         c_col = held("c_col", [P, LANES], F32)
         nc.gpsimd.tensor_tensor(out=c_col[:], in0=c1_col[:], in1=cf_col[:], op=ALU.mult)
-        c_turned = bank(2)
-        c_lanes = c_turned[:].rearrange("p (u m e) -> p u e m", u=2, e=2)
+        c_row = bank("c_row")
         for t in range(LANES):
-            nc.tensor.transpose(c_lanes[:, t // 2, t % 2, :], c_col[:, t : t + 1].to_broadcast([P, P]), ident[:])
-        c_row = c_turned
+            repeated = c_col[:, t : t + 1].to_broadcast([P, P])
+            nc.tensor.transpose(pair_places(c_row[:])[:, t // 2, t % 2, :], repeated, ident[:])
 
         w1_grouped = held("w1_grouped", [P, F * LANES], BF16)
         w1_dst = w1_grouped[:].rearrange("p (t m j) -> p m j t", t=LANES, j=LANES)
@@ -140,10 +157,10 @@ def tile_attend_gdepth_sil_pl_kernel(tc, xT, dyT, w1, w2, cf, gt, tx, c1, offs, 
 
         w2_grouped = held("w2_grouped", [P, F * LANES], BF16)
         w2_dst = w2_grouped[:].rearrange("p (u m e j) -> p m j u e", u=2, e=2, j=LANES)
-        w2_src = [half[:].rearrange("p j (m u e) -> p m j u e", u=2, e=2) for half in w2_raw]
+        w2_src = [part[:].rearrange("p j (m u e) -> p m j u e", u=2, e=2) for part in w2_raw]
         nc.scalar.copy(out=w2_dst[:, : P // 2], in_=w2_src[0])
 
-        factors = keep.tile([P, 3, CHUNKS], F32, name="factors", tag="x_plane0", align_bytes=64)
+        factors = held("factors", [P, 3, CHUNKS], F32, replaces="x_plane0")
         tx_neg, tx_half, gt_neg = (factors[:, k, :] for k in range(3))
         slot_factor = held("slot_factor", [P, CHUNKS], F32)
         nc.scalar.activation(out=tx_neg[:], in_=tx_cols, func=ACT.Copy, scale=-1.0)
@@ -152,110 +169,106 @@ def tile_attend_gdepth_sil_pl_kernel(tc, xT, dyT, w1, w2, cf, gt, tx, c1, offs, 
         nc.gpsimd.tensor_tensor(out=slot_factor[:], in0=gt_neg[:], in1=tx_half[:], op=ALU.mult)
 
         w1t_grouped = held("w1t_grouped", [P, D * LANES], BF16)
+        w1t_pairs = w1t_grouped[:].rearrange("p (h b q t) -> p h q t b", h=2, b=2, t=LANES)
         w1_words = w1_grouped[:].bitcast(F32).rearrange("p (t m h) -> p h t m", t=LANES, h=2)
 
-        def turn_w1(h, n):
-            turned = bank(n)
+        def turn_w1(h, replaces=""):
+            turned = bank(f"w1_turned{h}", replaces)
             for t in range(LANES):
                 nc.tensor.transpose(turned[:, block(t)], w1_words[:, h, t, :], ident[:])
             nc.scalar.copy(
-                out=w1t_grouped[:, h * 1024 : (h + 1) * 1024].rearrange("p (b q t) -> p q t b", b=2, t=LANES),
-                in_=turned[:].bitcast(BF16).rearrange("p (t q b) -> p q t b", t=LANES, b=2),
+                out=w1t_pairs[:, h], in_=turned[:].bitcast(BF16).rearrange("p (t q b) -> p q t b", t=LANES, b=2)
             )
 
-
-        turn_w1(0, 4)
+        turn_w1(0)
 
         a_scaled = held("a_scaled", [P, LANES, N], F32)
         for t in range(LANES):
-            a_bank = bank((5 + t) % 8)
+            a_bank = bank(f"a{t}", replaces="tx_turned" if t == LANES - 1 else "")
             product(a_bank, w1_mx, E4M3, block(t), x_mx, E4M3)
             nc.scalar.activation(out=a_scaled[:, t, :], in_=a_bank[:], func=ACT.Copy, scale=cf_col[:, t : t + 1])
 
         silu_neg = [held(f"silu_neg{c}", [P, F], F32) for c in range(CHUNKS)]
         tanh_half = [held(f"tanh_half{c}", [P, F], F32) for c in range(CHUNKS)]
-
         a_turned = {}
 
-        def turn_a(c):
-            a_turned[c] = bank((1, 3, 4, 0)[c])
+        def turn_a(c, replaces=""):
+            a_turned[c] = bank(f"a_turned{c}", replaces)
             for t in range(LANES):
                 nc.tensor.transpose(a_turned[c][:, block(t)], a_scaled[:, t, block(c)], ident[:])
 
-        def activations(c, which):
-            in_pair_order = a_turned[c][:].rearrange("p (u e m) -> p u m e", u=2, e=2)
-            for dst, func, scale in (((silu_neg, ACT.Silu, tx_neg), (tanh_half, ACT.Tanh, tx_half))[k] for k in which):
-                nc.scalar.activation(
-                    out=dst[c][:].rearrange("p (u m e) -> p u m e", u=2, e=2),
-                    in_=in_pair_order,
-                    func=func,
-                    scale=scale[:, c : c + 1],
-                )
-
-        def quantize_dy(h):
-            tag, rounding_copy = (("dy_grouped", nc.vector.tensor_copy), ("w2_grouped", nc.scalar.copy))[h]
-            grouped = keep.tile([P, 2 * P * LANES], BF16, name=f"dy_grouped{h}", tag=tag, align_bytes=64)
-            rounding_copy(
-                out=grouped[:].rearrange("p (c i t) -> p c t i", i=RUN, t=LANES),
-                in_=dy_got[:, :, 2 * P * h : 2 * P * (h + 1)].rearrange("p t (c i) -> p c t i", i=RUN),
+        def paired_activation(out, c, func, scale):
+            nc.scalar.activation(
+                out=out[c][:].rearrange("p (u m e) -> p u m e", u=2, e=2),
+                in_=in_pair_order(a_turned[c][:]),
+                func=func,
+                scale=scale[:, c : c + 1],
             )
-            return grouped
 
-        turn_w1(1, 5)
-        turn_a(0)
-        activations(0, (0,))
-        for c in (2, 3, 1):
-            turn_a(c)
+        turn_w1(1, replaces="a0")
+        turn_a(0, replaces="gt_turned")
+        paired_activation(silu_neg, 0, ACT.Silu, tx_neg)
+        turn_a(2, replaces="w1_turned0")
+        turn_a(3, replaces="a3")
+        turn_a(1)
         for c in (2, 3):
             nc.scalar.activation(out=tanh_half[c][:], in_=a_turned[c][:], func=ACT.Tanh, scale=tx_half[:, c : c + 1])
-        activations(0, (1,))
-        activations(1, (0, 1))
-        lifted = held("lifted", [P, LANES, 2 * P], F32)
-        for u, n in ((0, 5), (1, 1)):
-            by_unit = bank(n)
+        paired_activation(tanh_half, 0, ACT.Tanh, tx_half)
+        paired_activation(silu_neg, 1, ACT.Silu, tx_neg)
+        paired_activation(tanh_half, 1, ACT.Tanh, tx_half)
+
+        lifted = held("lifted", [P, LANES, HALF], F32)
+        for u, replaces in enumerate(("w1_turned1", "a_turned0")):
+            tanh_turned = bank(f"tanh_turned{u}", replaces)
             for e in range(2):
-                t = 2 * u + e
                 for c in (2, 3):
-                    nc.tensor.transpose(by_unit[:, block(2 * e + c - 2)], tanh_half[c][:, block(t)], ident[:])
+                    nc.tensor.transpose(tanh_turned[:, block(2 * e + c - 2)], tanh_half[c][:, block(2 * u + e)], ident[:])
             for e in range(2):
                 t = 2 * u + e
                 nc.scalar.activation(
                     out=lifted[:, t, :],
-                    in_=by_unit[:, e * 2 * P : (e + 1) * 2 * P],
+                    in_=tanh_turned[:, half(e)],
                     func=ACT.Identity,
                     scale=c_col[:, t : t + 1],
                     bias=c_col[:, t : t + 1],
                 )
-        dy_got = keep.tile([P, LANES, N], F32, name="dy_got", tag="w1_raw", align_bytes=64)
+
+        dy_got = held("dy_got", [P, LANES, N], F32, replaces="w1_raw")
         for t in range(LANES - 1):
             nc.vector.tensor_copy(out=dy_got[:, t, :], in_=dy_pool[t][:].indirect(offsets[:]))
-        for first in (0, N // 2):
-            nc.vector.tensor_copy(
-                out=dy_got[:, LANES - 1, first : first + N // 2],
-                in_=dy_pool[LANES - 1][:].indirect(offsets[:, first // 16 : (first + N // 2) // 16]),
+        for h in range(2):
+            window = dy_pool[LANES - 1][:].indirect(entries(h * HALF, (h + 1) * HALF))
+            nc.vector.tensor_copy(out=dy_got[:, LANES - 1, half(h)], in_=window)
+
+        def round_dy(h, rounding_copy, replaces=""):
+            grouped = held(f"dy_grouped{h}", [P, HALF * LANES], BF16, replaces)
+            rounding_copy(
+                out=grouped[:].rearrange("p (c i t) -> p c t i", i=RUN, t=LANES),
+                in_=dy_got[:, :, half(h)].rearrange("p t (c i) -> p c t i", i=RUN),
             )
+            return grouped
 
         dh_banks = []
 
-        def make_dh(dy_mx, banks):
-            for e, n in enumerate(banks):
-                dh_banks.append(bank(n))
+        def make_dh(dy_mx, replaced):
+            for e, replaces in enumerate(replaced):
+                dh_banks.append(bank(f"dh{len(dh_banks)}", replaces))
                 product(dh_banks[-1], dy_mx, E5M2, block(e), w2_mx, E4M3)
 
-        dy_first = quantize_dy(0)
+        dy_rounded = round_dy(0, nc.vector.tensor_copy)
         nc.vector.tensor_copy(out=w2_dst[:, P // 2 :], in_=w2_src[1])
-        dy_first = quantize("dy0", dy_first[:], E5M2, tag="w2_raw1")
+        dy0_mx = quantize("dy0", dy_rounded[:], E5M2, replaces="w2_raw1")
         w2_mx = quantize("w2", w2_grouped[:], E4M3)
+        make_dh(dy0_mx, ("a1", "a2"))
 
-
-        make_dh(dy_first, (6, 7))
         slope = [held(f"slope{c}", [P, F], F32) for c in range(CHUNKS)]
         da_mx = (held("da_codes", [P, N], U32), held("da_scales", [P, N], U8))
-        nc.gpsimd.memset(da_mx[0][:, N // 2 :].bitcast(I32), 0)
-        nc.gpsimd.memset(da_mx[1][:, N // 2 :].bitcast(I32), 0)
+        nc.gpsimd.memset(da_mx[0][:, half(1)].bitcast(I32), 0)
+        nc.gpsimd.memset(da_mx[1][:, half(1)].bitcast(I32), 0)
         da_grouped = held("da_grouped", [P, N * LANES], BF16)
+        da_words = da_grouped[:].bitcast(F32).rearrange("p (c i u) -> p c i u", c=CHUNKS, u=2)
 
-        def make_slope(c):
+        def plain_slope(c):
             part = held(f"part{c}", [P, F], F32)
             nc.vector.scalar_tensor_tensor(
                 out=part[:], in0=silu_neg[c][:], scalar=-1.0, in1=c_row[:], op0=ALU.add, op1=ALU.mult
@@ -264,8 +277,18 @@ def tile_attend_gdepth_sil_pl_kernel(tc, xT, dyT, w1, w2, cf, gt, tx, c1, offs, 
                 out=slope[c][:], in0=tanh_half[c][:], scalar=1.0, in1=part[:], op0=ALU.add, op1=ALU.mult
             )
 
+        def lifted_slope(c, replaces):
+            lifted_back = bank(f"lifted_back{c}", replaces)
+            for t in range(LANES):
+                nc.tensor.transpose(
+                    pair_places(lifted_back[:])[:, t // 2, t % 2, :], lifted[:, t, block(c - 2)], ident[:]
+                )
+            nc.vector.scalar_tensor_tensor(
+                out=slope[c][:], in0=silu_neg[c][:], scalar=-1.0, in1=lifted_back[:], op0=ALU.add, op1=ALU.mult
+            )
+
         def make_da(c, turned):
-            da = keep.tile([P, F], BF16, name=f"da{c}", tag=f"da{c % 2}", align_bytes=64)
+            da = held(f"da{c}", [P, F], BF16, replaces=f"da{c - 2}")
             nc.vector.scalar_tensor_tensor(
                 out=da[:],
                 in0=dh_banks[c][:],
@@ -279,112 +302,88 @@ def tile_attend_gdepth_sil_pl_kernel(tc, xT, dyT, w1, w2, cf, gt, tx, c1, offs, 
 
         def fetch_da(first, count, turned):
             nc.scalar.copy(
-                out=da_grouped[:].bitcast(F32)[:, first * 2 * P : (first + count) * 2 * P].rearrange(
-                    "p (c i u) -> p c i u", c=count, u=2
-                ),
-                in_=turned.rearrange("p (c u i) -> p c i u", c=count, u=2),
+                out=da_words[:, first : first + count], in_=turned.rearrange("p (c u i) -> p c i u", c=count, u=2)
             )
 
         def quantize_da(h):
-            slots = slice(h * N // 2, (h + 1) * N // 2)
             nc.vector.quantize_mx(
-                out=da_mx[0][:, slots].bitcast(E5M2),
-                scales=da_mx[1][:, slots],
-                in_=da_grouped[:, h * N // 2 * LANES : (h + 1) * N // 2 * LANES],
+                out=da_mx[0][:, half(h)].bitcast(E5M2),
+                scales=da_mx[1][:, half(h)],
+                in_=da_grouped[:, h * HALF * LANES : (h + 1) * HALF * LANES],
             )
 
-        def silu_only(c):
-            nc.scalar.activation(
-                out=silu_neg[c][:].rearrange("p (u m e) -> p u m e", u=2, e=2),
-                in_=a_turned[c][:].rearrange("p (u e m) -> p u m e", u=2, e=2),
-                func=ACT.Silu,
-                scale=tx_neg[:, c : c + 1],
-            )
+        def make_dx(name, j, replaces):
+            dx_bank = bank(name, replaces)
+            product(dx_bank, w1t_mx, E4M3, block(j), da_mx, E5M2)
+            return dx_bank
 
-        def lifted_slope(c, n):
-            by_slot = bank(n)
-            lanes = by_slot[:].rearrange("p (u m e) -> p u e m", u=2, e=2)
-            for t in range(LANES):
-                nc.tensor.transpose(lanes[:, t // 2, t % 2, :], lifted[:, t, block(c - 2)], ident[:])
-            nc.vector.scalar_tensor_tensor(
-                out=slope[c][:], in0=silu_neg[c][:], scalar=-1.0, in1=by_slot[:], op0=ALU.add, op1=ALU.mult
-            )
-
-        make_slope(0)
-        make_slope(1)
-        first_bank = bank(3)
-        make_da(0, first_bank[:, : 2 * P])
-        make_da(1, first_bank[:, 2 * P :])
-        w1t_mx = quantize("w1t", w1t_grouped[:], E4M3, tag="slope1")
-        make_dh(quantize("dy1", quantize_dy(1)[:], E5M2), (2, 6))
-        silu_only(2)
-        fetch_da(0, 2, first_bank[:])
+        plain_slope(0)
+        plain_slope(1)
+        for c, replaces in enumerate(("a_turned1", "dh1")):
+            da_turned = bank(f"da_turned{c}", replaces)
+            make_da(c, da_turned[:, half(0)])
+            fetch_da(c, 1, da_turned[:, half(0)])
+        w1t_mx = quantize("w1t", w1t_grouped[:], E4M3, replaces="slope1")
+        dy_rounded = round_dy(1, nc.scalar.copy, replaces="w2_grouped")
+        make_dh(quantize("dy1", dy_rounded[:], E5M2), ("c_row", "dh0"))
+        paired_activation(silu_neg, 2, ACT.Silu, tx_neg)
         quantize_da(0)
-        early_banks = [bank(7)]
-        product(early_banks[0], w1t_mx, E4M3, block(PLANE_ORDER[0]), da_mx, E5M2)
-        silu_only(3)
-        lifted_slope(2, 5)
-        lifted_slope(3, 1)
-        second_bank = bank(3)
-        make_da(2, second_bank[:, : 2 * P])
-        make_da(3, second_bank[:, 2 * P :])
-        fetch_da(2, 2, second_bank[:])
-        early_banks.append(bank(6))
-        product(early_banks[1], w1t_mx, E4M3, block(PLANE_ORDER[1]), da_mx, E5M2)
+        early_banks = [make_dx("dx_early0", PLANE_ORDER[0], replaces="da_turned0")]
+
+        paired_activation(silu_neg, 3, ACT.Silu, tx_neg)
+        lifted_slope(2, replaces="tanh_turned0")
+        lifted_slope(3, replaces="tanh_turned1")
+        da_turned = bank("da_turned23", replaces="da_turned1")
+        make_da(2, da_turned[:, half(0)])
+        make_da(3, da_turned[:, half(1)])
+        fetch_da(2, 2, da_turned[:])
+        early_banks.append(make_dx("dx_early1", PLANE_ORDER[1], replaces="dh3"))
         quantize_da(1)
+
+        def fetch_dx(name, dx_bank, first, last, replaces=""):
+            dx = held(name, [P, last - first], F32, replaces)
+            nc.scalar.copy(out=dx[:], in_=dx_bank[:, first:last])
+            return dx
 
         def scatter(t, first, last, dx):
             nc.vector.tensor_tensor(
-                out=out_plane[t][:].indirect(offsets[:, first // 16 : last // 16]),
-                in0=dx,
-                in1=dy_got[:, t, first:last],
-                op=ALU.add,
+                out=out_plane[t][:].indirect(entries(first, last)), in0=dx[:], in1=dy_got[:, t, first:last], op=ALU.add
             )
 
-        for j, early_bank, tag in zip(PLANE_ORDER, early_banks, ("silu_neg3", "dx_early")):
-            dx_early = keep.tile([P, N // 2], F32, name=f"dx_early{j}", tag=tag, align_bytes=64)
-            nc.scalar.copy(out=dx_early[:], in_=early_bank[:, : N // 2])
-            scatter(j, 0, N // 2, dx_early[:])
+        for k, replaces in enumerate(("silu_neg3", "")):
+            scatter(PLANE_ORDER[k], 0, HALF, fetch_dx(f"dx_first{k}", early_banks[k], 0, HALF, replaces))
 
-        dx_banks = {}
-        done = {j: N // 2 if j in PLANE_ORDER[:2] else 0 for j in PLANE_ORDER}
-        for j, n in zip(PLANE_ORDER, (4, 0, 5, 1)):
-            dx_banks[j] = bank(n)
-            product(dx_banks[j], w1t_mx, E4M3, block(j), da_mx, E5M2)
+        done = {t: HALF if t in PLANE_ORDER[:2] else 0 for t in PLANE_ORDER}
+        freed = ("a_turned2", "a_turned3", "lifted_back2", "lifted_back3")
+        dx_banks = {t: make_dx(f"dx{t}", t, replaces) for t, replaces in zip(PLANE_ORDER, freed)}
+        first_plane, last_plane = PLANE_ORDER[0], PLANE_ORDER[-1]
+        dx_rest = {t: fetch_dx(f"dx_rest{t}", dx_banks[t], done[t], N) for t in PLANE_ORDER[:-1]}
 
-        def fetch_dx(j, tag):
-            dx = keep.tile([P, N - done[j]], F32, name=f"dx_rest{j}", tag=tag, align_bytes=64)
-            nc.scalar.copy(out=dx[:], in_=dx_banks[j][:, done[j] :])
-            return dx
-
-        dx_rest = {j: fetch_dx(j, f"dx_rest{j}") for j in PLANE_ORDER[:-1]}
-
-        out_pairs = keep.tile([P, 2, 2 * T], BF16, name="out_pairs", tag="dy_pool0", align_bytes=64)
+        out_pairs = held("out_pairs", [P, 2, 2 * T], BF16, replaces="dy_pool0")
         out_lane = [out_pairs[:, t // 2, :].rearrange("p (n e) -> p n e", e=2)[:, :, t % 2] for t in range(LANES)]
         out_rows = out_0.rearrange("(p t) n -> p t n", t=LANES)
-        final = PLANE_ORDER[-1]
         for t in PLANE_ORDER:
-            scatter(t, done[t], N, dx_rest[t][:])
+            scatter(t, done[t], N, dx_rest[t])
             nc.sync.dma_start(out=out_rows[:, t, :], in_=out_plane[t][:])
-            if t != final:
+            if t != last_plane:
                 nc.scalar.copy(out=out_lane[t], in_=out_plane[t][:])
-            if t == PLANE_ORDER[0]:
-                dx_rest[final] = fetch_dx(final, f"dx_rest{t}")
-        nc.scalar.copy(out=out_lane[final][:, OUT_VECTOR:], in_=out_plane[final][:, OUT_VECTOR:])
-        for cols in (slice(0, HALF), slice(HALF, OUT_VECTOR)):
-            nc.vector.tensor_copy(out=out_lane[final][:, cols], in_=out_plane[final][:, cols])
+            if t == first_plane:
+                dx_rest[last_plane] = fetch_dx("dx_last", dx_banks[last_plane], 0, N, replaces=f"dx_rest{t}")
+        nc.scalar.copy(out=out_lane[last_plane][:, LAST_VECTOR:], in_=out_plane[last_plane][:, LAST_VECTOR:])
+        for cols in (slice(0, T // 2), slice(T // 2, LAST_VECTOR)):
+            nc.vector.tensor_copy(out=out_lane[last_plane][:, cols], in_=out_plane[last_plane][:, cols])
 
         out_grouped = held("out_grouped", [P, T * LANES], BF16)
         woven = out_grouped[:].bitcast(U32).rearrange("p (n u) -> p n u", u=2)
         pair_words = out_pairs[:].bitcast(U32).rearrange("p u n -> p n u")
         nc.scalar.copy(out=woven[:, WEAVE_VECTOR:], in_=pair_words[:, WEAVE_VECTOR:])
-        for cols in (slice(0, HALF), slice(HALF, WEAVE_VECTOR)):
+        for cols in (slice(0, T // 2), slice(T // 2, WEAVE_VECTOR)):
             nc.vector.tensor_copy(out=woven[:, cols].bitcast(I32), in_=pair_words[:, cols].bitcast(I32))
 
         out_codes = held("out_codes", [P, T], U32)
         out_scales = held("out_scales", [P, T], U8)
         words_hbm = out_1[0].rearrange("p n l -> p (n l)").bitcast(I32)
-        for first, last in ((0, HALF), (HALF, 3 * T // 4), (3 * T // 4, T)):
+        for first, last in ((0, T // 2), (T // 2, 3 * T // 4), (3 * T // 4, T)):
             cols = slice(first, last)
             nc.vector.quantize_mx(
                 out=out_codes[:, cols].bitcast(E4M3),
@@ -393,6 +392,6 @@ def tile_attend_gdepth_sil_pl_kernel(tc, xT, dyT, w1, w2, cf, gt, tx, c1, offs, 
             )
             nc.sync.dma_start(out=words_hbm[:, cols], in_=out_codes[:, cols].bitcast(I32))
         scales_hbm = out_2[0].bitcast(I32)
-        for q in range(4):
+        for q in range(P // QUAD):
             queue = (nc.scalar, nc.sync)[q % 2]
             queue.dma_start(out=scales_hbm[4 * q : 4 * q + 4, :], in_=out_scales[QUAD * q : QUAD * q + 4, :].bitcast(I32))

@@ -26,10 +26,10 @@ BAND = 16
 QUAD = 32
 RUN = 4
 LAST = P - 1
-W1_VECTOR = 56
 LAST_VECTOR = 640
 WEAVE_VECTOR = 576
 PLANE_ORDER = (2, 0, 1, 3)
+WHOLE_PLANE = 0
 FLOPS = 3 * 2 * D * F * N
 
 
@@ -57,12 +57,6 @@ def tile_attend_gdepth_sil_pl_kernel(tc, xT, dyT, w1, w2, cf, gt, tx, c1, offs, 
         def entries(first, last):
             return offsets[:, first // BAND : last // BAND]
 
-        def in_pair_order(lane_ordered):
-            return lane_ordered.rearrange("p (u e m) -> p u m e", u=2, e=2)
-
-        def pair_places(pair_ordered):
-            return pair_ordered.rearrange("p (u m e) -> p u e m", u=2, e=2)
-
         def quantize(name, values, fmt, replaces=""):
             width = values.shape[1] // LANES
             codes = held(name + "_codes", [P, width], U32, replaces)
@@ -88,12 +82,11 @@ def tile_attend_gdepth_sil_pl_kernel(tc, xT, dyT, w1, w2, cf, gt, tx, c1, offs, 
         gt_pool = held("gt_pool", [P, T], F32)
         x_plane = [held(f"x_plane{t}", [P, T], F32) for t in range(LANES)]
         w1_raw = held("w1_raw", [P, LANES, F], F32)
-        w2_raw = [held(f"w2_raw{h}", [P, LANES, F // 2], F32) for h in range(2)]
+        w2_raw = held("w2_raw", [P, LANES, F], F32)
         dy_pool = [held(f"dy_pool{t}", [P, T], F32) for t in range(LANES)]
         out_plane = [held(f"out_plane{t}", [P, T], F32) for t in range(LANES)]
         x_rows = xT.rearrange("(p t) n -> p t n", t=LANES)
         dy_rows = dyT.rearrange("(p t) n -> p t n", t=LANES)
-        w2_rows = w2.rearrange("(p j) (h f) -> h p j f", j=LANES, h=2)
         scalar_lanes, vector_lanes = (2, 3), (0, 1)
 
         nc.sync.dma_start(offsets[:], offs)
@@ -101,14 +94,15 @@ def tile_attend_gdepth_sil_pl_kernel(tc, xT, dyT, w1, w2, cf, gt, tx, c1, offs, 
         nc.sync.dma_start(out=gt_pool[LAST:, :], in_=gt[LAST:, :])
         nc.scalar.dma_start(out=cf_col[:], in_=cf.rearrange("(m t) o -> m (t o)", t=LANES))
         nc.scalar.dma_start(out=c1_col[:], in_=c1.rearrange("(m t) o -> m (t o)", t=LANES))
-        for t in scalar_lanes + vector_lanes:
+        for t in (2, 0):
             nc.sync.dma_start(out=x_plane[t][:], in_=x_rows[:, t, :])
         nc.sync.dma_start(out=w1_raw[:], in_=w1.rearrange("(p j) f -> p j f", j=LANES))
-        nc.sync.dma_start(out=w2_raw[0][:], in_=w2_rows[0])
+        for t in (3, 1):
+            nc.sync.dma_start(out=x_plane[t][:], in_=x_rows[:, t, :])
         for t in range(LANES):
             nc.sync.dma_start(out=dy_pool[t][:], in_=dy_rows[:, t, :])
-        nc.sync.dma_start(out=w2_raw[1][:], in_=w2_rows[1])
-        for t in range(LANES):
+        nc.sync.dma_start(out=w2_raw[:], in_=w2.rearrange("(p j) f -> p j f", j=LANES))
+        for t in PLANE_ORDER:
             nc.sync.dma_start(out=out_plane[t][:], in_=dy_rows[:, t, :])
 
         ident = held("ident", [P, P], F32)
@@ -134,31 +128,8 @@ def tile_attend_gdepth_sil_pl_kernel(tc, xT, dyT, w1, w2, cf, gt, tx, c1, offs, 
         x_lanes = x_grouped[:].rearrange("p (i t) -> p i t", t=LANES)
         x_rounded = {t: held(f"x_rounded{t}", [P, T], BF16) for t in scalar_lanes}
         nc.scalar.activation(out=x_rounded[2][:], in_=x_plane[2][:], func=ACT.Copy)
-        nc.vector.tensor_copy(out=x_rounded[3][:], in_=x_plane[3][:])
-        for t in scalar_lanes:
-            nc.scalar.activation(out=x_lanes[:, :, t], in_=x_rounded[t][:].indirect(offsets[:]), func=ACT.Copy)
-        for t in vector_lanes:
-            nc.vector.tensor_copy(out=x_lanes[:, :, t], in_=x_plane[t][:].indirect(offsets[:]))
-        x_mx = quantize("x", x_grouped[:], E4M3)
-
-        c_col = held("c_col", [P, LANES], F32)
-        nc.gpsimd.tensor_tensor(out=c_col[:], in0=c1_col[:], in1=cf_col[:], op=ALU.mult)
-        c_row = bank("c_row")
-        for t in range(LANES):
-            repeated = c_col[:, t : t + 1].to_broadcast([P, P])
-            nc.tensor.transpose(pair_places(c_row[:])[:, t // 2, t % 2, :], repeated, ident[:])
-
-        w1_grouped = held("w1_grouped", [P, F * LANES], BF16)
-        w1_dst = w1_grouped[:].rearrange("p (t m j) -> p m j t", t=LANES, j=LANES)
-        w1_src = w1_raw[:].rearrange("p j (m t) -> p m j t", t=LANES)
-        nc.vector.tensor_copy(out=w1_dst[:, :W1_VECTOR], in_=w1_src[:, :W1_VECTOR])
-        nc.scalar.copy(out=w1_dst[:, W1_VECTOR:], in_=w1_src[:, W1_VECTOR:])
-        w1_mx = quantize("w1", w1_grouped[:], E4M3)
-
-        w2_grouped = held("w2_grouped", [P, F * LANES], BF16)
-        w2_dst = w2_grouped[:].rearrange("p (u m e j) -> p m j u e", u=2, e=2, j=LANES)
-        w2_src = [part[:].rearrange("p j (m u e) -> p m j u e", u=2, e=2) for part in w2_raw]
-        nc.scalar.copy(out=w2_dst[:, : P // 2], in_=w2_src[0])
+        nc.scalar.activation(out=x_lanes[:, :, 2], in_=x_rounded[2][:].indirect(offsets[:]), func=ACT.Copy)
+        nc.vector.tensor_copy(out=x_lanes[:, :, 0], in_=x_plane[0][:].indirect(offsets[:]))
 
         factors = held("factors", [P, 3, CHUNKS], F32, replaces="x_plane0")
         tx_neg, tx_half, gt_neg = (factors[:, k, :] for k in range(3))
@@ -167,73 +138,106 @@ def tile_attend_gdepth_sil_pl_kernel(tc, xT, dyT, w1, w2, cf, gt, tx, c1, offs, 
         nc.scalar.activation(out=tx_half[:], in_=tx_cols, func=ACT.Copy, scale=0.5)
         nc.scalar.activation(out=gt_neg[:], in_=gt_cols, func=ACT.Copy, scale=-1.0)
         nc.gpsimd.tensor_tensor(out=slot_factor[:], in0=gt_neg[:], in1=tx_half[:], op=ALU.mult)
+        c_col = held("c_col", [P, LANES], F32)
+        nc.gpsimd.tensor_tensor(out=c_col[:], in0=c1_col[:], in1=cf_col[:], op=ALU.mult)
+        c_row = bank("c_row", replaces="tx_turned")
+        for t in range(LANES):
+            repeated = c_col[:, t : t + 1].to_broadcast([P, P])
+            nc.tensor.transpose(c_row[:, block(2 * (t % 2) + t // 2)], repeated, ident[:])
 
-        w1t_grouped = held("w1t_grouped", [P, D * LANES], BF16)
+        w1_grouped = held("w1_grouped", [P, F * LANES], BF16)
+        nc.vector.tensor_copy(
+            out=w1_grouped[:].rearrange("p (t m j) -> p m j t", t=LANES, j=LANES),
+            in_=w1_raw[:].rearrange("p j (m t) -> p m j t", t=LANES),
+        )
+        nc.vector.tensor_copy(out=x_rounded[3][:], in_=x_plane[3][:])
+        w1_mx = quantize("w1", w1_grouped[:], E4M3)
+        nc.scalar.activation(out=x_lanes[:, :, 3], in_=x_rounded[3][:].indirect(offsets[:]), func=ACT.Copy)
+        nc.vector.tensor_copy(out=x_lanes[:, :, 1], in_=x_plane[1][:].indirect(offsets[:]))
+        x_mx = quantize("x", x_grouped[:], E4M3)
+
+        w1t_grouped = held("w1t_grouped", [P, D * LANES], BF16, replaces="x_plane3")
         w1t_pairs = w1t_grouped[:].rearrange("p (h b q t) -> p h q t b", h=2, b=2, t=LANES)
         w1_words = w1_grouped[:].bitcast(F32).rearrange("p (t m h) -> p h t m", t=LANES, h=2)
-
-        def turn_w1(h, replaces=""):
-            turned = bank(f"w1_turned{h}", replaces)
+        for h in range(2):
+            turned = bank(f"w1_turned{h}")
             for t in range(LANES):
                 nc.tensor.transpose(turned[:, block(t)], w1_words[:, h, t, :], ident[:])
             nc.scalar.copy(
                 out=w1t_pairs[:, h], in_=turned[:].bitcast(BF16).rearrange("p (t q b) -> p q t b", t=LANES, b=2)
             )
 
-        turn_w1(0)
+        a_banks = {}
+        for h in range(2):
+            for u in range(2):
+                a_banks[h, u] = bank(f"a{h}{u}")
+                for e in range(2):
+                    nc.tensor.matmul_mx(
+                        out=a_banks[h, u][:, half(e)],
+                        lhsT=w1_mx[0][:, block(2 * u + e)].bitcast(E4M3),
+                        lhsT_scale=w1_mx[1][:, block(2 * u + e)],
+                        rhs=x_mx[0][:, half(h)].bitcast(E4M3),
+                        rhs_scale=x_mx[1][:, half(h)],
+                        start=True,
+                        stop=True,
+                    )
 
-        a_scaled = held("a_scaled", [P, LANES, N], F32)
-        for t in range(LANES):
-            a_bank = bank(f"a{t}", replaces="tx_turned" if t == LANES - 1 else "")
-            product(a_bank, w1_mx, E4M3, block(t), x_mx, E4M3)
-            nc.scalar.activation(out=a_scaled[:, t, :], in_=a_bank[:], func=ACT.Copy, scale=cf_col[:, t : t + 1])
-
-        silu_neg = [held(f"silu_neg{c}", [P, F], F32) for c in range(CHUNKS)]
-        tanh_half = [held(f"tanh_half{c}", [P, F], F32) for c in range(CHUNKS)]
-        a_turned = {}
-
-        def turn_a(c, replaces=""):
-            a_turned[c] = bank(f"a_turned{c}", replaces)
+        def scale_lanes(name, banks, func, column, bias):
+            scaled = held(name, [P, LANES, HALF], F32)
             for t in range(LANES):
-                nc.tensor.transpose(a_turned[c][:, block(t)], a_scaled[:, t, block(c)], ident[:])
+                extra = {"bias": column[:, t : t + 1]} if bias else {}
+                nc.scalar.activation(
+                    out=scaled[:, t, :], in_=banks[t // 2][:, half(t % 2)], func=func, scale=column[:, t : t + 1], **extra
+                )
+            return scaled
 
-        def paired_activation(out, c, func, scale):
+        def turn_to_slots(name, lanes, e, replaces):
+            turned = bank(name, replaces)
+            for t in range(LANES):
+                nc.tensor.transpose(turned[:, block(2 * (t % 2) + t // 2)], lanes[:, t, block(e)], ident[:])
+            return turned
+
+        def read_in_pairs(turned):
+            return turned[:].rearrange("p (b n) -> p n b", b=2)
+
+        def as_pairs(pair_ordered):
+            return pair_ordered[:].rearrange("p (n b) -> p n b", b=2)
+
+        silu_neg, tanh_half, a_turned = {}, {}, {}
+
+        def turn_a(h, replaced):
+            a_scaled = scale_lanes(f"a_scaled{h}", (a_banks[h, 0], a_banks[h, 1]), ACT.Copy, cf_col, False)
+            for e in range(2):
+                a_turned[2 * h + e] = turn_to_slots(f"a_turned{2 * h + e}", a_scaled, e, replaced[e])
+
+        def activate(kept, name, c, func, scale, paired=True):
+            kept[c] = held(f"{name}{c}", [P, F], F32)
             nc.scalar.activation(
-                out=out[c][:].rearrange("p (u m e) -> p u m e", u=2, e=2),
-                in_=in_pair_order(a_turned[c][:]),
+                out=as_pairs(kept[c]) if paired else kept[c][:],
+                in_=read_in_pairs(a_turned[c]) if paired else a_turned[c][:],
                 func=func,
                 scale=scale[:, c : c + 1],
             )
 
-        turn_w1(1, replaces="a0")
-        turn_a(0, replaces="gt_turned")
-        paired_activation(silu_neg, 0, ACT.Silu, tx_neg)
-        turn_a(2, replaces="w1_turned0")
-        turn_a(3, replaces="a3")
-        turn_a(1)
+        turn_a(0, ("gt_turned", "w1_turned0"))
+        turn_a(1, ("w1_turned1", "a00"))
+        activate(silu_neg, "silu_neg", 0, ACT.Silu, tx_neg)
+        activate(tanh_half, "tanh_half", 0, ACT.Tanh, tx_half)
         for c in (2, 3):
-            nc.scalar.activation(out=tanh_half[c][:], in_=a_turned[c][:], func=ACT.Tanh, scale=tx_half[:, c : c + 1])
-        paired_activation(tanh_half, 0, ACT.Tanh, tx_half)
-        paired_activation(silu_neg, 1, ACT.Silu, tx_neg)
-        paired_activation(tanh_half, 1, ACT.Tanh, tx_half)
+            activate(tanh_half, "tanh_half", c, ACT.Tanh, tx_half, paired=False)
+        activate(silu_neg, "silu_neg", 1, ACT.Silu, tx_neg)
+        activate(tanh_half, "tanh_half", 1, ACT.Tanh, tx_half)
 
-        lifted = held("lifted", [P, LANES, HALF], F32)
-        for u, replaces in enumerate(("w1_turned1", "a_turned0")):
-            tanh_turned = bank(f"tanh_turned{u}", replaces)
-            for e in range(2):
-                for c in (2, 3):
-                    nc.tensor.transpose(tanh_turned[:, block(2 * e + c - 2)], tanh_half[c][:, block(2 * u + e)], ident[:])
-            for e in range(2):
-                t = 2 * u + e
-                nc.scalar.activation(
-                    out=lifted[:, t, :],
-                    in_=tanh_turned[:, half(e)],
-                    func=ACT.Identity,
-                    scale=c_col[:, t : t + 1],
-                    bias=c_col[:, t : t + 1],
-                )
+        tanh_turned = []
+        for u, replaces in enumerate(("a01", "a10")):
+            tanh_turned.append(bank(f"tanh_turned{u}", replaces))
+            for b in range(2):
+                for e in range(2):
+                    nc.tensor.transpose(
+                        tanh_turned[u][:, block(2 * b + e)], tanh_half[2 + e][:, block(2 * b + u)], ident[:]
+                    )
 
-        dy_got = held("dy_got", [P, LANES, N], F32, replaces="w1_raw")
+        dy_got = held("dy_got", [P, LANES, N], F32)
         for t in range(LANES - 1):
             nc.vector.tensor_copy(out=dy_got[:, t, :], in_=dy_pool[t][:].indirect(offsets[:]))
         for h in range(2):
@@ -256,39 +260,42 @@ def tile_attend_gdepth_sil_pl_kernel(tc, xT, dyT, w1, w2, cf, gt, tx, c1, offs, 
                 product(dh_banks[-1], dy_mx, E5M2, block(e), w2_mx, E4M3)
 
         dy_rounded = round_dy(0, nc.vector.tensor_copy)
-        nc.vector.tensor_copy(out=w2_dst[:, P // 2 :], in_=w2_src[1])
-        dy0_mx = quantize("dy0", dy_rounded[:], E5M2, replaces="w2_raw1")
+        w2_grouped = held("w2_grouped", [P, F * LANES], BF16)
+        nc.vector.tensor_copy(
+            out=w2_grouped[:].rearrange("p (u m e j) -> p m j u e", u=2, e=2, j=LANES),
+            in_=w2_raw[:].rearrange("p j (m u e) -> p m j u e", u=2, e=2),
+        )
+        dy0_mx = quantize("dy0", dy_rounded[:], E5M2, replaces="w2_raw")
         w2_mx = quantize("w2", w2_grouped[:], E4M3)
-        make_dh(dy0_mx, ("a1", "a2"))
+        make_dh(dy0_mx, ("a11", "a_turned0"))
+        lifted = scale_lanes("lifted", tanh_turned, ACT.Identity, c_col, True)
+        lifted_back = {
+            2 + e: turn_to_slots(f"lifted_back{2 + e}", lifted, e, replaces)
+            for e, replaces in enumerate(("a_turned1", "tanh_turned0"))
+        }
 
-        slope = [held(f"slope{c}", [P, F], F32) for c in range(CHUNKS)]
+
+        slope = {}
         da_mx = (held("da_codes", [P, N], U32), held("da_scales", [P, N], U8))
         nc.gpsimd.memset(da_mx[0][:, half(1)].bitcast(I32), 0)
         nc.gpsimd.memset(da_mx[1][:, half(1)].bitcast(I32), 0)
         da_grouped = held("da_grouped", [P, N * LANES], BF16)
         da_words = da_grouped[:].bitcast(F32).rearrange("p (c i u) -> p c i u", c=CHUNKS, u=2)
 
-        def plain_slope(c):
-            part = held(f"part{c}", [P, F], F32)
+        def times_bank(name, c, factor):
+            result = held(name, [P, F], F32)
             nc.vector.scalar_tensor_tensor(
-                out=part[:], in0=silu_neg[c][:], scalar=-1.0, in1=c_row[:], op0=ALU.add, op1=ALU.mult
+                out=as_pairs(result),
+                in0=as_pairs(silu_neg[c]),
+                scalar=-1.0,
+                in1=read_in_pairs(factor),
+                op0=ALU.add,
+                op1=ALU.mult,
             )
-            nc.vector.scalar_tensor_tensor(
-                out=slope[c][:], in0=tanh_half[c][:], scalar=1.0, in1=part[:], op0=ALU.add, op1=ALU.mult
-            )
-
-        def lifted_slope(c, replaces):
-            lifted_back = bank(f"lifted_back{c}", replaces)
-            for t in range(LANES):
-                nc.tensor.transpose(
-                    pair_places(lifted_back[:])[:, t // 2, t % 2, :], lifted[:, t, block(c - 2)], ident[:]
-                )
-            nc.vector.scalar_tensor_tensor(
-                out=slope[c][:], in0=silu_neg[c][:], scalar=-1.0, in1=lifted_back[:], op0=ALU.add, op1=ALU.mult
-            )
+            return result
 
         def make_da(c, turned):
-            da = held(f"da{c}", [P, F], BF16, replaces=f"da{c - 2}")
+            da = held(f"da{c}", [P, F], BF16)
             nc.vector.scalar_tensor_tensor(
                 out=da[:],
                 in0=dh_banks[c][:],
@@ -317,29 +324,6 @@ def tile_attend_gdepth_sil_pl_kernel(tc, xT, dyT, w1, w2, cf, gt, tx, c1, offs, 
             product(dx_bank, w1t_mx, E4M3, block(j), da_mx, E5M2)
             return dx_bank
 
-        plain_slope(0)
-        plain_slope(1)
-        for c, replaces in enumerate(("a_turned1", "dh1")):
-            da_turned = bank(f"da_turned{c}", replaces)
-            make_da(c, da_turned[:, half(0)])
-            fetch_da(c, 1, da_turned[:, half(0)])
-        w1t_mx = quantize("w1t", w1t_grouped[:], E4M3, replaces="slope1")
-        dy_rounded = round_dy(1, nc.scalar.copy, replaces="w2_grouped")
-        make_dh(quantize("dy1", dy_rounded[:], E5M2), ("c_row", "dh0"))
-        paired_activation(silu_neg, 2, ACT.Silu, tx_neg)
-        quantize_da(0)
-        early_banks = [make_dx("dx_early0", PLANE_ORDER[0], replaces="da_turned0")]
-
-        paired_activation(silu_neg, 3, ACT.Silu, tx_neg)
-        lifted_slope(2, replaces="tanh_turned0")
-        lifted_slope(3, replaces="tanh_turned1")
-        da_turned = bank("da_turned23", replaces="da_turned1")
-        make_da(2, da_turned[:, half(0)])
-        make_da(3, da_turned[:, half(1)])
-        fetch_da(2, 2, da_turned[:])
-        early_banks.append(make_dx("dx_early1", PLANE_ORDER[1], replaces="dh3"))
-        quantize_da(1)
-
         def fetch_dx(name, dx_bank, first, last, replaces=""):
             dx = held(name, [P, last - first], F32, replaces)
             nc.scalar.copy(out=dx[:], in_=dx_bank[:, first:last])
@@ -350,11 +334,42 @@ def tile_attend_gdepth_sil_pl_kernel(tc, xT, dyT, w1, w2, cf, gt, tx, c1, offs, 
                 out=out_plane[t][:].indirect(entries(first, last)), in0=dx[:], in1=dy_got[:, t, first:last], op=ALU.add
             )
 
-        for k, replaces in enumerate(("silu_neg3", "")):
-            scatter(PLANE_ORDER[k], 0, HALF, fetch_dx(f"dx_first{k}", early_banks[k], 0, HALF, replaces))
+        part = [times_bank(f"part{c}", c, c_row) for c in range(2)]
+        for c in range(2):
+            slope[c] = held(f"slope{c}", [P, F], F32)
+            nc.vector.scalar_tensor_tensor(
+                out=slope[c][:], in0=tanh_half[c][:], scalar=1.0, in1=part[c][:], op0=ALU.add, op1=ALU.mult
+            )
+        dy_rounded = round_dy(1, nc.scalar.copy, replaces="c_col")
+        for c, replaces in enumerate(("tanh_turned1", "c_row")):
+            da_turned = bank(f"da_turned{c}", replaces)
+            make_da(c, da_turned[:, half(0)])
+            fetch_da(c, 1, da_turned[:, half(0)])
+        activate(silu_neg, "silu_neg", 2, ACT.Silu, tx_neg)
+        activate(silu_neg, "silu_neg", 3, ACT.Silu, tx_neg)
+        make_dh(quantize("dy1", dy_rounded[:], E5M2, replaces="slope0"), ("dh0", "dh1"))
+        w1t_mx = quantize("w1t", w1t_grouped[:], E4M3, replaces="slope1")
+        quantize_da(0)
+        early = [t for t in PLANE_ORDER if t != WHOLE_PLANE]
+        early_banks = [make_dx("dx_early0", early[0], "da_turned0")]
+        for c in (2, 3):
+            slope[c] = times_bank(f"slope{c}", c, lifted_back[c])
+        da_turned = bank("da_turned23", replaces="da_turned1")
+        make_da(2, da_turned[:, half(0)])
+        make_da(3, da_turned[:, half(1)])
+        early_banks.append(make_dx("dx_early1", early[1], "a_turned2"))
+        early_banks.append(make_dx("dx_early2", early[2], "a_turned3"))
+        dx_early = [fetch_dx("dx_first0", early_banks[0], 0, HALF, replaces="silu_neg3")]
+        fetch_da(2, 2, da_turned[:])
+        dx_early.append(fetch_dx("dx_first1", early_banks[1], 0, HALF, replaces="slope3"))
+        scatter(early[0], 0, HALF, dx_early[0])
+        quantize_da(1)
+        scatter(early[1], 0, HALF, dx_early[1])
+        dx_early.append(fetch_dx("dx_first2", early_banks[2], 0, HALF, replaces="da3"))
+        scatter(early[2], 0, HALF, dx_early[2])
 
-        done = {t: HALF if t in PLANE_ORDER[:2] else 0 for t in PLANE_ORDER}
-        freed = ("a_turned2", "a_turned3", "lifted_back2", "lifted_back3")
+        done = {t: HALF if t in early else 0 for t in PLANE_ORDER}
+        freed = ("lifted_back2", "lifted_back3", "dh2", "dh3")
         dx_banks = {t: make_dx(f"dx{t}", t, replaces) for t, replaces in zip(PLANE_ORDER, freed)}
         first_plane, last_plane = PLANE_ORDER[0], PLANE_ORDER[-1]
         dx_rest = {t: fetch_dx(f"dx_rest{t}", dx_banks[t], done[t], N) for t in PLANE_ORDER[:-1]}
@@ -368,7 +383,7 @@ def tile_attend_gdepth_sil_pl_kernel(tc, xT, dyT, w1, w2, cf, gt, tx, c1, offs, 
             if t != last_plane:
                 nc.scalar.copy(out=out_lane[t], in_=out_plane[t][:])
             if t == first_plane:
-                dx_rest[last_plane] = fetch_dx("dx_last", dx_banks[last_plane], 0, N, replaces=f"dx_rest{t}")
+                dx_rest[last_plane] = fetch_dx("dx_last", dx_banks[last_plane], done[last_plane], N, replaces=f"dx_rest{t}")
         nc.scalar.copy(out=out_lane[last_plane][:, LAST_VECTOR:], in_=out_plane[last_plane][:, LAST_VECTOR:])
         for cols in (slice(0, T // 2), slice(T // 2, LAST_VECTOR)):
             nc.vector.tensor_copy(out=out_lane[last_plane][:, cols], in_=out_plane[last_plane][:, cols])

@@ -29,7 +29,6 @@ LAST = P - 1
 LAST_VECTOR = 640
 WEAVE_VECTOR = 576
 PLANE_ORDER = (2, 0, 1, 3)
-WHOLE_PLANE = 0
 FLOPS = 3 * 2 * D * F * N
 
 
@@ -56,6 +55,9 @@ def tile_attend_gdepth_sil_pl_kernel(tc, xT, dyT, w1, w2, cf, gt, tx, c1, offs, 
 
         def entries(first, last):
             return offsets[:, first // BAND : last // BAND]
+
+        def lane_places(pair_ordered, t):
+            return pair_ordered[:].rearrange("p (u m e) -> p u e m", u=2, e=2)[:, t // 2, t % 2, :]
 
         def quantize(name, values, fmt, replaces=""):
             width = values.shape[1] // LANES
@@ -143,7 +145,7 @@ def tile_attend_gdepth_sil_pl_kernel(tc, xT, dyT, w1, w2, cf, gt, tx, c1, offs, 
         c_row = bank("c_row", replaces="tx_turned")
         for t in range(LANES):
             repeated = c_col[:, t : t + 1].to_broadcast([P, P])
-            nc.tensor.transpose(c_row[:, block(2 * (t % 2) + t // 2)], repeated, ident[:])
+            nc.tensor.transpose(lane_places(c_row, t), repeated, ident[:])
 
         w1_grouped = held("w1_grouped", [P, F * LANES], BF16)
         nc.vector.tensor_copy(
@@ -270,9 +272,11 @@ def tile_attend_gdepth_sil_pl_kernel(tc, xT, dyT, w1, w2, cf, gt, tx, c1, offs, 
         make_dh(dy0_mx, ("a11", "a_turned0"))
         lifted = scale_lanes("lifted", tanh_turned, ACT.Identity, c_col, True)
         lifted_back = {
-            2 + e: turn_to_slots(f"lifted_back{2 + e}", lifted, e, replaces)
-            for e, replaces in enumerate(("a_turned1", "tanh_turned0"))
+            2 + e: bank(f"lifted_back{2 + e}", replaces) for e, replaces in enumerate(("a_turned1", "tanh_turned0"))
         }
+        for e in range(2):
+            for t in range(LANES):
+                nc.tensor.transpose(lane_places(lifted_back[2 + e], t), lifted[:, t, block(e)], ident[:])
 
 
         slope = {}
@@ -285,10 +289,10 @@ def tile_attend_gdepth_sil_pl_kernel(tc, xT, dyT, w1, w2, cf, gt, tx, c1, offs, 
         def times_bank(name, c, factor):
             result = held(name, [P, F], F32)
             nc.vector.scalar_tensor_tensor(
-                out=as_pairs(result),
-                in0=as_pairs(silu_neg[c]),
+                out=result[:],
+                in0=silu_neg[c][:],
                 scalar=-1.0,
-                in1=read_in_pairs(factor),
+                in1=factor[:],
                 op0=ALU.add,
                 op1=ALU.mult,
             )
@@ -350,7 +354,7 @@ def tile_attend_gdepth_sil_pl_kernel(tc, xT, dyT, w1, w2, cf, gt, tx, c1, offs, 
         make_dh(quantize("dy1", dy_rounded[:], E5M2, replaces="slope0"), ("dh0", "dh1"))
         w1t_mx = quantize("w1t", w1t_grouped[:], E4M3, replaces="slope1")
         quantize_da(0)
-        early = [t for t in PLANE_ORDER if t != WHOLE_PLANE]
+        early = (PLANE_ORDER[0], PLANE_ORDER[2])
         early_banks = [make_dx("dx_early0", early[0], "da_turned0")]
         for c in (2, 3):
             slope[c] = times_bank(f"slope{c}", c, lifted_back[c])
@@ -358,21 +362,24 @@ def tile_attend_gdepth_sil_pl_kernel(tc, xT, dyT, w1, w2, cf, gt, tx, c1, offs, 
         make_da(2, da_turned[:, half(0)])
         make_da(3, da_turned[:, half(1)])
         early_banks.append(make_dx("dx_early1", early[1], "a_turned2"))
-        early_banks.append(make_dx("dx_early2", early[2], "a_turned3"))
         dx_early = [fetch_dx("dx_first0", early_banks[0], 0, HALF, replaces="silu_neg3")]
         fetch_da(2, 2, da_turned[:])
-        dx_early.append(fetch_dx("dx_first1", early_banks[1], 0, HALF, replaces="slope3"))
+        dx_early.append(fetch_dx("dx_first1", early_banks[1], 0, HALF, replaces="da3"))
         scatter(early[0], 0, HALF, dx_early[0])
         quantize_da(1)
         scatter(early[1], 0, HALF, dx_early[1])
-        dx_early.append(fetch_dx("dx_first2", early_banks[2], 0, HALF, replaces="da3"))
-        scatter(early[2], 0, HALF, dx_early[2])
 
-        done = {t: HALF if t in early else 0 for t in PLANE_ORDER}
+        done = {t: 0 if t == PLANE_ORDER[-1] else HALF for t in PLANE_ORDER}
         freed = ("lifted_back2", "lifted_back3", "dh2", "dh3")
-        dx_banks = {t: make_dx(f"dx{t}", t, replaces) for t, replaces in zip(PLANE_ORDER, freed)}
+        split_plane = PLANE_ORDER[1]
+        pass_order = (split_plane, *early, PLANE_ORDER[-1])
+        dx_banks = {t: make_dx(f"dx{t}", t, replaces) for t, replaces in zip(pass_order, freed)}
         first_plane, last_plane = PLANE_ORDER[0], PLANE_ORDER[-1]
-        dx_rest = {t: fetch_dx(f"dx_rest{t}", dx_banks[t], done[t], N) for t in PLANE_ORDER[:-1]}
+        scatter(split_plane, 0, HALF, fetch_dx("dx_first2", dx_banks[split_plane], 0, HALF))
+        dx_rest = {
+            t: fetch_dx(f"dx_rest{t}", dx_banks[t], done[t], N, "dx_first2" if t == split_plane else "")
+            for t in PLANE_ORDER[:-1]
+        }
 
         out_pairs = held("out_pairs", [P, 2, 2 * T], BF16, replaces="dy_pool0")
         out_lane = [out_pairs[:, t // 2, :].rearrange("p (n e) -> p n e", e=2)[:, :, t % 2] for t in range(LANES)]

@@ -26,6 +26,7 @@ BAND = 16
 QUAD = 32
 RUN = 4
 LAST = P - 1
+W2_VECTOR = 128
 LAST_VECTOR = 640
 WEAVE_VECTOR = 576
 PLANE_ORDER = (2, 0, 1, 3)
@@ -56,9 +57,6 @@ def tile_attend_gdepth_sil_pl_kernel(tc, xT, dyT, w1, w2, cf, gt, tx, c1, offs, 
         def entries(first, last):
             return offsets[:, first // BAND : last // BAND]
 
-        def lane_places(pair_ordered, t):
-            return pair_ordered[:].rearrange("p (u m e) -> p u e m", u=2, e=2)[:, t // 2, t % 2, :]
-
         def quantize(name, values, fmt, replaces=""):
             width = values.shape[1] // LANES
             codes = held(name + "_codes", [P, width], U32, replaces)
@@ -78,8 +76,7 @@ def tile_attend_gdepth_sil_pl_kernel(tc, xT, dyT, w1, w2, cf, gt, tx, c1, offs, 
             )
 
         offsets = keep.tile([P, N // BAND], U16, name="offsets")
-        cf_col = held("cf_col", [P, LANES], F32)
-        c1_col = held("c1_col", [P, LANES], F32)
+        unit_rows = held("unit_rows", [P, 2, F // 2], F32)
         tx_pool = held("tx_pool", [P, T], F32)
         gt_pool = held("gt_pool", [P, T], F32)
         x_plane = [held(f"x_plane{t}", [P, T], F32) for t in range(LANES)]
@@ -94,8 +91,8 @@ def tile_attend_gdepth_sil_pl_kernel(tc, xT, dyT, w1, w2, cf, gt, tx, c1, offs, 
         nc.sync.dma_start(offsets[:], offs)
         nc.sync.dma_start(out=tx_pool[LAST:, :], in_=tx[LAST:, :])
         nc.sync.dma_start(out=gt_pool[LAST:, :], in_=gt[LAST:, :])
-        nc.scalar.dma_start(out=cf_col[:], in_=cf.rearrange("(m t) o -> m (t o)", t=LANES))
-        nc.scalar.dma_start(out=c1_col[:], in_=c1.rearrange("(m t) o -> m (t o)", t=LANES))
+        for k, vector in enumerate((cf, c1)):
+            nc.scalar.dma_start(out=unit_rows[P - 2 :, k, :], in_=vector.rearrange("(g n) o -> g (n o)", g=2))
         for t in (2, 0):
             nc.sync.dma_start(out=x_plane[t][:], in_=x_rows[:, t, :])
         nc.sync.dma_start(out=w1_raw[:], in_=w1.rearrange("(p j) f -> p j f", j=LANES))
@@ -108,12 +105,19 @@ def tile_attend_gdepth_sil_pl_kernel(tc, xT, dyT, w1, w2, cf, gt, tx, c1, offs, 
             nc.sync.dma_start(out=out_plane[t][:], in_=dy_rows[:, t, :])
 
         ident = held("ident", [P, P], F32)
+        nc.gpsimd.memset(unit_rows[: P - 2], 0.0)
         make_identity(nc, ident[:])
         for pool_tile in (tx_pool, gt_pool):
             nc.vector.memset(pool_tile[:LAST, :], 0.0)
 
         warm = held("warm", [P, 1], F32)
         nc.scalar.activation(out=warm[:QUAD, :], in_=tx_pool[:QUAD, 0:1], func=ACT.Silu)
+
+        unit_sorted = held("unit_sorted", [P, 2, F // 2], F32)
+        nc.scalar.copy(
+            out=unit_sorted[:].rearrange("p v (u m e) -> p v u m e", u=2, e=2),
+            in_=unit_rows[:].rearrange("p v (m u e) -> p v u m e", u=2, e=2),
+        )
 
         def slot_columns(name, pool_tile):
             got = held(name + "_got", [P, N], F32)
@@ -133,111 +137,130 @@ def tile_attend_gdepth_sil_pl_kernel(tc, xT, dyT, w1, w2, cf, gt, tx, c1, offs, 
         nc.scalar.activation(out=x_lanes[:, :, 2], in_=x_rounded[2][:].indirect(offsets[:]), func=ACT.Copy)
         nc.vector.tensor_copy(out=x_lanes[:, :, 0], in_=x_plane[0][:].indirect(offsets[:]))
 
-        factors = held("factors", [P, 3, CHUNKS], F32, replaces="x_plane0")
-        tx_neg, tx_half, gt_neg = (factors[:, k, :] for k in range(3))
+        factors = held("factors", [P, 3, CHUNKS], F32, replaces="x_rounded2")
+        tx_neg, tx_half, tx_neg_half = (factors[:, k, :] for k in range(3))
         slot_factor = held("slot_factor", [P, CHUNKS], F32)
         nc.scalar.activation(out=tx_neg[:], in_=tx_cols, func=ACT.Copy, scale=-1.0)
         nc.scalar.activation(out=tx_half[:], in_=tx_cols, func=ACT.Copy, scale=0.5)
-        nc.scalar.activation(out=gt_neg[:], in_=gt_cols, func=ACT.Copy, scale=-1.0)
-        nc.gpsimd.tensor_tensor(out=slot_factor[:], in0=gt_neg[:], in1=tx_half[:], op=ALU.mult)
-        c_col = held("c_col", [P, LANES], F32)
-        nc.gpsimd.tensor_tensor(out=c_col[:], in0=c1_col[:], in1=cf_col[:], op=ALU.mult)
-        c_row = bank("c_row", replaces="tx_turned")
-        for t in range(LANES):
-            repeated = c_col[:, t : t + 1].to_broadcast([P, P])
-            nc.tensor.transpose(lane_places(c_row, t), repeated, ident[:])
+        nc.scalar.activation(out=tx_neg_half[:], in_=tx_cols, func=ACT.Copy, scale=-0.5)
+        for c in range(CHUNKS):
+            nc.scalar.activation(
+                out=slot_factor[:, c : c + 1], in_=gt_cols[:, c : c + 1], func=ACT.Copy, scale=tx_neg_half[:, c : c + 1]
+            )
 
-        w1_grouped = held("w1_grouped", [P, F * LANES], BF16)
-        nc.vector.tensor_copy(
-            out=w1_grouped[:].rearrange("p (t m j) -> p m j t", t=LANES, j=LANES),
-            in_=w1_raw[:].rearrange("p j (m t) -> p m j t", t=LANES),
+        unit_turned = bank("unit_turned")
+        for v in range(2):
+            for u in range(2):
+                nc.tensor.transpose(unit_turned[:, block(2 * v + u)], unit_sorted[:, v, block(u)], ident[:])
+        unit_cols = held("unit_cols", [P, 2 * LANES], F32)
+        nc.scalar.copy(
+            out=unit_cols[:].rearrange("p (b g) -> p b g", g=2),
+            in_=unit_turned[:].rearrange("p (b r) -> p b r", r=P)[:, :, P - 2 :],
         )
+        cf_col = unit_cols[:, :LANES]
+        c_col = held("c_col", [P, LANES], F32)
+        for k in range(LANES):
+            nc.scalar.activation(
+                out=c_col[:, k : k + 1], in_=unit_cols[:, LANES + k : LANES + k + 1], func=ACT.Copy, scale=cf_col[:, k : k + 1]
+            )
+
+        def round_weights(name, raw, share):
+            grouped = held(name, [P, F * LANES], BF16)
+            dst = grouped[:].rearrange("p (u m e j) -> p m j u e", u=2, e=2, j=LANES)
+            src = raw[:].rearrange("p j (m u e) -> p m j u e", u=2, e=2)
+            nc.vector.tensor_copy(out=dst[:, :share], in_=src[:, :share])
+            if share < P:
+                nc.scalar.copy(out=dst[:, share:], in_=src[:, share:])
+            return grouped
+
+        w1_grouped = round_weights("w1_grouped", w1_raw, P)
         nc.vector.tensor_copy(out=x_rounded[3][:], in_=x_plane[3][:])
         w1_mx = quantize("w1", w1_grouped[:], E4M3)
         nc.scalar.activation(out=x_lanes[:, :, 3], in_=x_rounded[3][:].indirect(offsets[:]), func=ACT.Copy)
-        nc.vector.tensor_copy(out=x_lanes[:, :, 1], in_=x_plane[1][:].indirect(offsets[:]))
-        x_mx = quantize("x", x_grouped[:], E4M3)
+        for h in range(2):
+            window = x_plane[1][:].indirect(entries(h * HALF, (h + 1) * HALF))
+            nc.vector.tensor_copy(out=x_lanes[:, half(h), 1], in_=window)
+        x_mx = [quantize(f"x{h}", x_grouped[:, h * HALF * LANES : (h + 1) * HALF * LANES], E4M3) for h in range(2)]
 
         w1t_grouped = held("w1t_grouped", [P, D * LANES], BF16, replaces="x_plane3")
-        w1t_pairs = w1t_grouped[:].rearrange("p (h b q t) -> p h q t b", h=2, b=2, t=LANES)
-        w1_words = w1_grouped[:].bitcast(F32).rearrange("p (t m h) -> p h t m", t=LANES, h=2)
+        w1t_pairs = w1t_grouped[:].rearrange("p (h b c i t) -> p h c t i b", h=2, b=2, i=2, t=LANES)
+        w1_words = w1_grouped[:].bitcast(F32).rearrange("p (u m e h) -> p h u e m", u=2, e=2, h=2)
         for h in range(2):
-            turned = bank(f"w1_turned{h}")
+            turned = bank(f"w1_turned{h}", replaces="unit_turned" if h else "")
             for t in range(LANES):
-                nc.tensor.transpose(turned[:, block(t)], w1_words[:, h, t, :], ident[:])
+                nc.tensor.transpose(turned[:, block(t)], w1_words[:, h, t // 2, t % 2, :], ident[:])
             nc.scalar.copy(
-                out=w1t_pairs[:, h], in_=turned[:].bitcast(BF16).rearrange("p (t q b) -> p q t b", t=LANES, b=2)
+                out=w1t_pairs[:, h], in_=turned[:].bitcast(BF16).rearrange("p (t c i b) -> p c t i b", t=LANES, i=2, b=2)
             )
 
-        a_banks = {}
-        for h in range(2):
-            for u in range(2):
-                a_banks[h, u] = bank(f"a{h}{u}")
-                for e in range(2):
-                    nc.tensor.matmul_mx(
-                        out=a_banks[h, u][:, half(e)],
-                        lhsT=w1_mx[0][:, block(2 * u + e)].bitcast(E4M3),
-                        lhsT_scale=w1_mx[1][:, block(2 * u + e)],
-                        rhs=x_mx[0][:, half(h)].bitcast(E4M3),
-                        rhs_scale=x_mx[1][:, half(h)],
-                        start=True,
-                        stop=True,
-                    )
+        c_row = bank("c_row", replaces="tx_turned")
+        for k in range(LANES):
+            nc.tensor.transpose(c_row[:, block(k)], c_col[:, k : k + 1].to_broadcast([P, P]), ident[:])
 
-        def scale_lanes(name, banks, func, column, bias):
-            scaled = held(name, [P, LANES, HALF], F32)
-            for t in range(LANES):
-                extra = {"bias": column[:, t : t + 1]} if bias else {}
-                nc.scalar.activation(
-                    out=scaled[:, t, :], in_=banks[t // 2][:, half(t % 2)], func=func, scale=column[:, t : t + 1], **extra
-                )
+        def scale_blocks(name, blocks, func, column, bias):
+            scaled = held(name, [P, LANES, blocks[0].shape[1]], F32)
+            for k in range(LANES):
+                extra = {"bias": column[:, k : k + 1]} if bias else {}
+                nc.scalar.activation(out=scaled[:, k, :], in_=blocks[k], func=func, scale=column[:, k : k + 1], **extra)
             return scaled
 
-        def turn_to_slots(name, lanes, e, replaces):
+        def halves_of(banks):
+            return [banks[k // 2][:, half(k % 2)] for k in range(LANES)]
+
+        def turn_to_slots(name, scaled, e, replaces):
             turned = bank(name, replaces)
-            for t in range(LANES):
-                nc.tensor.transpose(turned[:, block(2 * (t % 2) + t // 2)], lanes[:, t, block(e)], ident[:])
+            for k in range(LANES):
+                nc.tensor.transpose(turned[:, block(k)], scaled[:, k, block(e)], ident[:])
             return turned
-
-        def read_in_pairs(turned):
-            return turned[:].rearrange("p (b n) -> p n b", b=2)
-
-        def as_pairs(pair_ordered):
-            return pair_ordered[:].rearrange("p (n b) -> p n b", b=2)
 
         silu_neg, tanh_half, a_turned = {}, {}, {}
 
-        def turn_a(h, replaced):
-            a_scaled = scale_lanes(f"a_scaled{h}", (a_banks[h, 0], a_banks[h, 1]), ACT.Copy, cf_col, False)
-            for e in range(2):
-                a_turned[2 * h + e] = turn_to_slots(f"a_turned{2 * h + e}", a_scaled, e, replaced[e])
+        def first_product(h, chunks, replaced):
+            banks = [bank(f"a{h}{u}") for u in range(2)]
+            for k, out in enumerate(halves_of(banks)):
+                nc.tensor.matmul_mx(
+                    out=out,
+                    lhsT=w1_mx[0][:, block(k)].bitcast(E4M3),
+                    lhsT_scale=w1_mx[1][:, block(k)],
+                    rhs=x_mx[h][0][:].bitcast(E4M3),
+                    rhs_scale=x_mx[h][1][:],
+                    start=True,
+                    stop=True,
+                )
+            a_scaled = scale_blocks(f"a_scaled{h}", halves_of(banks), ACT.Copy, cf_col, False)
+            for c, replaces in zip(chunks, replaced):
+                a_turned[c] = turn_to_slots(f"a_turned{c}", a_scaled, c % 2, replaces)
 
-        def activate(kept, name, c, func, scale, paired=True):
+        def activate(kept, name, c, func, scale):
             kept[c] = held(f"{name}{c}", [P, F], F32)
-            nc.scalar.activation(
-                out=as_pairs(kept[c]) if paired else kept[c][:],
-                in_=read_in_pairs(a_turned[c]) if paired else a_turned[c][:],
-                func=func,
-                scale=scale[:, c : c + 1],
-            )
+            nc.scalar.activation(out=kept[c][:], in_=a_turned[c][:], func=func, scale=scale[:, c : c + 1])
 
-        turn_a(0, ("gt_turned", "w1_turned0"))
-        turn_a(1, ("w1_turned1", "a00"))
+        def turn_tanh(chunks, replaced):
+            banks = [bank(f"tanh_turned{c}", replaces) for c, replaces in zip(chunks, replaced)]
+            width = len(chunks) * P
+            blocks = [banks[k * width // 512][:, k * width % 512 :][:, :width] for k in range(LANES)]
+            for k in range(LANES):
+                for e, c in enumerate(chunks):
+                    nc.tensor.transpose(blocks[k][:, block(e)], tanh_half[c][:, block(k)], ident[:])
+            return blocks
+
+        lifted_back = {}
+
+        def lift(chunks, blocks, replaced):
+            lifted = scale_blocks(f"lifted{chunks[0]}", blocks, ACT.Identity, c_col, True)
+            for e, c in enumerate(chunks):
+                lifted_back[c] = turn_to_slots(f"lifted_back{c}", lifted, e, replaced[e])
+
+        first_product(0, (1, 0), ("gt_turned", "w1_turned0"))
+        first_product(1, (2, 3), ("w1_turned1", "a00"))
+        for c in (1, 2, 3):
+            activate(tanh_half, "tanh_half", c, ACT.Tanh, tx_half)
+        early_blocks = turn_tanh((1,), ("a01",))
+        late_blocks = turn_tanh((2, 3), ("a11", "a10"))
+        lift((1,), early_blocks, ("tanh_turned1",))
         activate(silu_neg, "silu_neg", 0, ACT.Silu, tx_neg)
-        activate(tanh_half, "tanh_half", 0, ACT.Tanh, tx_half)
-        for c in (2, 3):
-            activate(tanh_half, "tanh_half", c, ACT.Tanh, tx_half, paired=False)
         activate(silu_neg, "silu_neg", 1, ACT.Silu, tx_neg)
-        activate(tanh_half, "tanh_half", 1, ACT.Tanh, tx_half)
-
-        tanh_turned = []
-        for u, replaces in enumerate(("a01", "a10")):
-            tanh_turned.append(bank(f"tanh_turned{u}", replaces))
-            for b in range(2):
-                for e in range(2):
-                    nc.tensor.transpose(
-                        tanh_turned[u][:, block(2 * b + e)], tanh_half[2 + e][:, block(2 * b + u)], ident[:]
-                    )
+        activate(tanh_half, "tanh_half", 0, ACT.Tanh, tx_half)
 
         dy_got = held("dy_got", [P, LANES, N], F32)
         for t in range(LANES - 1):
@@ -254,42 +277,28 @@ def tile_attend_gdepth_sil_pl_kernel(tc, xT, dyT, w1, w2, cf, gt, tx, c1, offs, 
             )
             return grouped
 
-        dh_banks = []
+        dh_banks = {}
 
-        def make_dh(dy_mx, replaced):
-            for e, replaces in enumerate(replaced):
-                dh_banks.append(bank(f"dh{len(dh_banks)}", replaces))
-                product(dh_banks[-1], dy_mx, E5M2, block(e), w2_mx, E4M3)
+        def make_dh(dy_mx, chunks, replaced):
+            for c, replaces in zip(chunks, replaced):
+                dh_banks[c] = bank(f"dh{c}", replaces)
+                product(dh_banks[c], dy_mx, E5M2, block(c % 2), w2_mx, E4M3)
 
         dy_rounded = round_dy(0, nc.vector.tensor_copy)
-        w2_grouped = held("w2_grouped", [P, F * LANES], BF16)
-        nc.vector.tensor_copy(
-            out=w2_grouped[:].rearrange("p (u m e j) -> p m j u e", u=2, e=2, j=LANES),
-            in_=w2_raw[:].rearrange("p j (m u e) -> p m j u e", u=2, e=2),
-        )
-        dy0_mx = quantize("dy0", dy_rounded[:], E5M2, replaces="w2_raw")
+        w2_grouped = round_weights("w2_grouped", w2_raw, W2_VECTOR)
+        da_mx = (held("da_codes", [P, N], U32, replaces="tanh_half1"), held("da_scales", [P, N], U8))
+        dy0_mx = tuple(part[:, half(1)] for part in da_mx)
+        nc.vector.quantize_mx(out=dy0_mx[0].bitcast(E5M2), scales=dy0_mx[1], in_=dy_rounded[:])
         w2_mx = quantize("w2", w2_grouped[:], E4M3)
-        make_dh(dy0_mx, ("a11", "a_turned0"))
-        lifted = scale_lanes("lifted", tanh_turned, ACT.Identity, c_col, True)
-        lifted_back = {
-            2 + e: bank(f"lifted_back{2 + e}", replaces) for e, replaces in enumerate(("a_turned1", "tanh_turned0"))
-        }
-        for e in range(2):
-            for t in range(LANES):
-                nc.tensor.transpose(lane_places(lifted_back[2 + e], t), lifted[:, t, block(e)], ident[:])
-
+        make_dh(dy0_mx, (1, 0), ("a_turned1", "a_turned0"))
 
         slope = {}
-        da_mx = (held("da_codes", [P, N], U32), held("da_scales", [P, N], U8))
-        nc.gpsimd.memset(da_mx[0][:, half(1)].bitcast(I32), 0)
-        nc.gpsimd.memset(da_mx[1][:, half(1)].bitcast(I32), 0)
         da_grouped = held("da_grouped", [P, N * LANES], BF16)
-        da_words = da_grouped[:].bitcast(F32).rearrange("p (c i u) -> p c i u", c=CHUNKS, u=2)
+        da_words = da_grouped[:].bitcast(F32).rearrange("p (c g i u) -> p c g u i", c=CHUNKS, u=2, i=RUN)
 
-        def times_bank(name, c, factor):
-            result = held(name, [P, F], F32)
+        def times_bank(result, c, factor):
             nc.vector.scalar_tensor_tensor(
-                out=result[:],
+                out=result,
                 in0=silu_neg[c][:],
                 scalar=-1.0,
                 in1=factor[:],
@@ -304,7 +313,7 @@ def tile_attend_gdepth_sil_pl_kernel(tc, xT, dyT, w1, w2, cf, gt, tx, c1, offs, 
                 out=da[:],
                 in0=dh_banks[c][:],
                 scalar=slot_factor[:, c : c + 1],
-                in1=slope[c][:],
+                in1=slope[c],
                 op0=ALU.mult,
                 op1=ALU.mult,
             )
@@ -313,7 +322,7 @@ def tile_attend_gdepth_sil_pl_kernel(tc, xT, dyT, w1, w2, cf, gt, tx, c1, offs, 
 
         def fetch_da(first, count, turned):
             nc.scalar.copy(
-                out=da_words[:, first : first + count], in_=turned.rearrange("p (c u i) -> p c i u", c=count, u=2)
+                out=da_words[:, first : first + count], in_=turned.rearrange("p (c u g i) -> p c g u i", c=count, u=2, i=RUN)
             )
 
         def quantize_da(h):
@@ -338,26 +347,25 @@ def tile_attend_gdepth_sil_pl_kernel(tc, xT, dyT, w1, w2, cf, gt, tx, c1, offs, 
                 out=out_plane[t][:].indirect(entries(first, last)), in0=dx[:], in1=dy_got[:, t, first:last], op=ALU.add
             )
 
-        part = [times_bank(f"part{c}", c, c_row) for c in range(2)]
-        for c in range(2):
-            slope[c] = held(f"slope{c}", [P, F], F32)
-            nc.vector.scalar_tensor_tensor(
-                out=slope[c][:], in0=tanh_half[c][:], scalar=1.0, in1=part[c][:], op0=ALU.add, op1=ALU.mult
-            )
-        dy_rounded = round_dy(1, nc.scalar.copy, replaces="c_col")
-        for c, replaces in enumerate(("tanh_turned1", "c_row")):
-            da_turned = bank(f"da_turned{c}", replaces)
+        part = times_bank(held("part", [P, F], F32, replaces="w2_raw")[:], 0, c_row)
+        slope[1] = times_bank(held("slope1", [P, F], F32, replaces="w2_grouped")[:], 1, lifted_back[1])
+        slope[0] = held("slope0", [P, F], F32)[:]
+        nc.vector.scalar_tensor_tensor(out=slope[0], in0=tanh_half[0][:], scalar=1.0, in1=part, op0=ALU.add, op1=ALU.mult)
+        lift((2, 3), late_blocks, ("c_row", "lifted_back1"))
+        dy_rounded = round_dy(1, nc.scalar.copy, replaces="silu_neg0")
+        for c in (1, 0):
+            da_turned = bank(f"da_turned{c}", f"tanh_turned{3 - c}")
             make_da(c, da_turned[:, half(0)])
             fetch_da(c, 1, da_turned[:, half(0)])
         activate(silu_neg, "silu_neg", 2, ACT.Silu, tx_neg)
         activate(silu_neg, "silu_neg", 3, ACT.Silu, tx_neg)
-        make_dh(quantize("dy1", dy_rounded[:], E5M2, replaces="slope0"), ("dh0", "dh1"))
+        make_dh(quantize("dy1", dy_rounded[:], E5M2, replaces="part"), (2, 3), ("dh1", "dh0"))
         w1t_mx = quantize("w1t", w1t_grouped[:], E4M3, replaces="slope1")
         quantize_da(0)
         early = (PLANE_ORDER[0], PLANE_ORDER[2])
         early_banks = [make_dx("dx_early0", early[0], "da_turned0")]
         for c in (2, 3):
-            slope[c] = times_bank(f"slope{c}", c, lifted_back[c])
+            slope[c] = times_bank(held(f"slope{c}", [P, F], F32)[:], c, lifted_back[c])
         da_turned = bank("da_turned23", replaces="da_turned1")
         make_da(2, da_turned[:, half(0)])
         make_da(3, da_turned[:, half(1)])
@@ -396,10 +404,10 @@ def tile_attend_gdepth_sil_pl_kernel(tc, xT, dyT, w1, w2, cf, gt, tx, c1, offs, 
             nc.vector.tensor_copy(out=out_lane[last_plane][:, cols], in_=out_plane[last_plane][:, cols])
 
         out_grouped = held("out_grouped", [P, T * LANES], BF16)
-        woven = out_grouped[:].bitcast(U32).rearrange("p (n u) -> p n u", u=2)
-        pair_words = out_pairs[:].bitcast(U32).rearrange("p u n -> p n u")
-        nc.scalar.copy(out=woven[:, WEAVE_VECTOR:], in_=pair_words[:, WEAVE_VECTOR:])
-        for cols in (slice(0, T // 2), slice(T // 2, WEAVE_VECTOR)):
+        woven = out_grouped[:].bitcast(U32).rearrange("p (g i u) -> p g u i", u=2, i=RUN)
+        pair_words = out_pairs[:].bitcast(U32).rearrange("p u (g i) -> p g u i", i=RUN)
+        nc.scalar.copy(out=woven[:, WEAVE_VECTOR // RUN :], in_=pair_words[:, WEAVE_VECTOR // RUN :])
+        for cols in (slice(0, T // 2 // RUN), slice(T // 2 // RUN, WEAVE_VECTOR // RUN)):
             nc.vector.tensor_copy(out=woven[:, cols].bitcast(I32), in_=pair_words[:, cols].bitcast(I32))
 
         out_codes = held("out_codes", [P, T], U32)

@@ -27,8 +27,6 @@ QUAD = 32
 RUN = 4
 LAST = P - 1
 W2_VECTOR = 128
-LAST_VECTOR = 640
-WEAVE_VECTOR = 576
 PLANE_ORDER = (2, 0, 1, 3)
 FLOPS = 3 * 2 * D * F * N
 
@@ -89,8 +87,8 @@ def tile_attend_gdepth_sil_pl_kernel(tc, xT, dyT, w1, w2, cf, gt, tx, c1, offs, 
         scalar_lanes, vector_lanes = (2, 3), (0, 1)
 
         nc.sync.dma_start(offsets[:], offs)
-        nc.sync.dma_start(out=tx_pool[LAST:, :], in_=tx[LAST:, :])
-        nc.sync.dma_start(out=gt_pool[LAST:, :], in_=gt[LAST:, :])
+        nc.scalar.dma_start(out=tx_pool[LAST:, :], in_=tx[LAST:, :])
+        nc.scalar.dma_start(out=gt_pool[LAST:, :], in_=gt[LAST:, :])
         for k, vector in enumerate((cf, c1)):
             nc.scalar.dma_start(out=unit_rows[P - 2 :, k, :], in_=vector.rearrange("(g n) o -> g (n o)", g=2))
         for t in (2, 0):
@@ -193,10 +191,6 @@ def tile_attend_gdepth_sil_pl_kernel(tc, xT, dyT, w1, w2, cf, gt, tx, c1, offs, 
                 out=w1t_pairs[:, h], in_=turned[:].bitcast(BF16).rearrange("p (t c i b) -> p c t i b", t=LANES, i=2, b=2)
             )
 
-        c_row = bank("c_row", replaces="tx_turned")
-        for k in range(LANES):
-            nc.tensor.transpose(c_row[:, block(k)], c_col[:, k : k + 1].to_broadcast([P, P]), ident[:])
-
         def scale_blocks(name, blocks, func, column, bias):
             scaled = held(name, [P, LANES, blocks[0].shape[1]], F32)
             for k in range(LANES):
@@ -251,16 +245,15 @@ def tile_attend_gdepth_sil_pl_kernel(tc, xT, dyT, w1, w2, cf, gt, tx, c1, offs, 
             for e, c in enumerate(chunks):
                 lifted_back[c] = turn_to_slots(f"lifted_back{c}", lifted, e, replaced[e])
 
-        first_product(0, (1, 0), ("gt_turned", "w1_turned0"))
-        first_product(1, (2, 3), ("w1_turned1", "a00"))
-        for c in (1, 2, 3):
+        first_product(0, (0, 1), ("gt_turned", "w1_turned0"))
+        first_product(1, (2, 3), ("w1_turned1", "tx_turned"))
+        for c in range(CHUNKS):
             activate(tanh_half, "tanh_half", c, ACT.Tanh, tx_half)
-        early_blocks = turn_tanh((1,), ("a01",))
-        late_blocks = turn_tanh((2, 3), ("a11", "a10"))
-        lift((1,), early_blocks, ("tanh_turned1",))
+        early_blocks = turn_tanh((0, 1), ("a00", "a01"))
+        late_blocks = turn_tanh((2, 3), ("a10", "a11"))
+        lift((0, 1), early_blocks, ("tanh_turned0", "tanh_turned1"))
         activate(silu_neg, "silu_neg", 0, ACT.Silu, tx_neg)
         activate(silu_neg, "silu_neg", 1, ACT.Silu, tx_neg)
-        activate(tanh_half, "tanh_half", 0, ACT.Tanh, tx_half)
 
         dy_got = held("dy_got", [P, LANES, N], F32)
         for t in range(LANES - 1):
@@ -290,7 +283,7 @@ def tile_attend_gdepth_sil_pl_kernel(tc, xT, dyT, w1, w2, cf, gt, tx, c1, offs, 
         dy0_mx = tuple(part[:, half(1)] for part in da_mx)
         nc.vector.quantize_mx(out=dy0_mx[0].bitcast(E5M2), scales=dy0_mx[1], in_=dy_rounded[:])
         w2_mx = quantize("w2", w2_grouped[:], E4M3)
-        make_dh(dy0_mx, (1, 0), ("a_turned1", "a_turned0"))
+        make_dh(dy0_mx, (0, 1), ("a_turned0", "a_turned1"))
 
         slope = {}
         da_grouped = held("da_grouped", [P, N * LANES], BF16)
@@ -347,20 +340,26 @@ def tile_attend_gdepth_sil_pl_kernel(tc, xT, dyT, w1, w2, cf, gt, tx, c1, offs, 
                 out=out_plane[t][:].indirect(entries(first, last)), in0=dx[:], in1=dy_got[:, t, first:last], op=ALU.add
             )
 
-        part = times_bank(held("part", [P, F], F32, replaces="w2_raw")[:], 0, c_row)
-        slope[1] = times_bank(held("slope1", [P, F], F32, replaces="w2_grouped")[:], 1, lifted_back[1])
-        slope[0] = held("slope0", [P, F], F32)[:]
-        nc.vector.scalar_tensor_tensor(out=slope[0], in0=tanh_half[0][:], scalar=1.0, in1=part, op0=ALU.add, op1=ALU.mult)
-        lift((2, 3), late_blocks, ("c_row", "lifted_back1"))
-        dy_rounded = round_dy(1, nc.scalar.copy, replaces="silu_neg0")
-        for c in (1, 0):
-            da_turned = bank(f"da_turned{c}", f"tanh_turned{3 - c}")
+        w1t_mx = quantize("w1t", w1t_grouped[:], E4M3, replaces="w2_raw")
+        for c in range(2):
+            slope[c] = times_bank(held(f"slope{c}", [P, F], F32)[:], c, lifted_back[c])
+        dy_rounded = held("dy_grouped1", [P, HALF * LANES], BF16, replaces="w1t_grouped")
+        nc.gpsimd.tensor_scalar(
+            out=dy_rounded[:].rearrange("p (i t) -> p i t", t=LANES),
+            in0=dy_got[:, :, half(1)].rearrange("p t i -> p i t"),
+            scalar1=1.0,
+            scalar2=0.0,
+            op0=ALU.mult,
+            op1=ALU.add,
+        )
+        for c in range(2):
+            da_turned = bank(f"da_turned{c}", f"tanh_turned{2 + c}")
             make_da(c, da_turned[:, half(0)])
             fetch_da(c, 1, da_turned[:, half(0)])
+        lift((2, 3), late_blocks, ("lifted_back0", "lifted_back1"))
         activate(silu_neg, "silu_neg", 2, ACT.Silu, tx_neg)
         activate(silu_neg, "silu_neg", 3, ACT.Silu, tx_neg)
-        make_dh(quantize("dy1", dy_rounded[:], E5M2, replaces="part"), (2, 3), ("dh1", "dh0"))
-        w1t_mx = quantize("w1t", w1t_grouped[:], E4M3, replaces="slope1")
+        make_dh(quantize("dy1", dy_rounded[:], E5M2, replaces="slope0"), (2, 3), ("dh0", "dh1"))
         quantize_da(0)
         early = (PLANE_ORDER[0], PLANE_ORDER[2])
         early_banks = [make_dx("dx_early0", early[0], "da_turned0")]
@@ -399,26 +398,28 @@ def tile_attend_gdepth_sil_pl_kernel(tc, xT, dyT, w1, w2, cf, gt, tx, c1, offs, 
                 nc.scalar.copy(out=out_lane[t], in_=out_plane[t][:])
             if t == first_plane:
                 dx_rest[last_plane] = fetch_dx("dx_last", dx_banks[last_plane], done[last_plane], N, replaces=f"dx_rest{t}")
-        nc.scalar.copy(out=out_lane[last_plane][:, LAST_VECTOR:], in_=out_plane[last_plane][:, LAST_VECTOR:])
-        for cols in (slice(0, T // 2), slice(T // 2, LAST_VECTOR)):
-            nc.vector.tensor_copy(out=out_lane[last_plane][:, cols], in_=out_plane[last_plane][:, cols])
-
         out_grouped = held("out_grouped", [P, T * LANES], BF16)
         woven = out_grouped[:].bitcast(U32).rearrange("p (g i u) -> p g u i", u=2, i=RUN)
         pair_words = out_pairs[:].bitcast(U32).rearrange("p u (g i) -> p g u i", i=RUN)
-        nc.scalar.copy(out=woven[:, WEAVE_VECTOR // RUN :], in_=pair_words[:, WEAVE_VECTOR // RUN :])
-        for cols in (slice(0, T // 2 // RUN), slice(T // 2 // RUN, WEAVE_VECTOR // RUN)):
+        quarters = [slice(k * T // 4, (k + 1) * T // 4) for k in range(4)]
+        runs = [slice(k * T // 4 // RUN, (k + 1) * T // 4 // RUN) for k in range(4)]
+        for cols in quarters[2:]:
+            nc.scalar.copy(out=out_lane[last_plane][:, cols], in_=out_plane[last_plane][:, cols])
+        for cols in quarters[:2]:
+            nc.vector.tensor_copy(out=out_lane[last_plane][:, cols], in_=out_plane[last_plane][:, cols])
+        for cols in runs[2:]:
+            nc.scalar.copy(out=woven[:, cols], in_=pair_words[:, cols])
+        for cols in runs[:2]:
             nc.vector.tensor_copy(out=woven[:, cols].bitcast(I32), in_=pair_words[:, cols].bitcast(I32))
 
         out_codes = held("out_codes", [P, T], U32)
         out_scales = held("out_scales", [P, T], U8)
         words_hbm = out_1[0].rearrange("p n l -> p (n l)").bitcast(I32)
-        for first, last in ((0, T // 2), (T // 2, 3 * T // 4), (3 * T // 4, T)):
-            cols = slice(first, last)
+        for cols in quarters:
             nc.vector.quantize_mx(
                 out=out_codes[:, cols].bitcast(E4M3),
                 scales=out_scales[:, cols],
-                in_=out_grouped[:, first * LANES : last * LANES],
+                in_=out_grouped[:, cols.start * LANES : cols.stop * LANES],
             )
             nc.sync.dma_start(out=words_hbm[:, cols], in_=out_codes[:, cols].bitcast(I32))
         scales_hbm = out_2[0].bitcast(I32)

@@ -103,8 +103,8 @@ def tile_attend_gdepth_sil_pl_kernel(tc, xT, dyT, w1, w2, cf, gt, tx, c1, offs, 
             nc.sync.dma_start(out=out_plane[t][:], in_=dy_rows[:, t, :])
 
         ident = held("ident", [P, P], F32)
-        nc.gpsimd.memset(unit_rows[: P - 2], 0.0)
         make_identity(nc, ident[:])
+        nc.gpsimd.memset(unit_rows[: P - 2], 0.0)
         for pool_tile in (tx_pool, gt_pool):
             nc.vector.memset(pool_tile[:LAST, :], 0.0)
 
@@ -112,10 +112,9 @@ def tile_attend_gdepth_sil_pl_kernel(tc, xT, dyT, w1, w2, cf, gt, tx, c1, offs, 
         nc.scalar.activation(out=warm[:QUAD, :], in_=tx_pool[:QUAD, 0:1], func=ACT.Silu)
 
         unit_sorted = held("unit_sorted", [P, 2, F // 2], F32)
-        nc.scalar.copy(
-            out=unit_sorted[:].rearrange("p v (u m e) -> p v u m e", u=2, e=2),
-            in_=unit_rows[:].rearrange("p v (m u e) -> p v u m e", u=2, e=2),
-        )
+        sorted_rows = unit_sorted[:].rearrange("p v (u m e) -> p v u m e", u=2, e=2)
+        loaded_rows = unit_rows[:].rearrange("p v (m u e) -> p v u m e", u=2, e=2)
+        nc.scalar.copy(out=sorted_rows[:, 0], in_=loaded_rows[:, 0])
 
         def slot_columns(name, pool_tile):
             got = held(name + "_got", [P, N], F32)
@@ -146,6 +145,7 @@ def tile_attend_gdepth_sil_pl_kernel(tc, xT, dyT, w1, w2, cf, gt, tx, c1, offs, 
                 out=slot_factor[:, c : c + 1], in_=gt_cols[:, c : c + 1], func=ACT.Copy, scale=tx_neg_half[:, c : c + 1]
             )
 
+        nc.gpsimd.tensor_tensor(out=sorted_rows[:, 1], in0=loaded_rows[:, 0], in1=loaded_rows[:, 1], op=ALU.mult)
         unit_turned = bank("unit_turned")
         for v in range(2):
             for u in range(2):
@@ -155,12 +155,7 @@ def tile_attend_gdepth_sil_pl_kernel(tc, xT, dyT, w1, w2, cf, gt, tx, c1, offs, 
             out=unit_cols[:].rearrange("p (b g) -> p b g", g=2),
             in_=unit_turned[:].rearrange("p (b r) -> p b r", r=P)[:, :, P - 2 :],
         )
-        cf_col = unit_cols[:, :LANES]
-        c_col = held("c_col", [P, LANES], F32)
-        for k in range(LANES):
-            nc.scalar.activation(
-                out=c_col[:, k : k + 1], in_=unit_cols[:, LANES + k : LANES + k + 1], func=ACT.Copy, scale=cf_col[:, k : k + 1]
-            )
+        cf_col, c_col = unit_cols[:, :LANES], unit_cols[:, LANES:]
 
         def round_weights(name, raw, share):
             grouped = held(name, [P, F * LANES], BF16)
@@ -184,7 +179,7 @@ def tile_attend_gdepth_sil_pl_kernel(tc, xT, dyT, w1, w2, cf, gt, tx, c1, offs, 
         w1t_pairs = w1t_grouped[:].rearrange("p (h b c i t) -> p h c t i b", h=2, b=2, i=2, t=LANES)
         w1_words = w1_grouped[:].bitcast(F32).rearrange("p (u m e h) -> p h u e m", u=2, e=2, h=2)
         for h in range(2):
-            turned = bank(f"w1_turned{h}", replaces="unit_turned" if h else "")
+            turned = bank(f"w1_turned{h}", replaces="tx_turned" if h else "")
             for t in range(LANES):
                 nc.tensor.transpose(turned[:, block(t)], w1_words[:, h, t // 2, t % 2, :], ident[:])
             nc.scalar.copy(
@@ -246,7 +241,7 @@ def tile_attend_gdepth_sil_pl_kernel(tc, xT, dyT, w1, w2, cf, gt, tx, c1, offs, 
                 lifted_back[c] = turn_to_slots(f"lifted_back{c}", lifted, e, replaced[e])
 
         first_product(0, (0, 1), ("gt_turned", "w1_turned0"))
-        first_product(1, (2, 3), ("w1_turned1", "tx_turned"))
+        first_product(1, (2, 3), ("w1_turned1", "unit_turned"))
         for c in range(CHUNKS):
             activate(tanh_half, "tanh_half", c, ACT.Tanh, tx_half)
         early_blocks = turn_tanh((0, 1), ("a00", "a01"))

@@ -103,18 +103,14 @@ def tile_attend_gdepth_sil_pl_kernel(tc, xT, dyT, w1, w2, cf, gt, tx, c1, offs, 
             nc.sync.dma_start(out=out_plane[t][:], in_=dy_rows[:, t, :])
 
         ident = held("ident", [P, P], F32)
-        make_identity(nc, ident[:])
-        nc.gpsimd.memset(unit_rows[: P - 2], 0.0)
+        nc.vector.memset(ident[:], 0.0)
+        make_identity(nc, ident[:], nomemset=True)
         for pool_tile in (tx_pool, gt_pool):
             nc.vector.memset(pool_tile[:LAST, :], 0.0)
 
-        warm = held("warm", [P, 1], F32)
-        nc.scalar.activation(out=warm[:QUAD, :], in_=tx_pool[:QUAD, 0:1], func=ACT.Silu)
-
-        unit_sorted = held("unit_sorted", [P, 2, F // 2], F32)
-        sorted_rows = unit_sorted[:].rearrange("p v (u m e) -> p v u m e", u=2, e=2)
-        loaded_rows = unit_rows[:].rearrange("p v (m u e) -> p v u m e", u=2, e=2)
-        nc.scalar.copy(out=sorted_rows[:, 0], in_=loaded_rows[:, 0])
+        nc.scalar.activation(
+            out=unit_rows[: P - 2].rearrange("p v n -> p (v n)"), in_=tx_pool[: P - 2, :F], func=ACT.Silu
+        )
 
         def slot_columns(name, pool_tile):
             got = held(name + "_got", [P, N], F32)
@@ -145,17 +141,25 @@ def tile_attend_gdepth_sil_pl_kernel(tc, xT, dyT, w1, w2, cf, gt, tx, c1, offs, 
                 out=slot_factor[:, c : c + 1], in_=gt_cols[:, c : c + 1], func=ACT.Copy, scale=tx_neg_half[:, c : c + 1]
             )
 
-        nc.gpsimd.tensor_tensor(out=sorted_rows[:, 1], in0=loaded_rows[:, 0], in1=loaded_rows[:, 1], op=ALU.mult)
-        unit_turned = bank("unit_turned")
-        for v in range(2):
+        def unit_columns(name, rows):
+            ordered = held(name + "_ordered", [P, F // 2], F32)
+            nc.scalar.copy(
+                out=ordered[:].rearrange("p (u m e) -> p u m e", u=2, e=2),
+                in_=rows.rearrange("p (m u e) -> p u m e", u=2, e=2),
+            )
+            turned = bank(name + "_turned")
             for u in range(2):
-                nc.tensor.transpose(unit_turned[:, block(2 * v + u)], unit_sorted[:, v, block(u)], ident[:])
-        unit_cols = held("unit_cols", [P, 2 * LANES], F32)
-        nc.scalar.copy(
-            out=unit_cols[:].rearrange("p (b g) -> p b g", g=2),
-            in_=unit_turned[:].rearrange("p (b r) -> p b r", r=P)[:, :, P - 2 :],
-        )
-        cf_col, c_col = unit_cols[:, :LANES], unit_cols[:, LANES:]
+                nc.tensor.transpose(turned[:, block(u)], ordered[:, block(u)], ident[:])
+            return turned[:, half(0)].rearrange("p (u r) -> p u r", u=2)[:, :, P - 2 :]
+
+        cf_col = held("cf_col", [P, LANES], F32)
+        c_col = held("c_col", [P, LANES], F32)
+        nc.scalar.copy(out=cf_col[:].rearrange("p (u g) -> p u g", u=2), in_=unit_columns("cf", unit_rows[:, 0, :]))
+        c1_cols = unit_columns("c1", unit_rows[:, 1, :])
+        for k in range(LANES):
+            nc.scalar.activation(
+                out=c_col[:, k : k + 1], in_=c1_cols[:, k // 2, k % 2 : k % 2 + 1], func=ACT.Copy, scale=cf_col[:, k : k + 1]
+            )
 
         def round_weights(name, raw, share):
             grouped = held(name, [P, F * LANES], BF16)
@@ -205,7 +209,7 @@ def tile_attend_gdepth_sil_pl_kernel(tc, xT, dyT, w1, w2, cf, gt, tx, c1, offs, 
         silu_neg, tanh_half, a_turned = {}, {}, {}
 
         def first_product(h, chunks, replaced):
-            banks = [bank(f"a{h}{u}") for u in range(2)]
+            banks = [bank(f"a{h}{u}", "c1_turned" if h and u else "") for u in range(2)]
             for k, out in enumerate(halves_of(banks)):
                 nc.tensor.matmul_mx(
                     out=out,
@@ -241,7 +245,7 @@ def tile_attend_gdepth_sil_pl_kernel(tc, xT, dyT, w1, w2, cf, gt, tx, c1, offs, 
                 lifted_back[c] = turn_to_slots(f"lifted_back{c}", lifted, e, replaced[e])
 
         first_product(0, (0, 1), ("gt_turned", "w1_turned0"))
-        first_product(1, (2, 3), ("w1_turned1", "unit_turned"))
+        first_product(1, (2, 3), ("w1_turned1", "cf_turned"))
         for c in range(CHUNKS):
             activate(tanh_half, "tanh_half", c, ACT.Tanh, tx_half)
         early_blocks = turn_tanh((0, 1), ("a00", "a01"))

@@ -21,13 +21,15 @@ F = 512
 T = 1024
 N = 512
 CHUNKS = N // P
+GROUPS = F // P
 HALF = N // 2
 BAND = 16
 QUAD = 32
 RUN = 4
 LAST = P - 1
-W2_VECTOR = 128
+UNIT_ROW = P - 2
 PLANE_ORDER = (2, 0, 1, 3)
+EARLY_PLANES = (2, 1)
 FLOPS = 3 * 2 * D * F * N
 
 
@@ -64,7 +66,7 @@ def tile_attend_gdepth_sil_pl_kernel(tc, xT, dyT, w1, w2, cf, gt, tx, c1, offs, 
 
         def product(out, still, still_fmt, cols, moving, moving_fmt):
             nc.tensor.matmul_mx(
-                out=out[:],
+                out=out,
                 lhsT=still[0][:, cols].bitcast(still_fmt),
                 lhsT_scale=still[1][:, cols],
                 rhs=moving[0][:].bitcast(moving_fmt),
@@ -84,13 +86,12 @@ def tile_attend_gdepth_sil_pl_kernel(tc, xT, dyT, w1, w2, cf, gt, tx, c1, offs, 
         out_plane = [held(f"out_plane{t}", [P, T], F32) for t in range(LANES)]
         x_rows = xT.rearrange("(p t) n -> p t n", t=LANES)
         dy_rows = dyT.rearrange("(p t) n -> p t n", t=LANES)
-        scalar_lanes, vector_lanes = (2, 3), (0, 1)
 
         nc.sync.dma_start(offsets[:], offs)
         nc.scalar.dma_start(out=tx_pool[LAST:, :], in_=tx[LAST:, :])
         nc.scalar.dma_start(out=gt_pool[LAST:, :], in_=gt[LAST:, :])
-        for k, vector in enumerate((cf, c1)):
-            nc.scalar.dma_start(out=unit_rows[P - 2 :, k, :], in_=vector.rearrange("(g n) o -> g (n o)", g=2))
+        for v, vector in enumerate((cf, c1)):
+            nc.scalar.dma_start(out=unit_rows[UNIT_ROW:, v, :], in_=vector.rearrange("(g n) o -> g (n o)", g=2))
         for t in (2, 0):
             nc.sync.dma_start(out=x_plane[t][:], in_=x_rows[:, t, :])
         nc.sync.dma_start(out=w1_raw[:], in_=w1.rearrange("(p j) f -> p j f", j=LANES))
@@ -109,7 +110,7 @@ def tile_attend_gdepth_sil_pl_kernel(tc, xT, dyT, w1, w2, cf, gt, tx, c1, offs, 
             nc.vector.memset(pool_tile[:LAST, :], 0.0)
 
         nc.scalar.activation(
-            out=unit_rows[: P - 2].rearrange("p v n -> p (v n)"), in_=tx_pool[: P - 2, :F], func=ACT.Silu
+            out=unit_rows[:UNIT_ROW].rearrange("p v n -> p (v n)"), in_=tx_pool[:UNIT_ROW, :F], func=ACT.Silu
         )
 
         def slot_columns(name, pool_tile):
@@ -125,13 +126,13 @@ def tile_attend_gdepth_sil_pl_kernel(tc, xT, dyT, w1, w2, cf, gt, tx, c1, offs, 
 
         x_grouped = held("x_grouped", [P, N * LANES], BF16)
         x_lanes = x_grouped[:].rearrange("p (i t) -> p i t", t=LANES)
-        x_rounded = {t: held(f"x_rounded{t}", [P, T], BF16) for t in scalar_lanes}
+        x_rounded = {t: held(f"x_rounded{t}", [P, T], BF16) for t in (2, 3)}
         nc.scalar.activation(out=x_rounded[2][:], in_=x_plane[2][:], func=ACT.Copy)
         nc.scalar.activation(out=x_lanes[:, :, 2], in_=x_rounded[2][:].indirect(offsets[:]), func=ACT.Copy)
         nc.vector.tensor_copy(out=x_lanes[:, :, 0], in_=x_plane[0][:].indirect(offsets[:]))
 
         factors = held("factors", [P, 3, CHUNKS], F32, replaces="x_rounded2")
-        tx_neg, tx_half, tx_neg_half = (factors[:, k, :] for k in range(3))
+        tx_neg, tx_half, tx_neg_half = (factors[:, n, :] for n in range(3))
         slot_factor = held("slot_factor", [P, CHUNKS], F32)
         nc.scalar.activation(out=tx_neg[:], in_=tx_cols, func=ACT.Copy, scale=-1.0)
         nc.scalar.activation(out=tx_half[:], in_=tx_cols, func=ACT.Copy, scale=0.5)
@@ -150,27 +151,26 @@ def tile_attend_gdepth_sil_pl_kernel(tc, xT, dyT, w1, w2, cf, gt, tx, c1, offs, 
             turned = bank(name + "_turned")
             for u in range(2):
                 nc.tensor.transpose(turned[:, block(u)], ordered[:, block(u)], ident[:])
-            return turned[:, half(0)].rearrange("p (u r) -> p u r", u=2)[:, :, P - 2 :]
+            return turned[:, : 2 * P].rearrange("p (u r) -> p u r", u=2)[:, :, UNIT_ROW:]
 
-        cf_col = held("cf_col", [P, LANES], F32)
-        c_col = held("c_col", [P, LANES], F32)
+        cf_col = held("cf_col", [P, GROUPS], F32)
+        c_col = held("c_col", [P, GROUPS], F32)
         nc.scalar.copy(out=cf_col[:].rearrange("p (u g) -> p u g", u=2), in_=unit_columns("cf", unit_rows[:, 0, :]))
         c1_cols = unit_columns("c1", unit_rows[:, 1, :])
-        for k in range(LANES):
+        for k in range(GROUPS):
             nc.scalar.activation(
                 out=c_col[:, k : k + 1], in_=c1_cols[:, k // 2, k % 2 : k % 2 + 1], func=ACT.Copy, scale=cf_col[:, k : k + 1]
             )
 
-        def round_weights(name, raw, share):
+        def round_weights(name, raw):
             grouped = held(name, [P, F * LANES], BF16)
-            dst = grouped[:].rearrange("p (u m e j) -> p m j u e", u=2, e=2, j=LANES)
-            src = raw[:].rearrange("p j (m u e) -> p m j u e", u=2, e=2)
-            nc.vector.tensor_copy(out=dst[:, :share], in_=src[:, :share])
-            if share < P:
-                nc.scalar.copy(out=dst[:, share:], in_=src[:, share:])
+            nc.vector.tensor_copy(
+                out=grouped[:].rearrange("p (u m e j) -> p m j u e", u=2, e=2, j=LANES),
+                in_=raw[:].rearrange("p j (m u e) -> p m j u e", u=2, e=2),
+            )
             return grouped
 
-        w1_grouped = round_weights("w1_grouped", w1_raw, P)
+        w1_grouped = round_weights("w1_grouped", w1_raw)
         nc.vector.tensor_copy(out=x_rounded[3][:], in_=x_plane[3][:])
         w1_mx = quantize("w1", w1_grouped[:], E4M3)
         nc.scalar.activation(out=x_lanes[:, :, 3], in_=x_rounded[3][:].indirect(offsets[:]), func=ACT.Copy)
@@ -180,79 +180,62 @@ def tile_attend_gdepth_sil_pl_kernel(tc, xT, dyT, w1, w2, cf, gt, tx, c1, offs, 
         x_mx = [quantize(f"x{h}", x_grouped[:, h * HALF * LANES : (h + 1) * HALF * LANES], E4M3) for h in range(2)]
 
         w1t_grouped = held("w1t_grouped", [P, D * LANES], BF16, replaces="x_plane3")
-        w1t_pairs = w1t_grouped[:].rearrange("p (h b c i t) -> p h c t i b", h=2, b=2, i=2, t=LANES)
-        w1_words = w1_grouped[:].bitcast(F32).rearrange("p (u m e h) -> p h u e m", u=2, e=2, h=2)
-        for h in range(2):
-            turned = bank(f"w1_turned{h}", replaces="tx_turned" if h else "")
+        w1t_pairs = w1t_grouped[:].rearrange("p (s b n i t) -> p s n t i b", s=2, b=2, i=2, t=LANES)
+        w1_words = w1_grouped[:].bitcast(F32).rearrange("p (u m e s) -> p s u e m", u=2, e=2, s=2)
+        for s, replaces in enumerate(("", "tx_turned")):
+            turned = bank(f"w1_turned{s}", replaces)
             for t in range(LANES):
-                nc.tensor.transpose(turned[:, block(t)], w1_words[:, h, t // 2, t % 2, :], ident[:])
+                nc.tensor.transpose(turned[:, block(t)], w1_words[:, s, t // 2, t % 2, :], ident[:])
             nc.scalar.copy(
-                out=w1t_pairs[:, h], in_=turned[:].bitcast(BF16).rearrange("p (t c i b) -> p c t i b", t=LANES, i=2, b=2)
+                out=w1t_pairs[:, s], in_=turned[:].bitcast(BF16).rearrange("p (t n i b) -> p n t i b", t=LANES, i=2, b=2)
             )
 
-        def scale_blocks(name, blocks, func, column, bias):
-            scaled = held(name, [P, LANES, blocks[0].shape[1]], F32)
-            for k in range(LANES):
-                extra = {"bias": column[:, k : k + 1]} if bias else {}
-                nc.scalar.activation(out=scaled[:, k, :], in_=blocks[k], func=func, scale=column[:, k : k + 1], **extra)
+        def groups_of(banks):
+            return [banks[k // 2][:, half(k % 2)] for k in range(GROUPS)]
+
+        def scale_groups(name, groups, func, column, with_bias):
+            scaled = held(name, [P, GROUPS, HALF], F32)
+            for k in range(GROUPS):
+                extra = {"bias": column[:, k : k + 1]} if with_bias else {}
+                nc.scalar.activation(out=scaled[:, k, :], in_=groups[k], func=func, scale=column[:, k : k + 1], **extra)
             return scaled
 
-        def halves_of(banks):
-            return [banks[k // 2][:, half(k % 2)] for k in range(LANES)]
-
-        def turn_to_slots(name, scaled, e, replaces):
-            turned = bank(name, replaces)
-            for k in range(LANES):
-                nc.tensor.transpose(turned[:, block(k)], scaled[:, k, block(e)], ident[:])
+        def turn_to_slots(name, scaled, h, replaced):
+            turned = {}
+            for c, replaces in zip((2 * h, 2 * h + 1), replaced):
+                turned[c] = bank(f"{name}{c}", replaces)
+                for k in range(GROUPS):
+                    nc.tensor.transpose(turned[c][:, block(k)], scaled[:, k, block(c % 2)], ident[:])
             return turned
 
-        silu_neg, tanh_half, a_turned = {}, {}, {}
+        def first_product(h, replaced, replaced_turned):
+            groups = groups_of([bank(f"a{h}{u}", replaces) for u, replaces in enumerate(replaced)])
+            for k in range(GROUPS):
+                product(groups[k], w1_mx, E4M3, block(k), x_mx[h], E4M3)
+            return turn_to_slots("a_turned", scale_groups(f"a_scaled{h}", groups, ACT.Copy, cf_col, False), h, replaced_turned)
 
-        def first_product(h, chunks, replaced):
-            banks = [bank(f"a{h}{u}", "c1_turned" if h and u else "") for u in range(2)]
-            for k, out in enumerate(halves_of(banks)):
-                nc.tensor.matmul_mx(
-                    out=out,
-                    lhsT=w1_mx[0][:, block(k)].bitcast(E4M3),
-                    lhsT_scale=w1_mx[1][:, block(k)],
-                    rhs=x_mx[h][0][:].bitcast(E4M3),
-                    rhs_scale=x_mx[h][1][:],
-                    start=True,
-                    stop=True,
-                )
-            a_scaled = scale_blocks(f"a_scaled{h}", halves_of(banks), ACT.Copy, cf_col, False)
-            for c, replaces in zip(chunks, replaced):
-                a_turned[c] = turn_to_slots(f"a_turned{c}", a_scaled, c % 2, replaces)
+        def activate(name, c, func, scale):
+            result = held(f"{name}{c}", [P, F], F32)
+            nc.scalar.activation(out=result[:], in_=a_turned[c][:], func=func, scale=scale[:, c : c + 1])
+            return result
 
-        def activate(kept, name, c, func, scale):
-            kept[c] = held(f"{name}{c}", [P, F], F32)
-            nc.scalar.activation(out=kept[c][:], in_=a_turned[c][:], func=func, scale=scale[:, c : c + 1])
+        def turn_tanh(h, replaced):
+            groups = groups_of([bank(f"tanh_turned{2 * h + u}", replaces) for u, replaces in enumerate(replaced)])
+            for k in range(GROUPS):
+                for e in range(2):
+                    nc.tensor.transpose(groups[k][:, block(e)], tanh_half[2 * h + e][:, block(k)], ident[:])
+            return groups
 
-        def turn_tanh(chunks, replaced):
-            banks = [bank(f"tanh_turned{c}", replaces) for c, replaces in zip(chunks, replaced)]
-            width = len(chunks) * P
-            blocks = [banks[k * width // 512][:, k * width % 512 :][:, :width] for k in range(LANES)]
-            for k in range(LANES):
-                for e, c in enumerate(chunks):
-                    nc.tensor.transpose(blocks[k][:, block(e)], tanh_half[c][:, block(k)], ident[:])
-            return blocks
+        def lift(h, replaced):
+            lifted = scale_groups(f"lifted{h}", tanh_groups[h], ACT.Identity, c_col, True)
+            return turn_to_slots("lifted_back", lifted, h, replaced)
 
-        lifted_back = {}
-
-        def lift(chunks, blocks, replaced):
-            lifted = scale_blocks(f"lifted{chunks[0]}", blocks, ACT.Identity, c_col, True)
-            for e, c in enumerate(chunks):
-                lifted_back[c] = turn_to_slots(f"lifted_back{c}", lifted, e, replaced[e])
-
-        first_product(0, (0, 1), ("gt_turned", "w1_turned0"))
-        first_product(1, (2, 3), ("w1_turned1", "cf_turned"))
-        for c in range(CHUNKS):
-            activate(tanh_half, "tanh_half", c, ACT.Tanh, tx_half)
-        early_blocks = turn_tanh((0, 1), ("a00", "a01"))
-        late_blocks = turn_tanh((2, 3), ("a10", "a11"))
-        lift((0, 1), early_blocks, ("tanh_turned0", "tanh_turned1"))
-        activate(silu_neg, "silu_neg", 0, ACT.Silu, tx_neg)
-        activate(silu_neg, "silu_neg", 1, ACT.Silu, tx_neg)
+        a_turned = first_product(0, ("", ""), ("gt_turned", "w1_turned0"))
+        a_turned.update(first_product(1, ("", "c1_turned"), ("w1_turned1", "cf_turned")))
+        tanh_half = [activate("tanh_half", c, ACT.Tanh, tx_half) for c in range(CHUNKS)]
+        tanh_groups = [turn_tanh(h, (f"a{h}0", f"a{h}1")) for h in range(2)]
+        lifted_back = lift(0, ("tanh_turned0", "tanh_turned1"))
+        silu_neg = [activate("silu_neg", c, ACT.Silu, tx_neg) for c in (0, 1)]
 
         dy_got = held("dy_got", [P, LANES, N], F32)
         for t in range(LANES - 1):
@@ -260,61 +243,49 @@ def tile_attend_gdepth_sil_pl_kernel(tc, xT, dyT, w1, w2, cf, gt, tx, c1, offs, 
         for h in range(2):
             window = dy_pool[LANES - 1][:].indirect(entries(h * HALF, (h + 1) * HALF))
             nc.vector.tensor_copy(out=dy_got[:, LANES - 1, half(h)], in_=window)
+        dy0_grouped = held("dy0_grouped", [P, HALF * LANES], BF16)
+        nc.vector.tensor_copy(
+            out=dy0_grouped[:].rearrange("p (n i t) -> p n t i", i=RUN, t=LANES),
+            in_=dy_got[:, :, half(0)].rearrange("p t (n i) -> p n t i", i=RUN),
+        )
+        w2_grouped = round_weights("w2_grouped", w2_raw)
 
-        def round_dy(h, rounding_copy, replaces=""):
-            grouped = held(f"dy_grouped{h}", [P, HALF * LANES], BF16, replaces)
-            rounding_copy(
-                out=grouped[:].rearrange("p (c i t) -> p c t i", i=RUN, t=LANES),
-                in_=dy_got[:, :, half(h)].rearrange("p t (c i) -> p c t i", i=RUN),
-            )
-            return grouped
-
-        dh_banks = {}
-
-        def make_dh(dy_mx, chunks, replaced):
-            for c, replaces in zip(chunks, replaced):
-                dh_banks[c] = bank(f"dh{c}", replaces)
-                product(dh_banks[c], dy_mx, E5M2, block(c % 2), w2_mx, E4M3)
-
-        dy_rounded = round_dy(0, nc.vector.tensor_copy)
-        w2_grouped = round_weights("w2_grouped", w2_raw, W2_VECTOR)
         da_mx = (held("da_codes", [P, N], U32, replaces="tanh_half1"), held("da_scales", [P, N], U8))
         dy0_mx = tuple(part[:, half(1)] for part in da_mx)
-        nc.vector.quantize_mx(out=dy0_mx[0].bitcast(E5M2), scales=dy0_mx[1], in_=dy_rounded[:])
+        nc.vector.quantize_mx(out=dy0_mx[0].bitcast(E5M2), scales=dy0_mx[1], in_=dy0_grouped[:])
         w2_mx = quantize("w2", w2_grouped[:], E4M3)
-        make_dh(dy0_mx, (0, 1), ("a_turned0", "a_turned1"))
 
-        slope = {}
+        def make_dh(h, dy_mx, replaced):
+            banks = {}
+            for c, replaces in zip((2 * h, 2 * h + 1), replaced):
+                banks[c] = bank(f"dh{c}", replaces)
+                product(banks[c][:], dy_mx, E5M2, block(c % 2), w2_mx, E4M3)
+            return banks
+
+        dh = make_dh(0, dy0_mx, ("a_turned0", "a_turned1"))
+
         da_grouped = held("da_grouped", [P, N * LANES], BF16)
-        da_words = da_grouped[:].bitcast(F32).rearrange("p (c g i u) -> p c g u i", c=CHUNKS, u=2, i=RUN)
+        da_words = da_grouped[:].bitcast(F32).rearrange("p (c n i u) -> p c n u i", c=CHUNKS, u=2, i=RUN)
 
-        def times_bank(result, c, factor):
+        def make_slope(c):
+            result = held(f"slope{c}", [P, F], F32)
             nc.vector.scalar_tensor_tensor(
-                out=result,
-                in0=silu_neg[c][:],
-                scalar=-1.0,
-                in1=factor[:],
-                op0=ALU.add,
-                op1=ALU.mult,
+                out=result[:], in0=silu_neg[c][:], scalar=-1.0, in1=lifted_back[c][:], op0=ALU.add, op1=ALU.mult
             )
             return result
 
         def make_da(c, turned):
             da = held(f"da{c}", [P, F], BF16)
             nc.vector.scalar_tensor_tensor(
-                out=da[:],
-                in0=dh_banks[c][:],
-                scalar=slot_factor[:, c : c + 1],
-                in1=slope[c],
-                op0=ALU.mult,
-                op1=ALU.mult,
+                out=da[:], in0=dh[c][:], scalar=slot_factor[:, c : c + 1], in1=slope[c][:], op0=ALU.mult, op1=ALU.mult
             )
             for u in range(2):
                 nc.tensor.transpose(turned[:, block(u)], da[:].bitcast(F32)[:, block(u)], ident[:])
 
         def fetch_da(first, count, turned):
             nc.scalar.copy(
-                out=da_words[:, first : first + count], in_=turned.rearrange("p (c u g i) -> p c g u i", c=count, u=2, i=RUN)
+                out=da_words[:, first : first + count],
+                in_=turned.rearrange("p (c u n i) -> p c n u i", c=count, u=2, i=RUN),
             )
 
         def quantize_da(h):
@@ -324,9 +295,9 @@ def tile_attend_gdepth_sil_pl_kernel(tc, xT, dyT, w1, w2, cf, gt, tx, c1, offs, 
                 in_=da_grouped[:, h * HALF * LANES : (h + 1) * HALF * LANES],
             )
 
-        def make_dx(name, j, replaces):
+        def make_dx(name, t, replaces):
             dx_bank = bank(name, replaces)
-            product(dx_bank, w1t_mx, E4M3, block(j), da_mx, E5M2)
+            product(dx_bank[:], w1t_mx, E4M3, block(t), da_mx, E5M2)
             return dx_bank
 
         def fetch_dx(name, dx_bank, first, last, replaces=""):
@@ -340,52 +311,43 @@ def tile_attend_gdepth_sil_pl_kernel(tc, xT, dyT, w1, w2, cf, gt, tx, c1, offs, 
             )
 
         w1t_mx = quantize("w1t", w1t_grouped[:], E4M3, replaces="w2_raw")
-        for c in range(2):
-            slope[c] = times_bank(held(f"slope{c}", [P, F], F32)[:], c, lifted_back[c])
-        dy_rounded = held("dy_grouped1", [P, HALF * LANES], BF16, replaces="w1t_grouped")
+        slope = [make_slope(c) for c in (0, 1)]
+        dy1_grouped = held("dy1_grouped", [P, HALF * LANES], BF16, replaces="w1t_grouped")
         nc.gpsimd.tensor_scalar(
-            out=dy_rounded[:].rearrange("p (i t) -> p i t", t=LANES),
+            out=dy1_grouped[:].rearrange("p (i t) -> p i t", t=LANES),
             in0=dy_got[:, :, half(1)].rearrange("p t i -> p i t"),
             scalar1=1.0,
             scalar2=0.0,
             op0=ALU.mult,
             op1=ALU.add,
         )
-        for c in range(2):
+        for c in (0, 1):
             da_turned = bank(f"da_turned{c}", f"tanh_turned{2 + c}")
             make_da(c, da_turned[:, half(0)])
             fetch_da(c, 1, da_turned[:, half(0)])
-        lift((2, 3), late_blocks, ("lifted_back0", "lifted_back1"))
-        activate(silu_neg, "silu_neg", 2, ACT.Silu, tx_neg)
-        activate(silu_neg, "silu_neg", 3, ACT.Silu, tx_neg)
-        make_dh(quantize("dy1", dy_rounded[:], E5M2, replaces="slope0"), (2, 3), ("dh0", "dh1"))
+        lifted_back.update(lift(1, ("lifted_back0", "lifted_back1")))
+        silu_neg += [activate("silu_neg", c, ACT.Silu, tx_neg) for c in (2, 3)]
+        dh.update(make_dh(1, quantize("dy1", dy1_grouped[:], E5M2, replaces="slope0"), ("dh0", "dh1")))
+
         quantize_da(0)
-        early = (PLANE_ORDER[0], PLANE_ORDER[2])
-        early_banks = [make_dx("dx_early0", early[0], "da_turned0")]
-        for c in (2, 3):
-            slope[c] = times_bank(held(f"slope{c}", [P, F], F32)[:], c, lifted_back[c])
+        early_banks = [make_dx("dx_early0", EARLY_PLANES[0], "da_turned0")]
+        slope += [make_slope(c) for c in (2, 3)]
         da_turned = bank("da_turned23", replaces="da_turned1")
-        make_da(2, da_turned[:, half(0)])
-        make_da(3, da_turned[:, half(1)])
-        early_banks.append(make_dx("dx_early1", early[1], "a_turned2"))
+        for c in (2, 3):
+            make_da(c, da_turned[:, half(c % 2)])
+        early_banks.append(make_dx("dx_early1", EARLY_PLANES[1], "a_turned2"))
         dx_early = [fetch_dx("dx_first0", early_banks[0], 0, HALF, replaces="silu_neg3")]
         fetch_da(2, 2, da_turned[:])
         dx_early.append(fetch_dx("dx_first1", early_banks[1], 0, HALF, replaces="da3"))
-        scatter(early[0], 0, HALF, dx_early[0])
+        scatter(EARLY_PLANES[0], 0, HALF, dx_early[0])
         quantize_da(1)
-        scatter(early[1], 0, HALF, dx_early[1])
+        scatter(EARLY_PLANES[1], 0, HALF, dx_early[1])
 
-        done = {t: 0 if t == PLANE_ORDER[-1] else HALF for t in PLANE_ORDER}
+        done = {t: HALF if t in EARLY_PLANES else 0 for t in PLANE_ORDER}
         freed = ("lifted_back2", "lifted_back3", "dh2", "dh3")
-        split_plane = PLANE_ORDER[1]
-        pass_order = (split_plane, *early, PLANE_ORDER[-1])
-        dx_banks = {t: make_dx(f"dx{t}", t, replaces) for t, replaces in zip(pass_order, freed)}
+        dx_banks = {t: make_dx(f"dx{t}", t, replaces) for t, replaces in zip(PLANE_ORDER, freed)}
         first_plane, last_plane = PLANE_ORDER[0], PLANE_ORDER[-1]
-        scatter(split_plane, 0, HALF, fetch_dx("dx_first2", dx_banks[split_plane], 0, HALF))
-        dx_rest = {
-            t: fetch_dx(f"dx_rest{t}", dx_banks[t], done[t], N, "dx_first2" if t == split_plane else "")
-            for t in PLANE_ORDER[:-1]
-        }
+        dx_rest = {t: fetch_dx(f"dx_rest{t}", dx_banks[t], done[t], N) for t in PLANE_ORDER[:-1]}
 
         out_pairs = held("out_pairs", [P, 2, 2 * T], BF16, replaces="dy_pool0")
         out_lane = [out_pairs[:, t // 2, :].rearrange("p (n e) -> p n e", e=2)[:, :, t % 2] for t in range(LANES)]
@@ -396,20 +358,21 @@ def tile_attend_gdepth_sil_pl_kernel(tc, xT, dyT, w1, w2, cf, gt, tx, c1, offs, 
             if t != last_plane:
                 nc.scalar.copy(out=out_lane[t], in_=out_plane[t][:])
             if t == first_plane:
-                dx_rest[last_plane] = fetch_dx("dx_last", dx_banks[last_plane], done[last_plane], N, replaces=f"dx_rest{t}")
+                dx_rest[last_plane] = fetch_dx("dx_last", dx_banks[last_plane], 0, N, replaces=f"dx_rest{t}")
+
         out_grouped = held("out_grouped", [P, T * LANES], BF16)
-        woven = out_grouped[:].bitcast(U32).rearrange("p (g i u) -> p g u i", u=2, i=RUN)
-        pair_words = out_pairs[:].bitcast(U32).rearrange("p u (g i) -> p g u i", i=RUN)
-        quarters = [slice(k * T // 4, (k + 1) * T // 4) for k in range(4)]
-        runs = [slice(k * T // 4 // RUN, (k + 1) * T // 4 // RUN) for k in range(4)]
+        woven = out_grouped[:].bitcast(U32).rearrange("p (n i u) -> p n u i", u=2, i=RUN)
+        pair_words = out_pairs[:].bitcast(U32).rearrange("p u (n i) -> p n u i", i=RUN)
+        quarters = [slice(n * T // 4, (n + 1) * T // 4) for n in range(4)]
+        runs = [slice(cols.start // RUN, cols.stop // RUN) for cols in quarters]
         for cols in quarters[2:]:
             nc.scalar.copy(out=out_lane[last_plane][:, cols], in_=out_plane[last_plane][:, cols])
         for cols in quarters[:2]:
             nc.vector.tensor_copy(out=out_lane[last_plane][:, cols], in_=out_plane[last_plane][:, cols])
-        for cols in runs[2:]:
-            nc.scalar.copy(out=woven[:, cols], in_=pair_words[:, cols])
-        for cols in runs[:2]:
-            nc.vector.tensor_copy(out=woven[:, cols].bitcast(I32), in_=pair_words[:, cols].bitcast(I32))
+        for part in runs[2:]:
+            nc.scalar.copy(out=woven[:, part], in_=pair_words[:, part])
+        for part in runs[:2]:
+            nc.vector.tensor_copy(out=woven[:, part].bitcast(I32), in_=pair_words[:, part].bitcast(I32))
 
         out_codes = held("out_codes", [P, T], U32)
         out_scales = held("out_scales", [P, T], U8)

@@ -21,15 +21,12 @@ F = 512
 T = 1024
 N = 512
 CHUNKS = N // P
-GROUPS = F // P
 HALF = N // 2
 BAND = 16
 QUAD = 32
 RUN = 4
 LAST = P - 1
-UNIT_ROW = P - 2
-PLANE_ORDER = (2, 0, 1, 3)
-EARLY_PLANES = (2, 1)
+PLANE_ORDER = (2, 3, 1, 0)
 FLOPS = 3 * 2 * D * F * N
 
 
@@ -54,8 +51,8 @@ def tile_attend_gdepth_sil_pl_kernel(tc, xT, dyT, w1, w2, cf, gt, tx, c1, offs, 
         def half(h):
             return slice(h * HALF, (h + 1) * HALF)
 
-        def entries(first, last):
-            return offsets[:, first // BAND : last // BAND]
+        def entries(slots):
+            return offsets[:, slots.start // BAND : slots.stop // BAND]
 
         def quantize(name, values, fmt, replaces=""):
             width = values.shape[1] // LANES
@@ -75,10 +72,17 @@ def tile_attend_gdepth_sil_pl_kernel(tc, xT, dyT, w1, w2, cf, gt, tx, c1, offs, 
                 stop=True,
             )
 
+        def scalar_gather(out, window, slots):
+            nc.scalar.activation(out=out, in_=window[:].indirect(entries(slots)), func=ACT.Copy)
+
+        def vector_gather(out, window, slots):
+            nc.vector.tensor_copy(out=out, in_=window[:].indirect(entries(slots)))
+
         offsets = keep.tile([P, N // BAND], U16, name="offsets")
-        unit_rows = held("unit_rows", [P, 2, F // 2], F32)
         tx_pool = held("tx_pool", [P, T], F32)
         gt_pool = held("gt_pool", [P, T], F32)
+        cf_col = held("cf_col", [P, LANES], F32)
+        c1_col = held("c1_col", [P, LANES], F32)
         x_plane = [held(f"x_plane{t}", [P, T], F32) for t in range(LANES)]
         w1_raw = held("w1_raw", [P, LANES, F], F32)
         w2_raw = held("w2_raw", [P, LANES, F], F32)
@@ -90,289 +94,270 @@ def tile_attend_gdepth_sil_pl_kernel(tc, xT, dyT, w1, w2, cf, gt, tx, c1, offs, 
         nc.sync.dma_start(offsets[:], offs)
         nc.scalar.dma_start(out=tx_pool[LAST:, :], in_=tx[LAST:, :])
         nc.scalar.dma_start(out=gt_pool[LAST:, :], in_=gt[LAST:, :])
-        for v, vector in enumerate((cf, c1)):
-            nc.scalar.dma_start(out=unit_rows[UNIT_ROW:, v, :], in_=vector.rearrange("(g n) o -> g (n o)", g=2))
-        for t in (2, 0):
-            nc.sync.dma_start(out=x_plane[t][:], in_=x_rows[:, t, :])
+        nc.scalar.dma_start(out=cf_col[:], in_=cf.rearrange("(m t) o -> m (t o)", t=LANES))
+        nc.scalar.dma_start(out=c1_col[:], in_=c1.rearrange("(m t) o -> m (t o)", t=LANES))
         nc.sync.dma_start(out=w1_raw[:], in_=w1.rearrange("(p j) f -> p j f", j=LANES))
-        for t in (3, 1):
+        for t in range(LANES):
             nc.sync.dma_start(out=x_plane[t][:], in_=x_rows[:, t, :])
+        nc.sync.dma_start(out=w2_raw[:], in_=w2.rearrange("(p j) f -> p j f", j=LANES))
         for t in range(LANES):
             nc.sync.dma_start(out=dy_pool[t][:], in_=dy_rows[:, t, :])
-        nc.sync.dma_start(out=w2_raw[:], in_=w2.rearrange("(p j) f -> p j f", j=LANES))
         for t in PLANE_ORDER:
             nc.sync.dma_start(out=out_plane[t][:], in_=dy_rows[:, t, :])
 
         ident = held("ident", [P, P], F32)
+        seed = held("seed", [P, 1], F32)
+        zeros = held("zeros", [P, 1], F32)
+        nc.vector.memset(seed[:], 0.0)
+        nc.scalar.activation(out=zeros[:], in_=seed[:], func=ACT.Silu)
         nc.vector.memset(ident[:], 0.0)
         make_identity(nc, ident[:], nomemset=True)
-        for pool_tile in (tx_pool, gt_pool):
-            nc.vector.memset(pool_tile[:LAST, :], 0.0)
+        nc.vector.memset(tx_pool[:LAST, :], 0.0)
+        nc.vector.memset(gt_pool[:LAST, :], 0.0)
 
-        nc.scalar.activation(
-            out=unit_rows[:UNIT_ROW].rearrange("p v n -> p (v n)"), in_=tx_pool[:UNIT_ROW, :F], func=ACT.Silu
-        )
-
-        def slot_columns(name, pool_tile):
+        def slot_columns(name, pool_tile, gather):
             got = held(name + "_got", [P, N], F32)
-            nc.vector.tensor_copy(out=got[:], in_=pool_tile[:].indirect(offsets[:]))
+            gather(got[:], pool_tile, slice(0, N))
             turned = bank(name + "_turned")
             for c in range(CHUNKS):
                 nc.tensor.transpose(turned[:, block(c)], got[:, block(c)], ident[:])
             return turned[:].rearrange("p (c r) -> p c r", r=P)[:, :, LAST]
 
-        tx_cols = slot_columns("tx", tx_pool)
-        gt_cols = slot_columns("gt", gt_pool)
+        tx_cols = slot_columns("tx", tx_pool, vector_gather)
+        gt_cols = slot_columns("gt", gt_pool, scalar_gather)
+        tx_neg = held("tx_neg", [P, CHUNKS], F32)
+        tx_half = held("tx_half", [P, CHUNKS], F32)
+        nc.vector.tensor_scalar(out=tx_neg[:], in0=tx_cols, scalar1=-1.0, scalar2=zeros[:], op0=ALU.mult, op1=ALU.add)
+        nc.vector.tensor_scalar(out=tx_half[:], in0=tx_cols, scalar1=0.5, scalar2=None, op0=ALU.mult)
 
-        x_grouped = held("x_grouped", [P, N * LANES], BF16)
-        x_lanes = x_grouped[:].rearrange("p (i t) -> p i t", t=LANES)
-        x_rounded = {t: held(f"x_rounded{t}", [P, T], BF16) for t in (2, 3)}
-        nc.scalar.activation(out=x_rounded[2][:], in_=x_plane[2][:], func=ACT.Copy)
-        nc.scalar.activation(out=x_lanes[:, :, 2], in_=x_rounded[2][:].indirect(offsets[:]), func=ACT.Copy)
-        nc.vector.tensor_copy(out=x_lanes[:, :, 0], in_=x_plane[0][:].indirect(offsets[:]))
+        def unit_row(name, column):
+            row = bank(name)
+            places = row[:].rearrange("p (u m e) -> p u e m", u=2, e=2)
+            for t in range(LANES):
+                nc.tensor.transpose(places[:, t // 2, t % 2, :], column[:, t : t + 1].to_broadcast([P, P]), ident[:])
+            return row
 
-        factors = held("factors", [P, 3, CHUNKS], F32, replaces="x_rounded2")
-        tx_neg, tx_half, tx_neg_half = (factors[:, n, :] for n in range(3))
-        slot_factor = held("slot_factor", [P, CHUNKS], F32)
-        nc.scalar.activation(out=tx_neg[:], in_=tx_cols, func=ACT.Copy, scale=-1.0)
-        nc.scalar.activation(out=tx_half[:], in_=tx_cols, func=ACT.Copy, scale=0.5)
-        nc.scalar.activation(out=tx_neg_half[:], in_=tx_cols, func=ACT.Copy, scale=-0.5)
-        for c in range(CHUNKS):
-            nc.scalar.activation(
-                out=slot_factor[:, c : c + 1], in_=gt_cols[:, c : c + 1], func=ACT.Copy, scale=tx_neg_half[:, c : c + 1]
-            )
 
-        def unit_columns(name, rows):
-            ordered = held(name + "_ordered", [P, F // 2], F32)
-            nc.scalar.copy(
-                out=ordered[:].rearrange("p (u m e) -> p u m e", u=2, e=2),
-                in_=rows.rearrange("p (m u e) -> p u m e", u=2, e=2),
-            )
-            turned = bank(name + "_turned")
-            for u in range(2):
-                nc.tensor.transpose(turned[:, block(u)], ordered[:, block(u)], ident[:])
-            return turned[:, : 2 * P].rearrange("p (u r) -> p u r", u=2)[:, :, UNIT_ROW:]
-
-        cf_col = held("cf_col", [P, GROUPS], F32)
-        c_col = held("c_col", [P, GROUPS], F32)
-        nc.scalar.copy(out=cf_col[:].rearrange("p (u g) -> p u g", u=2), in_=unit_columns("cf", unit_rows[:, 0, :]))
-        c1_cols = unit_columns("c1", unit_rows[:, 1, :])
-        for k in range(GROUPS):
-            nc.scalar.activation(
-                out=c_col[:, k : k + 1], in_=c1_cols[:, k // 2, k % 2 : k % 2 + 1], func=ACT.Copy, scale=cf_col[:, k : k + 1]
-            )
-
-        def round_weights(name, raw):
-            grouped = held(name, [P, F * LANES], BF16)
+        def round_weights(name, raw, replaces):
+            grouped = held(name, [P, F * LANES], BF16, replaces)
             nc.vector.tensor_copy(
                 out=grouped[:].rearrange("p (u m e j) -> p m j u e", u=2, e=2, j=LANES),
                 in_=raw[:].rearrange("p j (m u e) -> p m j u e", u=2, e=2),
             )
             return grouped
 
-        w1_grouped = round_weights("w1_grouped", w1_raw)
-        nc.vector.tensor_copy(out=x_rounded[3][:], in_=x_plane[3][:])
-        w1_mx = quantize("w1", w1_grouped[:], E4M3)
-        nc.scalar.activation(out=x_lanes[:, :, 3], in_=x_rounded[3][:].indirect(offsets[:]), func=ACT.Copy)
-        for h in range(2):
-            window = x_plane[1][:].indirect(entries(h * HALF, (h + 1) * HALF))
-            nc.vector.tensor_copy(out=x_lanes[:, half(h), 1], in_=window)
-        x_mx = [quantize(f"x{h}", x_grouped[:, h * HALF * LANES : (h + 1) * HALF * LANES], E4M3) for h in range(2)]
-
-        w1t_grouped = held("w1t_grouped", [P, D * LANES], BF16, replaces="x_plane3")
-        w1t_pairs = w1t_grouped[:].rearrange("p (s b n i t) -> p s n t i b", s=2, b=2, i=2, t=LANES)
-        w1_words = w1_grouped[:].bitcast(F32).rearrange("p (u m e s) -> p s u e m", u=2, e=2, s=2)
-        for s, replaces in enumerate(("", "tx_turned")):
-            turned = bank(f"w1_turned{s}", replaces)
-            for t in range(LANES):
-                nc.tensor.transpose(turned[:, block(t)], w1_words[:, s, t // 2, t % 2, :], ident[:])
-            nc.scalar.copy(
-                out=w1t_pairs[:, s], in_=turned[:].bitcast(BF16).rearrange("p (t n i b) -> p n t i b", t=LANES, i=2, b=2)
-            )
-
-        def groups_of(banks):
-            return [banks[k // 2][:, half(k % 2)] for k in range(GROUPS)]
-
-        def scale_groups(name, groups, func, column, with_bias):
-            scaled = held(name, [P, GROUPS, HALF], F32)
-            for k in range(GROUPS):
-                extra = {"bias": column[:, k : k + 1]} if with_bias else {}
-                nc.scalar.activation(out=scaled[:, k, :], in_=groups[k], func=func, scale=column[:, k : k + 1], **extra)
-            return scaled
-
-        def turn_to_slots(name, scaled, h, replaced):
-            turned = {}
-            for c, replaces in zip((2 * h, 2 * h + 1), replaced):
-                turned[c] = bank(f"{name}{c}", replaces)
-                for k in range(GROUPS):
-                    nc.tensor.transpose(turned[c][:, block(k)], scaled[:, k, block(c % 2)], ident[:])
-            return turned
-
-        def first_product(h, replaced, replaced_turned):
-            groups = groups_of([bank(f"a{h}{u}", replaces) for u, replaces in enumerate(replaced)])
-            for k in range(GROUPS):
-                product(groups[k], w1_mx, E4M3, block(k), x_mx[h], E4M3)
-            return turn_to_slots("a_turned", scale_groups(f"a_scaled{h}", groups, ACT.Copy, cf_col, False), h, replaced_turned)
-
-        def activate(name, c, func, scale):
-            result = held(f"{name}{c}", [P, F], F32)
-            nc.scalar.activation(out=result[:], in_=a_turned[c][:], func=func, scale=scale[:, c : c + 1])
-            return result
-
-        def turn_tanh(h, replaced):
-            groups = groups_of([bank(f"tanh_turned{2 * h + u}", replaces) for u, replaces in enumerate(replaced)])
-            for k in range(GROUPS):
-                for e in range(2):
-                    nc.tensor.transpose(groups[k][:, block(e)], tanh_half[2 * h + e][:, block(k)], ident[:])
-            return groups
-
-        def lift(h, replaced):
-            lifted = scale_groups(f"lifted{h}", tanh_groups[h], ACT.Identity, c_col, True)
-            return turn_to_slots("lifted_back", lifted, h, replaced)
-
-        a_turned = first_product(0, ("", ""), ("gt_turned", "w1_turned0"))
-        a_turned.update(first_product(1, ("", "c1_turned"), ("w1_turned1", "cf_turned")))
-        tanh_half = [activate("tanh_half", c, ACT.Tanh, tx_half) for c in range(CHUNKS)]
-        tanh_groups = [turn_tanh(h, (f"a{h}0", f"a{h}1")) for h in range(2)]
-        lifted_back = lift(0, ("tanh_turned0", "tanh_turned1"))
-        silu_neg = [activate("silu_neg", c, ACT.Silu, tx_neg) for c in (0, 1)]
-
-        dy_got = held("dy_got", [P, LANES, N], F32)
-        for t in range(LANES - 1):
-            nc.vector.tensor_copy(out=dy_got[:, t, :], in_=dy_pool[t][:].indirect(offsets[:]))
-        for h in range(2):
-            window = dy_pool[LANES - 1][:].indirect(entries(h * HALF, (h + 1) * HALF))
-            nc.vector.tensor_copy(out=dy_got[:, LANES - 1, half(h)], in_=window)
-        dy0_grouped = held("dy0_grouped", [P, HALF * LANES], BF16)
+        w1_rounded = held("w1_rounded", [P, LANES, F], BF16)
         nc.vector.tensor_copy(
-            out=dy0_grouped[:].rearrange("p (n i t) -> p n t i", i=RUN, t=LANES),
-            in_=dy_got[:, :, half(0)].rearrange("p t (n i) -> p n t i", i=RUN),
+            out=w1_rounded[:].rearrange("p j (u m e) -> p j m u e", u=2, e=2),
+            in_=w1_raw[:].rearrange("p j (m u e) -> p j m u e", u=2, e=2),
         )
-        w2_grouped = round_weights("w2_grouped", w2_raw)
+        w1_grouped = held("w1_grouped", [P, F * LANES], BF16)
+        nc.vector.tensor_copy(
+            out=w1_grouped[:].rearrange("p (n i t) -> p n t i", i=RUN, t=LANES),
+            in_=w1_rounded[:].rearrange("p t (n i) -> p n t i", i=RUN),
+        )
+        w1_mx = quantize("w1", w1_grouped[:], E4M3)
+        x_got = held("x_got", [P, LANES, N], BF16)
+        scalar_gather(x_got[:, 0, :], x_plane[0], slice(0, N))
+        w1t_grouped = held("w1t_grouped", [P, D * LANES], BF16)
+        w1t_words = w1t_grouped[:].bitcast(F32).rearrange("p (s n i u) -> p s n u i", s=2, u=2, i=RUN)
+        w1_words = w1_rounded[:].rearrange("p j f -> p (j f)").bitcast(F32).rearrange("p (j u m) -> p j u m", j=LANES, u=2)
+        for s in range(2):
+            turned = bank(f"w1_turned{s}")
+            for u in range(2):
+                for b in range(2):
+                    nc.tensor.transpose(turned[:, block(2 * u + b)], w1_words[:, 2 * s + b, u, :], ident[:])
+            nc.scalar.copy(out=w1t_words[:, s], in_=turned[:].rearrange("p (u n i) -> p n u i", u=2, i=RUN))
+        slot_factor = held("slot_factor", [P, CHUNKS], F32, replaces="w1_raw")
+        nc.vector.scalar_tensor_tensor(
+            out=slot_factor[:], in0=gt_cols, scalar=0.5, in1=tx_neg[:], op0=ALU.mult, op1=ALU.mult
+        )
+        c_col = held("c_col", [P, LANES], F32)
+        nc.vector.tensor_tensor(out=c_col[:], in0=cf_col[:], in1=c1_col[:], op=ALU.mult)
+        cf_row = held("cf_row", [P, F], F32)
+        nc.scalar.copy(out=cf_row[:], in_=unit_row("cf_turned", cf_col)[:])
+        c_row = unit_row("c_row", c_col)
 
-        da_mx = (held("da_codes", [P, N], U32, replaces="tanh_half1"), held("da_scales", [P, N], U8))
-        dy0_mx = tuple(part[:, half(1)] for part in da_mx)
-        nc.vector.quantize_mx(out=dy0_mx[0].bitcast(E5M2), scales=dy0_mx[1], in_=dy0_grouped[:])
-        w2_mx = quantize("w2", w2_grouped[:], E4M3)
-
-        def make_dh(h, dy_mx, replaced):
-            banks = {}
-            for c, replaces in zip((2 * h, 2 * h + 1), replaced):
-                banks[c] = bank(f"dh{c}", replaces)
-                product(banks[c][:], dy_mx, E5M2, block(c % 2), w2_mx, E4M3)
-            return banks
-
-        dh = make_dh(0, dy0_mx, ("a_turned0", "a_turned1"))
-
-        da_grouped = held("da_grouped", [P, N * LANES], BF16)
-        da_words = da_grouped[:].bitcast(F32).rearrange("p (c n i u) -> p c n u i", c=CHUNKS, u=2, i=RUN)
-
-        def make_slope(c):
-            result = held(f"slope{c}", [P, F], F32)
-            nc.vector.scalar_tensor_tensor(
-                out=result[:], in0=silu_neg[c][:], scalar=-1.0, in1=lifted_back[c][:], op0=ALU.add, op1=ALU.mult
+        def interleave(copy, name, planes, replaces=""):
+            grouped = held(name, [P, planes.shape[2] * LANES], BF16, replaces)
+            copy(
+                out=grouped[:].rearrange("p (n i t) -> p n t i", i=RUN, t=LANES),
+                in_=planes.rearrange("p t (n i) -> p n t i", i=RUN),
             )
-            return result
+            return grouped
 
-        def make_da(c, turned):
+        vector_gather(x_got[:, 1, :], x_plane[1], slice(0, N))
+        scalar_gather(x_got[:, 2, :], x_plane[2], slice(0, N))
+        vector_gather(x_got[:, 3, half(0)], x_plane[3], half(0))
+        scalar_gather(x_got[:, 3, half(1)], x_plane[3], half(1))
+        x_grouped = [
+            interleave(copy, f"x_grouped{h}", x_got[:, :, half(h)])
+            for h, copy in enumerate((nc.vector.tensor_copy, nc.scalar.copy))
+        ]
+        x_mx = [quantize(f"x{h}", x_grouped[h][:], E4M3) for h in range(2)]
+        w1t_mx = quantize("w1t", w1t_grouped[:], E4M3, replaces="x_grouped0")
+
+        scaled, tanh_half, silu_neg, lifted, slope, dh, da_turned, da_grouped, dx = ({} for n in range(9))
+
+        def first_product(c, replaces):
+            a = bank(f"a{c}", replaces)
+            product(a[:], x_mx[c // 2], E4M3, block(c % 2), w1_mx, E4M3)
+            return a
+
+        def scale(c, a, replaces=""):
+            scaled[c] = held(f"scaled{c}", [P, F], F32, replaces)
+            nc.vector.tensor_tensor(out=scaled[c][:], in0=a[:], in1=cf_row[:], op=ALU.mult)
+
+        def tanh(c, replaces=""):
+            tanh_half[c] = held(f"tanh_half{c}", [P, F], F32, replaces)
+            nc.scalar.activation(out=tanh_half[c][:], in_=scaled[c][:], func=ACT.Tanh, scale=tx_half[:, c : c + 1])
+
+        def silu(c, replaces=""):
+            silu_neg[c] = held(f"silu_neg{c}", [P, F], F32, replaces)
+            nc.scalar.activation(out=silu_neg[c][:], in_=scaled[c][:], func=ACT.Silu, scale=tx_neg[:, c : c + 1])
+
+        def lift(c, replaces=""):
+            lifted[c] = held(f"lifted{c}", [P, F], F32, replaces)
+            nc.vector.scalar_tensor_tensor(
+                out=lifted[c][:], in0=tanh_half[c][:], scalar=1.0, in1=c_row[:], op0=ALU.add, op1=ALU.mult
+            )
+
+        def make_slope(c, replaces=""):
+            slope[c] = held(f"slope{c}", [P, F], F32, replaces)
+            nc.vector.scalar_tensor_tensor(
+                out=slope[c][:], in0=silu_neg[c][:], scalar=-1.0, in1=lifted[c][:], op0=ALU.add, op1=ALU.mult
+            )
+
+        def make_dh(c, dy_mx, cols, replaces):
+            dh[c] = bank(f"dh{c}", replaces)
+            product(dh[c][:], dy_mx, E5M2, cols, w2_mx, E4M3)
+
+        def make_da(c, replaces):
             da = held(f"da{c}", [P, F], BF16)
             nc.vector.scalar_tensor_tensor(
                 out=da[:], in0=dh[c][:], scalar=slot_factor[:, c : c + 1], in1=slope[c][:], op0=ALU.mult, op1=ALU.mult
             )
+            da_turned[c] = bank(f"da_turned{c}", replaces)
             for u in range(2):
-                nc.tensor.transpose(turned[:, block(u)], da[:].bitcast(F32)[:, block(u)], ident[:])
+                nc.tensor.transpose(da_turned[c][:, block(u)], da[:].bitcast(F32)[:, block(u)], ident[:])
 
-        def fetch_da(first, count, turned):
-            nc.scalar.copy(
-                out=da_words[:, first : first + count],
-                in_=turned.rearrange("p (c u n i) -> p c n u i", c=count, u=2, i=RUN),
+        def fetch_da(c, copy):
+            da_grouped[c] = held(f"da_grouped{c}", [P, P * LANES], BF16)
+            copy(
+                out=da_grouped[c][:].bitcast(F32).rearrange("p (n i u) -> p n u i", u=2, i=RUN),
+                in_=da_turned[c][:, half(0)].rearrange("p (u n i) -> p n u i", u=2, i=RUN),
             )
 
-        def quantize_da(h):
-            nc.vector.quantize_mx(
-                out=da_mx[0][:, half(h)].bitcast(E5M2),
-                scales=da_mx[1][:, half(h)],
-                in_=da_grouped[:, h * HALF * LANES : (h + 1) * HALF * LANES],
-            )
+        def make_dx(c, replaces):
+            da_mx = quantize(f"da{c}", da_grouped[c][:], E5M2)
+            dx[c] = bank(f"dx{c}", replaces)
+            for t in range(LANES):
+                product(dx[c][:, block(t)], w1t_mx, E4M3, block(t), da_mx, E5M2)
 
-        def make_dx(name, t, replaces):
-            dx_bank = bank(name, replaces)
-            product(dx_bank[:], w1t_mx, E4M3, block(t), da_mx, E5M2)
-            return dx_bank
+        new_cols = held("new_cols", [P, LANES, N], F32)
 
-        def fetch_dx(name, dx_bank, first, last, replaces=""):
-            dx = held(name, [P, last - first], F32, replaces)
-            nc.scalar.copy(out=dx[:], in_=dx_bank[:, first:last])
-            return dx
-
-        def scatter(t, first, last, dx):
+        def add_dy(c):
             nc.vector.tensor_tensor(
-                out=out_plane[t][:].indirect(entries(first, last)), in0=dx[:], in1=dy_got[:, t, first:last], op=ALU.add
+                out=new_cols[:, :, block(c)],
+                in0=dx[c][:].rearrange("p (t i) -> p t i", t=LANES),
+                in1=dy_got[c // 2][:, :, block(c % 2)],
+                op=ALU.add,
             )
 
-        w1t_mx = quantize("w1t", w1t_grouped[:], E4M3, replaces="w2_raw")
-        slope = [make_slope(c) for c in (0, 1)]
-        dy1_grouped = held("dy1_grouped", [P, HALF * LANES], BF16, replaces="w1t_grouped")
-        nc.gpsimd.tensor_scalar(
-            out=dy1_grouped[:].rearrange("p (i t) -> p i t", t=LANES),
-            in0=dy_got[:, :, half(1)].rearrange("p t i -> p i t"),
-            scalar1=1.0,
-            scalar2=0.0,
-            op0=ALU.mult,
-            op1=ALU.add,
-        )
-        for c in (0, 1):
-            da_turned = bank(f"da_turned{c}", f"tanh_turned{2 + c}")
-            make_da(c, da_turned[:, half(0)])
-            fetch_da(c, 1, da_turned[:, half(0)])
-        lifted_back.update(lift(1, ("lifted_back0", "lifted_back1")))
-        silu_neg += [activate("silu_neg", c, ACT.Silu, tx_neg) for c in (2, 3)]
-        dh.update(make_dh(1, quantize("dy1", dy1_grouped[:], E5M2, replaces="slope0"), ("dh0", "dh1")))
+        def scalar_scatter(t, slots):
+            nc.scalar.activation(out=out_plane[t][:].indirect(entries(slots)), in_=new_cols[:, t, slots], func=ACT.Copy)
 
-        quantize_da(0)
-        early_banks = [make_dx("dx_early0", EARLY_PLANES[0], "da_turned0")]
-        slope += [make_slope(c) for c in (2, 3)]
-        da_turned = bank("da_turned23", replaces="da_turned1")
-        for c in (2, 3):
-            make_da(c, da_turned[:, half(c % 2)])
-        early_banks.append(make_dx("dx_early1", EARLY_PLANES[1], "a_turned2"))
-        dx_early = [fetch_dx("dx_first0", early_banks[0], 0, HALF, replaces="silu_neg3")]
-        fetch_da(2, 2, da_turned[:])
-        dx_early.append(fetch_dx("dx_first1", early_banks[1], 0, HALF, replaces="da3"))
-        scatter(EARLY_PLANES[0], 0, HALF, dx_early[0])
-        quantize_da(1)
-        scatter(EARLY_PLANES[1], 0, HALF, dx_early[1])
+        def vector_scatter(t, slots):
+            nc.vector.tensor_copy(out=out_plane[t][:].indirect(entries(slots)), in_=new_cols[:, t, slots])
 
-        done = {t: HALF if t in EARLY_PLANES else 0 for t in PLANE_ORDER}
-        freed = ("lifted_back2", "lifted_back3", "dh2", "dh3")
-        dx_banks = {t: make_dx(f"dx{t}", t, replaces) for t, replaces in zip(PLANE_ORDER, freed)}
-        first_plane, last_plane = PLANE_ORDER[0], PLANE_ORDER[-1]
-        dx_rest = {t: fetch_dx(f"dx_rest{t}", dx_banks[t], done[t], N) for t in PLANE_ORDER[:-1]}
+        a = [first_product(c, replaces) for c, replaces in enumerate(("", "", "cf_turned", "tx_turned"))]
+        dy_got = [held("dy_got0", [P, LANES, HALF], F32)]
+        scale(0, a[0])
+        scale(1, a[1])
+        w2_grouped = round_weights("w2_grouped", w2_raw, "x0_codes")
+        tanh(0)
+        silu(0)
+        for t in range(LANES - 1):
+            scalar_gather(dy_got[0][:, t, :], dy_pool[t], half(0))
+        for c in range(2):
+            scalar_gather(dy_got[0][:, LANES - 1, block(c)], dy_pool[LANES - 1], block(c))
+        tanh(1)
+        silu(1)
+        lift(0)
+        w2_mx = quantize("w2", w2_grouped[:], E4M3)
+        make_slope(0)
+        dy_grouped = [interleave(nc.vector.tensor_copy, f"dy_grouped{c}", dy_got[0][:, :, block(c)]) for c in range(2)]
+        dy_mx = [quantize(f"dy{c}", dy_grouped[c][:], E5M2) for c in range(2)]
+        make_dh(0, dy_mx[0], block(0), "gt_turned")
+        make_dh(1, dy_mx[1], block(0), "w1_turned0")
+        lift(1)
+        make_slope(1)
+        dy_got.append(held("dy_got1", [P, LANES, HALF], F32, replaces="scaled1"))
+        make_da(0, "w1_turned1")
+        make_da(1, "a0")
+        fetch_da(0, nc.scalar.copy)
+        fetch_da(1, nc.scalar.copy)
+        make_dx(0, "a1")
+        make_dx(1, "dh0")
+        scale(2, a[2], "dy_grouped0")
+        scale(3, a[3], "dy_grouped1")
+        tanh(2)
+        silu(2)
+        for t in range(LANES):
+            scalar_gather(dy_got[1][:, t, :], dy_pool[t], half(1))
+        dy_late = quantize("dy_late", interleave(nc.scalar.copy, "dy_grouped_late", dy_got[1][:])[:], E5M2)
+        tanh(3)
+        silu(3)
+        make_dh(2, dy_late, block(0), "a2")
+        make_dh(3, dy_late, block(1), "a3")
+        add_dy(0)
+        lift(2)
+        make_slope(2)
+        make_da(2, "dh1")
+        fetch_da(2, nc.vector.tensor_copy)
+        make_dx(2, "da_turned0")
+        lift(3)
+        add_dy(1)
+        make_slope(3)
+        make_da(3, "da_turned1")
+        fetch_da(3, nc.vector.tensor_copy)
+        make_dx(3, "dx0")
+        add_dy(2)
+        add_dy(3)
 
-        out_pairs = held("out_pairs", [P, 2, 2 * T], BF16, replaces="dy_pool0")
-        out_lane = [out_pairs[:, t // 2, :].rearrange("p (n e) -> p n e", e=2)[:, :, t % 2] for t in range(LANES)]
         out_rows = out_0.rearrange("(p t) n -> p t n", t=LANES)
+        for c in range(2):
+            for t in (2, 3):
+                scalar_scatter(t, block(c))
+        scalar_scatter(1, half(0))
+        vector_scatter(0, block(0))
+        vector_scatter(2, block(2))
+        scalar_scatter(3, block(2))
+        scalar_scatter(0, block(1))
+        vector_scatter(2, block(3))
+        scalar_scatter(3, block(3))
+        scalar_scatter(1, half(1))
+        scalar_scatter(0, half(1))
         for t in PLANE_ORDER:
-            scatter(t, done[t], N, dx_rest[t])
             nc.sync.dma_start(out=out_rows[:, t, :], in_=out_plane[t][:])
-            if t != last_plane:
-                nc.scalar.copy(out=out_lane[t], in_=out_plane[t][:])
-            if t == first_plane:
-                dx_rest[last_plane] = fetch_dx("dx_last", dx_banks[last_plane], 0, N, replaces=f"dx_rest{t}")
 
+        out_pairs = held("out_pairs", [P, 2, 2 * T], BF16)
+        out_lane = [out_pairs[:, t // 2, :].rearrange("p (n e) -> p n e", e=2)[:, :, t % 2] for t in range(LANES)]
         out_grouped = held("out_grouped", [P, T * LANES], BF16)
         woven = out_grouped[:].bitcast(U32).rearrange("p (n i u) -> p n u i", u=2, i=RUN)
         pair_words = out_pairs[:].bitcast(U32).rearrange("p u (n i) -> p n u i", i=RUN)
         quarters = [slice(n * T // 4, (n + 1) * T // 4) for n in range(4)]
         runs = [slice(cols.start // RUN, cols.stop // RUN) for cols in quarters]
-        for cols in quarters[2:]:
-            nc.scalar.copy(out=out_lane[last_plane][:, cols], in_=out_plane[last_plane][:, cols])
-        for cols in quarters[:2]:
-            nc.vector.tensor_copy(out=out_lane[last_plane][:, cols], in_=out_plane[last_plane][:, cols])
-        for part in runs[2:]:
-            nc.scalar.copy(out=woven[:, part], in_=pair_words[:, part])
+        split = 3 * T // 4
+        for t in PLANE_ORDER[:2]:
+            nc.vector.tensor_copy(out=out_lane[t], in_=out_plane[t][:])
+        for t in PLANE_ORDER[2:]:
+            nc.vector.tensor_copy(out=out_lane[t][:, :split], in_=out_plane[t][:, :split])
+            nc.scalar.copy(out=out_lane[t][:, split:], in_=out_plane[t][:, split:])
         for part in runs[:2]:
             nc.vector.tensor_copy(out=woven[:, part].bitcast(I32), in_=pair_words[:, part].bitcast(I32))
+        for part in runs[:1:-1]:
+            nc.scalar.copy(out=woven[:, part], in_=pair_words[:, part])
 
         out_codes = held("out_codes", [P, T], U32)
         out_scales = held("out_scales", [P, T], U8)

@@ -99,8 +99,9 @@ def tile_attend_gdepth_sil_pl_kernel(tc, xT, dyT, w1, w2, cf, gt, tx, c1, offs, 
         nc.sync.dma_start(out=w1_raw[:], in_=w1.rearrange("(p j) f -> p j f", j=LANES))
         for t in range(LANES):
             nc.sync.dma_start(out=x_plane[t][:], in_=x_rows[:, t, :])
+        nc.sync.dma_start(out=dy_pool[0][:], in_=dy_rows[:, 0, :])
         nc.sync.dma_start(out=w2_raw[:], in_=w2.rearrange("(p j) f -> p j f", j=LANES))
-        for t in range(LANES):
+        for t in range(1, LANES):
             nc.sync.dma_start(out=dy_pool[t][:], in_=dy_rows[:, t, :])
         for t in PLANE_ORDER:
             nc.sync.dma_start(out=out_plane[t][:], in_=dy_rows[:, t, :])
@@ -138,14 +139,6 @@ def tile_attend_gdepth_sil_pl_kernel(tc, xT, dyT, w1, w2, cf, gt, tx, c1, offs, 
             return row
 
 
-        def round_weights(name, raw, replaces):
-            grouped = held(name, [P, F * LANES], BF16, replaces)
-            nc.vector.tensor_copy(
-                out=grouped[:].rearrange("p (u m e j) -> p m j u e", u=2, e=2, j=LANES),
-                in_=raw[:].rearrange("p j (m u e) -> p m j u e", u=2, e=2),
-            )
-            return grouped
-
         w1_rounded = held("w1_rounded", [P, LANES, F], BF16)
         nc.vector.tensor_copy(
             out=w1_rounded[:].rearrange("p j (u m e) -> p j m u e", u=2, e=2),
@@ -157,8 +150,9 @@ def tile_attend_gdepth_sil_pl_kernel(tc, xT, dyT, w1, w2, cf, gt, tx, c1, offs, 
             in_=w1_rounded[:].rearrange("p t (n i) -> p n t i", i=RUN),
         )
         w1_mx = quantize("w1", w1_grouped[:], E4M3)
-        x_got = held("x_got", [P, LANES, N], BF16)
-        scalar_gather(x_got[:, 0, :], x_plane[0], slice(0, N))
+        x_got = [held(f"x_got{h}", [P, LANES, HALF], BF16) for h in range(2)]
+        for h in range(2):
+            scalar_gather(x_got[h][:, 0, :], x_plane[0], half(h))
         w1t_grouped = held("w1t_grouped", [P, D * LANES], BF16)
         w1t_words = w1t_grouped[:].bitcast(F32).rearrange("p (s n i u) -> p s n u i", s=2, u=2, i=RUN)
         w1_words = w1_rounded[:].rearrange("p j f -> p (j f)").bitcast(F32).rearrange("p (j u m) -> p j u m", j=LANES, u=2)
@@ -172,11 +166,6 @@ def tile_attend_gdepth_sil_pl_kernel(tc, xT, dyT, w1, w2, cf, gt, tx, c1, offs, 
         nc.vector.scalar_tensor_tensor(
             out=slot_factor[:], in0=gt_cols, scalar=0.5, in1=tx_neg[:], op0=ALU.mult, op1=ALU.mult
         )
-        c_col = held("c_col", [P, LANES], F32)
-        nc.vector.tensor_tensor(out=c_col[:], in0=cf_col[:], in1=c1_col[:], op=ALU.mult)
-        cf_row = held("cf_row", [P, F], F32)
-        nc.scalar.copy(out=cf_row[:], in_=unit_row("cf_turned", cf_col)[:])
-        c_row = unit_row("c_row", c_col)
 
         def interleave(copy, name, planes, replaces=""):
             grouped = held(name, [P, planes.shape[2] * LANES], BF16, replaces)
@@ -186,46 +175,57 @@ def tile_attend_gdepth_sil_pl_kernel(tc, xT, dyT, w1, w2, cf, gt, tx, c1, offs, 
             )
             return grouped
 
-        vector_gather(x_got[:, 1, :], x_plane[1], slice(0, N))
-        scalar_gather(x_got[:, 2, :], x_plane[2], slice(0, N))
-        vector_gather(x_got[:, 3, half(0)], x_plane[3], half(0))
-        scalar_gather(x_got[:, 3, half(1)], x_plane[3], half(1))
-        x_grouped = [
-            interleave(copy, f"x_grouped{h}", x_got[:, :, half(h)])
-            for h, copy in enumerate((nc.vector.tensor_copy, nc.scalar.copy))
-        ]
-        x_mx = [quantize(f"x{h}", x_grouped[h][:], E4M3) for h in range(2)]
-        w1t_mx = quantize("w1t", w1t_grouped[:], E4M3, replaces="x_grouped0")
+        for h in range(2):
+            vector_gather(x_got[h][:, 1, :], x_plane[1], half(h))
+        for h in range(2):
+            scalar_gather(x_got[h][:, 2, :], x_plane[2], half(h))
+        for c in range(2):
+            vector_gather(x_got[0][:, 3, block(c)], x_plane[3], block(c))
+        scalar_gather(x_got[1][:, 3, :], x_plane[3], half(1))
+        x_grouped = [interleave(nc.vector.tensor_copy, f"x_grouped{c}", x_got[0][:, :, block(c)]) for c in range(2)]
+        x_grouped.append(interleave(nc.scalar.copy, "x_grouped2", x_got[1][:]))
+        x_mx = [quantize(f"x{n}", x_grouped[n][:], E4M3) for n in range(3)]
+        c_col = held("c_col", [P, LANES], F32, replaces="x_plane1")
+        nc.vector.tensor_tensor(out=c_col[:], in0=cf_col[:], in1=c1_col[:], op=ALU.mult)
+        cf_row = held("cf_row", [P, F], F32, replaces="x_plane3")
+        nc.scalar.copy(out=cf_row[:], in_=unit_row("cf_turned", cf_col)[:])
+        c_row = unit_row("c_row", c_col)
+        w1t_mx = quantize("w1t", w1t_grouped[:], E4M3, replaces="x_grouped1")
 
         scaled, tanh_half, silu_neg, lifted, slope, dh, da_turned, da_grouped, dx = ({} for n in range(9))
 
         def first_product(c, replaces):
             a = bank(f"a{c}", replaces)
-            product(a[:], x_mx[c // 2], E4M3, block(c % 2), w1_mx, E4M3)
+            product(a[:], x_mx[min(c, 2)], E4M3, block(max(c - 2, 0)), w1_mx, E4M3)
             return a
 
         def scale(c, a, replaces=""):
             scaled[c] = held(f"scaled{c}", [P, F], F32, replaces)
             nc.vector.tensor_tensor(out=scaled[c][:], in0=a[:], in1=cf_row[:], op=ALU.mult)
 
-        def tanh(c, replaces=""):
-            tanh_half[c] = held(f"tanh_half{c}", [P, F], F32, replaces)
-            nc.scalar.activation(out=tanh_half[c][:], in_=scaled[c][:], func=ACT.Tanh, scale=tx_half[:, c : c + 1])
+        def tanh(c, out):
+            tanh_half[c] = out
+            nc.scalar.activation(out=out, in_=scaled[c][:], func=ACT.Tanh, scale=tx_half[:, c : c + 1])
 
-        def silu(c, replaces=""):
-            silu_neg[c] = held(f"silu_neg{c}", [P, F], F32, replaces)
-            nc.scalar.activation(out=silu_neg[c][:], in_=scaled[c][:], func=ACT.Silu, scale=tx_neg[:, c : c + 1])
+        def silu(c, out):
+            silu_neg[c] = out
+            nc.scalar.activation(out=out, in_=scaled[c][:], func=ACT.Silu, scale=tx_neg[:, c : c + 1])
+
+        def activate(c, replaces=""):
+            both = held(f"activated{c}", [P, 2, F], F32, replaces)
+            tanh(c, both[:, 0, :])
+            silu(c, both[:, 1, :])
 
         def lift(c, replaces=""):
             lifted[c] = held(f"lifted{c}", [P, F], F32, replaces)
             nc.vector.scalar_tensor_tensor(
-                out=lifted[c][:], in0=tanh_half[c][:], scalar=1.0, in1=c_row[:], op0=ALU.add, op1=ALU.mult
+                out=lifted[c][:], in0=tanh_half[c], scalar=1.0, in1=c_row[:], op0=ALU.add, op1=ALU.mult
             )
 
         def make_slope(c, replaces=""):
             slope[c] = held(f"slope{c}", [P, F], F32, replaces)
             nc.vector.scalar_tensor_tensor(
-                out=slope[c][:], in0=silu_neg[c][:], scalar=-1.0, in1=lifted[c][:], op0=ALU.add, op1=ALU.mult
+                out=slope[c][:], in0=silu_neg[c], scalar=-1.0, in1=lifted[c][:], op0=ALU.add, op1=ALU.mult
             )
 
         def make_dh(c, dy_mx, cols, replaces):
@@ -254,90 +254,98 @@ def tile_attend_gdepth_sil_pl_kernel(tc, xT, dyT, w1, w2, cf, gt, tx, c1, offs, 
             for t in range(LANES):
                 product(dx[c][:, block(t)], w1t_mx, E4M3, block(t), da_mx, E5M2)
 
-        new_cols = held("new_cols", [P, LANES, N], F32)
+        new_cols = {}
 
-        def add_dy(c):
+        def add_dy(c, first=0, last=LANES, replaces=""):
+            sums = held(f"new_cols{c}{first}", [P, last - first, P], F32, replaces)
             nc.vector.tensor_tensor(
-                out=new_cols[:, :, block(c)],
-                in0=dx[c][:].rearrange("p (t i) -> p t i", t=LANES),
-                in1=dy_got[c // 2][:, :, block(c % 2)],
+                out=sums[:],
+                in0=dx[c][:].rearrange("p (t i) -> p t i", t=LANES)[:, first:last, :],
+                in1=dy_got[c // 2][:, first:last, block(c % 2)],
                 op=ALU.add,
             )
+            for t in range(first, last):
+                new_cols[t, c] = sums[:, t - first, :]
 
-        def scalar_scatter(t, slots):
-            nc.scalar.activation(out=out_plane[t][:].indirect(entries(slots)), in_=new_cols[:, t, slots], func=ACT.Copy)
+        def scalar_scatter(t, c):
+            nc.scalar.activation(out=out_plane[t][:].indirect(entries(block(c))), in_=new_cols[t, c], func=ACT.Copy)
 
-        def vector_scatter(t, slots):
-            nc.vector.tensor_copy(out=out_plane[t][:].indirect(entries(slots)), in_=new_cols[:, t, slots])
+        def vector_scatter(t, c):
+            nc.vector.tensor_copy(out=out_plane[t][:].indirect(entries(block(c))), in_=new_cols[t, c])
 
         a = [first_product(c, replaces) for c, replaces in enumerate(("", "", "cf_turned", "tx_turned"))]
         dy_got = [held("dy_got0", [P, LANES, HALF], F32)]
-        scale(0, a[0])
-        scale(1, a[1])
-        w2_grouped = round_weights("w2_grouped", w2_raw, "x0_codes")
-        tanh(0)
-        silu(0)
+        for c in range(CHUNKS):
+            scale(c, a[c])
+        w2_grouped = held("w2_grouped", [P, F * LANES], BF16, replaces="x_grouped2")
+        for u in range(2):
+            nc.gpsimd.tensor_scalar(
+                out=w2_grouped[:].rearrange("p (u m e j) -> p u m e j", u=2, e=2, j=LANES)[:, u],
+                in0=w2_raw[:].rearrange("p j (m u e) -> p u m e j", u=2, e=2)[:, u],
+                scalar1=1.0,
+                scalar2=0.0,
+                op0=ALU.mult,
+                op1=ALU.add,
+            )
+        activate(0)
+        tanh(1, held("tanh_half1", [P, F], F32)[:])
         for t in range(LANES - 1):
             scalar_gather(dy_got[0][:, t, :], dy_pool[t], half(0))
         for c in range(2):
             scalar_gather(dy_got[0][:, LANES - 1, block(c)], dy_pool[LANES - 1], block(c))
-        tanh(1)
-        silu(1)
-        lift(0)
-        w2_mx = quantize("w2", w2_grouped[:], E4M3)
-        make_slope(0)
         dy_grouped = [interleave(nc.vector.tensor_copy, f"dy_grouped{c}", dy_got[0][:, :, block(c)]) for c in range(2)]
         dy_mx = [quantize(f"dy{c}", dy_grouped[c][:], E5M2) for c in range(2)]
+        lift(0)
+        lift(1)
+        make_slope(0)
+        w2_mx = quantize("w2", w2_grouped[:], E4M3)
+        silu(1, held("silu_neg1", [P, F], F32, replaces="w2_grouped")[:])
         make_dh(0, dy_mx[0], block(0), "gt_turned")
         make_dh(1, dy_mx[1], block(0), "w1_turned0")
-        lift(1)
-        make_slope(1)
-        dy_got.append(held("dy_got1", [P, LANES, HALF], F32, replaces="scaled1"))
         make_da(0, "w1_turned1")
-        make_da(1, "a0")
-        fetch_da(0, nc.scalar.copy)
-        fetch_da(1, nc.scalar.copy)
+        fetch_da(0, nc.vector.tensor_copy)
         make_dx(0, "a1")
+        add_dy(0)
+        make_slope(1)
+        make_da(1, "a0")
+        fetch_da(1, nc.vector.tensor_copy)
         make_dx(1, "dh0")
-        scale(2, a[2], "dy_grouped0")
-        scale(3, a[3], "dy_grouped1")
-        tanh(2)
-        silu(2)
+        tanh(2, held("tanh_half2", [P, F], F32, replaces="scaled1")[:])
+        dy_got.append(held("dy_got1", [P, LANES, HALF], F32, replaces="dy_grouped1"))
         for t in range(LANES):
             scalar_gather(dy_got[1][:, t, :], dy_pool[t], half(1))
-        dy_late = quantize("dy_late", interleave(nc.scalar.copy, "dy_grouped_late", dy_got[1][:])[:], E5M2)
-        tanh(3)
-        silu(3)
+        silu(2, held("silu_neg2", [P, F], F32, replaces="dy_pool2")[:])
+        tanh(3, held("tanh_half3", [P, F], F32, replaces="dy_pool3")[:])
+        silu(3, held("silu_neg3", [P, F], F32, replaces="scaled2")[:])
+        dy_grouped_late = interleave(nc.vector.tensor_copy, "dy_grouped_late", dy_got[1][:], "da1")
+        dy_late = quantize("dy_late", dy_grouped_late[:], E5M2)
         make_dh(2, dy_late, block(0), "a2")
         make_dh(3, dy_late, block(1), "a3")
-        add_dy(0)
         lift(2)
-        make_slope(2)
+        make_slope(2, "da_grouped1")
         make_da(2, "dh1")
-        fetch_da(2, nc.vector.tensor_copy)
-        make_dx(2, "da_turned0")
-        lift(3)
-        add_dy(1)
+        lift(3, "dy_grouped_late")
         make_slope(3)
-        make_da(3, "da_turned1")
-        fetch_da(3, nc.vector.tensor_copy)
-        make_dx(3, "dx0")
+        add_dy(1, replaces="silu_neg3")
+        make_da(3, "da_turned0")
+        for c in (2, 3):
+            fetch_da(c, nc.vector.tensor_copy)
+        make_dx(2, "da_turned1")
+        make_dx(3, "c_row")
         add_dy(2)
         add_dy(3)
 
         out_rows = out_0.rearrange("(p t) n -> p t n", t=LANES)
-        for c in range(2):
-            for t in (2, 3):
-                scalar_scatter(t, block(c))
-        scalar_scatter(1, half(0))
-        vector_scatter(0, block(0))
-        vector_scatter(2, block(2))
-        scalar_scatter(3, block(2))
-        scalar_scatter(0, block(1))
-        vector_scatter(2, block(3))
-        scalar_scatter(3, block(3))
-        scalar_scatter(1, half(1))
-        scalar_scatter(0, half(1))
+        for t in PLANE_ORDER:
+            scalar_scatter(t, 0)
+        for t in PLANE_ORDER[:-1]:
+            scalar_scatter(t, 1)
+        vector_scatter(0, 1)
+        for c in (2, 3):
+            vector_scatter(2, c)
+        for t in PLANE_ORDER[1:]:
+            for c in (2, 3):
+                scalar_scatter(t, c)
         for t in PLANE_ORDER:
             nc.sync.dma_start(out=out_rows[:, t, :], in_=out_plane[t][:])
 

@@ -241,8 +241,8 @@ def tile_attend_gdepth_sil_pl_kernel(tc, xT, dyT, w1, w2, cf, gt, tx, c1, offs, 
             for u in range(2):
                 nc.tensor.transpose(da_turned[c][:, block(u)], da[:].bitcast(F32)[:, block(u)], ident[:])
 
-        def fetch_da(c, copy):
-            da_grouped[c] = held(f"da_grouped{c}", [P, P * LANES], BF16)
+        def fetch_da(c, copy, replaces=""):
+            da_grouped[c] = held(f"da_grouped{c}", [P, P * LANES], BF16, replaces)
             copy(
                 out=da_grouped[c][:].bitcast(F32).rearrange("p (n i u) -> p n u i", u=2, i=RUN),
                 in_=da_turned[c][:, half(0)].rearrange("p (u n i) -> p n u i", u=2, i=RUN),
@@ -275,63 +275,62 @@ def tile_attend_gdepth_sil_pl_kernel(tc, xT, dyT, w1, w2, cf, gt, tx, c1, offs, 
 
         a = [first_product(c, replaces) for c, replaces in enumerate(("", "", "cf_turned", "tx_turned"))]
         dy_got = [held("dy_got0", [P, LANES, HALF], F32)]
-        for c in range(CHUNKS):
-            scale(c, a[c])
-        w2_grouped = held("w2_grouped", [P, F * LANES], BF16, replaces="x_grouped2")
-        for u in range(2):
-            nc.gpsimd.tensor_scalar(
-                out=w2_grouped[:].rearrange("p (u m e j) -> p u m e j", u=2, e=2, j=LANES)[:, u],
-                in0=w2_raw[:].rearrange("p j (m u e) -> p u m e j", u=2, e=2)[:, u],
-                scalar1=1.0,
-                scalar2=0.0,
-                op0=ALU.mult,
-                op1=ALU.add,
-            )
+        scale(0, a[0])
+        scale(1, a[1])
+        w2_grouped = held("w2_grouped", [P, F * LANES], BF16, replaces="x1_codes")
+        nc.vector.tensor_copy(
+            out=w2_grouped[:].rearrange("p (u m e j) -> p m j u e", u=2, e=2, j=LANES),
+            in_=w2_raw[:].rearrange("p j (m u e) -> p m j u e", u=2, e=2),
+        )
         activate(0)
         tanh(1, held("tanh_half1", [P, F], F32)[:])
         for t in range(LANES - 1):
             scalar_gather(dy_got[0][:, t, :], dy_pool[t], half(0))
         for c in range(2):
             scalar_gather(dy_got[0][:, LANES - 1, block(c)], dy_pool[LANES - 1], block(c))
-        dy_grouped = [interleave(nc.vector.tensor_copy, f"dy_grouped{c}", dy_got[0][:, :, block(c)]) for c in range(2)]
-        dy_mx = [quantize(f"dy{c}", dy_grouped[c][:], E5M2) for c in range(2)]
         lift(0)
+        w2_mx = quantize("w2", w2_grouped[:], E4M3)
         lift(1)
         make_slope(0)
-        w2_mx = quantize("w2", w2_grouped[:], E4M3)
-        silu(1, held("silu_neg1", [P, F], F32, replaces="w2_grouped")[:])
+        dy_grouped = [
+            interleave(nc.vector.tensor_copy, f"dy_grouped{c}", dy_got[0][:, :, block(c)], replaces)
+            for c, replaces in enumerate(("tanh_half1", ""))
+        ]
+        dy_mx = [quantize(f"dy{c}", dy_grouped[c][:], E5M2) for c in range(2)]
+        silu(1, held("silu_neg1", [P, F], F32, replaces="lifted0")[:])
         make_dh(0, dy_mx[0], block(0), "gt_turned")
         make_dh(1, dy_mx[1], block(0), "w1_turned0")
         make_da(0, "w1_turned1")
-        fetch_da(0, nc.vector.tensor_copy)
-        make_dx(0, "a1")
-        add_dy(0)
         make_slope(1)
         make_da(1, "a0")
+        fetch_da(0, nc.vector.tensor_copy, "slope1")
         fetch_da(1, nc.vector.tensor_copy)
-        make_dx(1, "dh0")
-        tanh(2, held("tanh_half2", [P, F], F32, replaces="scaled1")[:])
-        dy_got.append(held("dy_got1", [P, LANES, HALF], F32, replaces="dy_grouped1"))
+        make_dx(0, "a1")
+        add_dy(0)
+        scale(2, a[2], "dy_grouped1")
+        scale(3, a[3], "slope0")
+        dy_got.append(held("dy_got1", [P, LANES, HALF], F32, replaces="scaled1"))
         for t in range(LANES):
             scalar_gather(dy_got[1][:, t, :], dy_pool[t], half(1))
-        silu(2, held("silu_neg2", [P, F], F32, replaces="dy_pool2")[:])
-        tanh(3, held("tanh_half3", [P, F], F32, replaces="dy_pool3")[:])
-        silu(3, held("silu_neg3", [P, F], F32, replaces="scaled2")[:])
+        activate(2, "dy_pool2")
+        activate(3, "dy_pool3")
         dy_grouped_late = interleave(nc.vector.tensor_copy, "dy_grouped_late", dy_got[1][:], "da1")
+        make_dx(1, "dh0")
         dy_late = quantize("dy_late", dy_grouped_late[:], E5M2)
         make_dh(2, dy_late, block(0), "a2")
         make_dh(3, dy_late, block(1), "a3")
-        lift(2)
-        make_slope(2, "da_grouped1")
-        make_da(2, "dh1")
-        lift(3, "dy_grouped_late")
+        lift(2, "dy_grouped_late")
+        lift(3, "da_grouped1")
+        make_slope(2)
         make_slope(3)
-        add_dy(1, replaces="silu_neg3")
+        make_da(2, "dh1")
+        add_dy(1, 1, LANES, "activated3")
         make_da(3, "da_turned0")
         for c in (2, 3):
             fetch_da(c, nc.vector.tensor_copy)
         make_dx(2, "da_turned1")
         make_dx(3, "c_row")
+        add_dy(1, 0, 1, "slope3")
         add_dy(2)
         add_dy(3)
 
@@ -343,9 +342,8 @@ def tile_attend_gdepth_sil_pl_kernel(tc, xT, dyT, w1, w2, cf, gt, tx, c1, offs, 
         vector_scatter(0, 1)
         for c in (2, 3):
             vector_scatter(2, c)
-        for t in PLANE_ORDER[1:]:
-            for c in (2, 3):
-                scalar_scatter(t, c)
+        for t, c in ((3, 2), (1, 2), (3, 3), (1, 3), (0, 2), (0, 3)):
+            scalar_scatter(t, c)
         for t in PLANE_ORDER:
             nc.sync.dma_start(out=out_rows[:, t, :], in_=out_plane[t][:])
 
@@ -359,8 +357,9 @@ def tile_attend_gdepth_sil_pl_kernel(tc, xT, dyT, w1, w2, cf, gt, tx, c1, offs, 
         split = 3 * T // 4
         for t in PLANE_ORDER[:2]:
             nc.vector.tensor_copy(out=out_lane[t], in_=out_plane[t][:])
-        for t in PLANE_ORDER[2:]:
-            nc.vector.tensor_copy(out=out_lane[t][:, :split], in_=out_plane[t][:, :split])
+        for t, cuts in zip(PLANE_ORDER[2:], ((0, split), (0, T // 4, split))):
+            for first, last in zip(cuts, cuts[1:]):
+                nc.vector.tensor_copy(out=out_lane[t][:, first:last], in_=out_plane[t][:, first:last])
             nc.scalar.copy(out=out_lane[t][:, split:], in_=out_plane[t][:, split:])
         for part in runs[:2]:
             nc.vector.tensor_copy(out=woven[:, part].bitcast(I32), in_=pair_words[:, part].bitcast(I32))
@@ -370,7 +369,7 @@ def tile_attend_gdepth_sil_pl_kernel(tc, xT, dyT, w1, w2, cf, gt, tx, c1, offs, 
         out_codes = held("out_codes", [P, T], U32)
         out_scales = held("out_scales", [P, T], U8)
         words_hbm = out_1[0].rearrange("p n l -> p (n l)").bitcast(I32)
-        for cols in quarters:
+        for cols in quarters[:2] + quarters[:1:-1]:
             nc.vector.quantize_mx(
                 out=out_codes[:, cols].bitcast(E4M3),
                 scales=out_scales[:, cols],

@@ -84,7 +84,7 @@ def tile_attend_gdepth_sil_pl_kernel(tc, xT, dyT, w1, w2, cf, gt, tx, c1, offs, 
         cf_col = held("cf_col", [P, LANES], F32)
         c1_col = held("c1_col", [P, LANES], F32)
         x_plane = [held(f"x_plane{t}", [P, T], F32) for t in range(LANES)]
-        w1_raw = held("w1_raw", [P, LANES, F], F32)
+        w1_raw = [held(f"w1_raw{s}", [P, 2, F], F32) for s in range(2)]
         w2_raw = held("w2_raw", [P, LANES, F], F32)
         dy_pool = [held(f"dy_pool{t}", [P, T], F32) for t in range(LANES)]
         out_plane = [held(f"out_plane{t}", [P, T], F32) for t in range(LANES)]
@@ -94,10 +94,12 @@ def tile_attend_gdepth_sil_pl_kernel(tc, xT, dyT, w1, w2, cf, gt, tx, c1, offs, 
         nc.sync.dma_start(offsets[:], offs)
         nc.scalar.dma_start(out=tx_pool[LAST:, :], in_=tx[LAST:, :])
         nc.scalar.dma_start(out=gt_pool[LAST:, :], in_=gt[LAST:, :])
-        nc.scalar.dma_start(out=cf_col[:], in_=cf.rearrange("(m t) o -> m (t o)", t=LANES))
         nc.scalar.dma_start(out=c1_col[:], in_=c1.rearrange("(m t) o -> m (t o)", t=LANES))
-        nc.sync.dma_start(out=w1_raw[:], in_=w1.rearrange("(p j) f -> p j f", j=LANES))
-        for t in range(LANES):
+        nc.sync.dma_start(out=cf_col[:], in_=cf.rearrange("(m t) o -> m (t o)", t=LANES))
+        nc.sync.dma_start(out=x_plane[0][:], in_=x_rows[:, 0, :])
+        for s in range(2):
+            nc.sync.dma_start(out=w1_raw[s][:], in_=w1.rearrange("(p j) f -> p j f", j=LANES)[:, 2 * s : 2 * s + 2, :])
+        for t in range(1, LANES):
             nc.sync.dma_start(out=x_plane[t][:], in_=x_rows[:, t, :])
         nc.sync.dma_start(out=dy_pool[0][:], in_=dy_rows[:, 0, :])
         nc.sync.dma_start(out=w2_raw[:], in_=w2.rearrange("(p j) f -> p j f", j=LANES))
@@ -116,20 +118,15 @@ def tile_attend_gdepth_sil_pl_kernel(tc, xT, dyT, w1, w2, cf, gt, tx, c1, offs, 
         nc.vector.memset(tx_pool[:LAST, :], 0.0)
         nc.vector.memset(gt_pool[:LAST, :], 0.0)
 
-        def slot_columns(name, pool_tile, gather):
+        def slot_columns(name, pool_tile, gather, replaces=""):
             got = held(name + "_got", [P, N], F32)
             gather(got[:], pool_tile, slice(0, N))
-            turned = bank(name + "_turned")
+            turned = bank(name + "_turned", replaces)
             for c in range(CHUNKS):
                 nc.tensor.transpose(turned[:, block(c)], got[:, block(c)], ident[:])
             return turned[:].rearrange("p (c r) -> p c r", r=P)[:, :, LAST]
 
         tx_cols = slot_columns("tx", tx_pool, vector_gather)
-        gt_cols = slot_columns("gt", gt_pool, scalar_gather)
-        tx_neg = held("tx_neg", [P, CHUNKS], F32)
-        tx_half = held("tx_half", [P, CHUNKS], F32)
-        nc.vector.tensor_scalar(out=tx_neg[:], in0=tx_cols, scalar1=-1.0, scalar2=zeros[:], op0=ALU.mult, op1=ALU.add)
-        nc.vector.tensor_scalar(out=tx_half[:], in0=tx_cols, scalar1=0.5, scalar2=None, op0=ALU.mult)
 
         def unit_row(name, column):
             row = bank(name)
@@ -138,34 +135,11 @@ def tile_attend_gdepth_sil_pl_kernel(tc, xT, dyT, w1, w2, cf, gt, tx, c1, offs, 
                 nc.tensor.transpose(places[:, t // 2, t % 2, :], column[:, t : t + 1].to_broadcast([P, P]), ident[:])
             return row
 
-
-        w1_rounded = held("w1_rounded", [P, LANES, F], BF16)
-        nc.vector.tensor_copy(
-            out=w1_rounded[:].rearrange("p j (u m e) -> p j m u e", u=2, e=2),
-            in_=w1_raw[:].rearrange("p j (m u e) -> p j m u e", u=2, e=2),
-        )
-        w1_grouped = held("w1_grouped", [P, F * LANES], BF16)
-        nc.vector.tensor_copy(
-            out=w1_grouped[:].rearrange("p (n i t) -> p n t i", i=RUN, t=LANES),
-            in_=w1_rounded[:].rearrange("p t (n i) -> p n t i", i=RUN),
-        )
-        w1_mx = quantize("w1", w1_grouped[:], E4M3)
-        x_got = [held(f"x_got{h}", [P, LANES, HALF], BF16) for h in range(2)]
-        for h in range(2):
-            scalar_gather(x_got[h][:, 0, :], x_plane[0], half(h))
-        w1t_grouped = held("w1t_grouped", [P, D * LANES], BF16)
-        w1t_words = w1t_grouped[:].bitcast(F32).rearrange("p (s n i u) -> p s n u i", s=2, u=2, i=RUN)
-        w1_words = w1_rounded[:].rearrange("p j f -> p (j f)").bitcast(F32).rearrange("p (j u m) -> p j u m", j=LANES, u=2)
-        for s in range(2):
-            turned = bank(f"w1_turned{s}")
-            for u in range(2):
-                for b in range(2):
-                    nc.tensor.transpose(turned[:, block(2 * u + b)], w1_words[:, 2 * s + b, u, :], ident[:])
-            nc.scalar.copy(out=w1t_words[:, s], in_=turned[:].rearrange("p (u n i) -> p n u i", u=2, i=RUN))
-        slot_factor = held("slot_factor", [P, CHUNKS], F32, replaces="w1_raw")
-        nc.vector.scalar_tensor_tensor(
-            out=slot_factor[:], in0=gt_cols, scalar=0.5, in1=tx_neg[:], op0=ALU.mult, op1=ALU.mult
-        )
+        cf_turned = unit_row("cf_turned", cf_col)
+        tx_neg = held("tx_neg", [P, CHUNKS], F32)
+        tx_half = held("tx_half", [P, CHUNKS], F32)
+        nc.vector.tensor_scalar(out=tx_neg[:], in0=tx_cols, scalar1=-1.0, scalar2=zeros[:], op0=ALU.mult, op1=ALU.add)
+        nc.vector.tensor_scalar(out=tx_half[:], in0=tx_cols, scalar1=0.5, scalar2=None, op0=ALU.mult)
 
         def interleave(copy, name, planes, replaces=""):
             grouped = held(name, [P, planes.shape[2] * LANES], BF16, replaces)
@@ -175,22 +149,46 @@ def tile_attend_gdepth_sil_pl_kernel(tc, xT, dyT, w1, w2, cf, gt, tx, c1, offs, 
             )
             return grouped
 
+        x_got = [held(f"x_got{h}", [P, LANES, HALF], BF16) for h in range(2)]
         for h in range(2):
-            vector_gather(x_got[h][:, 1, :], x_plane[1], half(h))
+            scalar_gather(x_got[h][:, 0, :], x_plane[0], half(h))
+        cf_row = held("cf_row", [P, F], F32, replaces="x_plane0")
+        nc.scalar.copy(out=cf_row[:], in_=cf_turned[:])
+        w1_rounded = held("w1_rounded", [P, LANES, F], BF16)
+        for s in range(2):
+            nc.vector.tensor_copy(
+                out=w1_rounded[:, 2 * s : 2 * s + 2, :].rearrange("p j (u m e) -> p j m u e", u=2, e=2),
+                in_=w1_raw[s][:].rearrange("p j (m u e) -> p j m u e", u=2, e=2),
+            )
+        w1_grouped = interleave(nc.vector.tensor_copy, "w1_grouped", w1_rounded[:])
+        w1_mx = quantize("w1", w1_grouped[:], E4M3)
+        w1_words = w1_rounded[:].rearrange("p j f -> p (j f)").bitcast(F32).rearrange("p (j u m) -> p j u m", j=LANES, u=2)
+
+        def turn_w1(s, replaces=""):
+            turned = bank(f"w1_turned{s}")
+            for u in range(2):
+                for b in range(2):
+                    nc.tensor.transpose(turned[:, block(2 * u + b)], w1_words[:, 2 * s + b, u, :], ident[:])
+            grouped = held(f"w1t_grouped{s}", [P, 2 * P * LANES], BF16, replaces)
+            nc.scalar.copy(
+                out=grouped[:].bitcast(F32).rearrange("p (n i u) -> p n u i", u=2, i=RUN),
+                in_=turned[:].rearrange("p (u n i) -> p n u i", u=2, i=RUN),
+            )
+            return grouped
+
+        w1t_grouped = [turn_w1(0)]
+        gt_cols = slot_columns("gt", gt_pool, vector_gather, "w1_turned0")
         for h in range(2):
-            scalar_gather(x_got[h][:, 2, :], x_plane[2], half(h))
+            scalar_gather(x_got[h][:, 1, :], x_plane[1], half(h))
+        vector_gather(x_got[0][:, 2, :], x_plane[2], half(0))
+        scalar_gather(x_got[1][:, 2, :], x_plane[2], half(1))
         for c in range(2):
             vector_gather(x_got[0][:, 3, block(c)], x_plane[3], block(c))
         scalar_gather(x_got[1][:, 3, :], x_plane[3], half(1))
         x_grouped = [interleave(nc.vector.tensor_copy, f"x_grouped{c}", x_got[0][:, :, block(c)]) for c in range(2)]
         x_grouped.append(interleave(nc.scalar.copy, "x_grouped2", x_got[1][:]))
-        x_mx = [quantize(f"x{n}", x_grouped[n][:], E4M3) for n in range(3)]
-        c_col = held("c_col", [P, LANES], F32, replaces="x_plane1")
-        nc.vector.tensor_tensor(out=c_col[:], in0=cf_col[:], in1=c1_col[:], op=ALU.mult)
-        cf_row = held("cf_row", [P, F], F32, replaces="x_plane3")
-        nc.scalar.copy(out=cf_row[:], in_=unit_row("cf_turned", cf_col)[:])
-        c_row = unit_row("c_row", c_col)
-        w1t_mx = quantize("w1t", w1t_grouped[:], E4M3, replaces="x_grouped1")
+        x_mx = [quantize(f"x{n}", x_grouped[n][:], E4M3) for n in range(2)]
+        w1t_grouped.append(turn_w1(1, "x_got1"))
 
         scaled, tanh_half, silu_neg, lifted, slope, dh, da_turned, da_grouped, dx = ({} for n in range(9))
 
@@ -232,8 +230,8 @@ def tile_attend_gdepth_sil_pl_kernel(tc, xT, dyT, w1, w2, cf, gt, tx, c1, offs, 
             dh[c] = bank(f"dh{c}", replaces)
             product(dh[c][:], dy_mx, E5M2, cols, w2_mx, E4M3)
 
-        def make_da(c, replaces):
-            da = held(f"da{c}", [P, F], BF16)
+        def make_da(c, replaces, after=""):
+            da = held(f"da{c}", [P, F], BF16, after)
             nc.vector.scalar_tensor_tensor(
                 out=da[:], in0=dh[c][:], scalar=slot_factor[:, c : c + 1], in1=slope[c][:], op0=ALU.mult, op1=ALU.mult
             )
@@ -252,7 +250,7 @@ def tile_attend_gdepth_sil_pl_kernel(tc, xT, dyT, w1, w2, cf, gt, tx, c1, offs, 
             da_mx = quantize(f"da{c}", da_grouped[c][:], E5M2)
             dx[c] = bank(f"dx{c}", replaces)
             for t in range(LANES):
-                product(dx[c][:, block(t)], w1t_mx, E4M3, block(t), da_mx, E5M2)
+                product(dx[c][:, block(t)], w1t_mx[t // 2], E4M3, block(t % 2), da_mx, E5M2)
 
         new_cols = {}
 
@@ -273,73 +271,81 @@ def tile_attend_gdepth_sil_pl_kernel(tc, xT, dyT, w1, w2, cf, gt, tx, c1, offs, 
         def vector_scatter(t, c):
             nc.vector.tensor_copy(out=out_plane[t][:].indirect(entries(block(c))), in_=new_cols[t, c])
 
-        a = [first_product(c, replaces) for c, replaces in enumerate(("", "", "cf_turned", "tx_turned"))]
-        dy_got = [held("dy_got0", [P, LANES, HALF], F32)]
+        dy_got = [held("dy_got0", [P, LANES, HALF], F32, replaces="x_grouped0")]
+        vector_gather(dy_got[0][:, 0, :], dy_pool[0], half(0))
+        w1t_mx = [quantize("w1t0", w1t_grouped[0][:], E4M3, "x_grouped1")]
+        a = [first_product(c, "") for c in range(2)]
         scale(0, a[0])
         scale(1, a[1])
-        w2_grouped = held("w2_grouped", [P, F * LANES], BF16, replaces="x1_codes")
+        c_col = held("c_col", [P, LANES], F32, replaces="x1_scales")
+        nc.vector.tensor_tensor(out=c_col[:], in0=cf_col[:], in1=c1_col[:], op=ALU.mult)
+        c_row = unit_row("c_row", c_col)
+        slot_factor = held("slot_factor", [P, CHUNKS], F32, replaces="x0_scales")
+        nc.vector.scalar_tensor_tensor(
+            out=slot_factor[:], in0=gt_cols, scalar=0.5, in1=tx_neg[:], op0=ALU.mult, op1=ALU.mult
+        )
+        x_mx.append(quantize("x2", x_grouped[2][:], E4M3, "x1_codes"))
+        a += [first_product(c, replaces) for c, replaces in ((2, ""), (3, "tx_turned"))]
+        w2_grouped = held("w2_grouped", [P, F * LANES], BF16, replaces="x0_codes")
         nc.vector.tensor_copy(
             out=w2_grouped[:].rearrange("p (u m e j) -> p m j u e", u=2, e=2, j=LANES),
             in_=w2_raw[:].rearrange("p j (m u e) -> p m j u e", u=2, e=2),
         )
         activate(0)
-        tanh(1, held("tanh_half1", [P, F], F32)[:])
-        for t in range(LANES - 1):
+        for t in range(1, LANES - 1):
             scalar_gather(dy_got[0][:, t, :], dy_pool[t], half(0))
-        for c in range(2):
-            scalar_gather(dy_got[0][:, LANES - 1, block(c)], dy_pool[LANES - 1], block(c))
         lift(0)
         w2_mx = quantize("w2", w2_grouped[:], E4M3)
-        lift(1)
         make_slope(0)
+        for c in range(2):
+            vector_gather(dy_got[0][:, LANES - 1, block(c)], dy_pool[LANES - 1], block(c))
         dy_grouped = [
             interleave(nc.vector.tensor_copy, f"dy_grouped{c}", dy_got[0][:, :, block(c)], replaces)
-            for c, replaces in enumerate(("tanh_half1", ""))
+            for c, replaces in enumerate(("activated0", ""))
         ]
         dy_mx = [quantize(f"dy{c}", dy_grouped[c][:], E5M2) for c in range(2)]
-        silu(1, held("silu_neg1", [P, F], F32, replaces="lifted0")[:])
+        activate(1, "w2_grouped")
         make_dh(0, dy_mx[0], block(0), "gt_turned")
-        make_dh(1, dy_mx[1], block(0), "w1_turned0")
+        make_dh(1, dy_mx[1], block(0), "cf_turned")
         make_da(0, "w1_turned1")
-        make_slope(1)
-        make_da(1, "a0")
-        fetch_da(0, nc.vector.tensor_copy, "slope1")
-        fetch_da(1, nc.vector.tensor_copy)
+        scale(2, a[2], "dy_grouped0")
+        scale(3, a[3], "dy_grouped1")
+        lift(1, "dy0_codes")
+        w1t_mx.append(quantize("w1t1", w1t_grouped[1][:], E4M3, "dy1_codes"))
+        fetch_da(0, nc.vector.tensor_copy)
         make_dx(0, "a1")
         add_dy(0)
-        scale(2, a[2], "dy_grouped1")
-        scale(3, a[3], "slope0")
+        make_slope(1)
+        make_da(1, "a0")
         dy_got.append(held("dy_got1", [P, LANES, HALF], F32, replaces="scaled1"))
         for t in range(LANES):
             scalar_gather(dy_got[1][:, t, :], dy_pool[t], half(1))
         activate(2, "dy_pool2")
         activate(3, "dy_pool3")
-        dy_grouped_late = interleave(nc.vector.tensor_copy, "dy_grouped_late", dy_got[1][:], "da1")
-        make_dx(1, "dh0")
+        dy_grouped_late = interleave(nc.vector.tensor_copy, "dy_grouped_late", dy_got[1][:], "lifted1")
         dy_late = quantize("dy_late", dy_grouped_late[:], E5M2)
+        fetch_da(1, nc.scalar.copy)
+        make_dx(1, "dh0")
         make_dh(2, dy_late, block(0), "a2")
         make_dh(3, dy_late, block(1), "a3")
-        lift(2, "dy_grouped_late")
-        lift(3, "da_grouped1")
+        lift(2, "slope1")
+        lift(3, "dy_grouped_late")
         make_slope(2)
-        make_slope(3)
+        add_dy(1)
         make_da(2, "dh1")
-        add_dy(1, 1, LANES, "activated3")
+        fetch_da(2, nc.vector.tensor_copy)
+        make_slope(3, "activated2")
         make_da(3, "da_turned0")
-        for c in (2, 3):
-            fetch_da(c, nc.vector.tensor_copy)
         make_dx(2, "da_turned1")
+        fetch_da(3, nc.vector.tensor_copy)
         make_dx(3, "c_row")
-        add_dy(1, 0, 1, "slope3")
         add_dy(2)
         add_dy(3)
 
         out_rows = out_0.rearrange("(p t) n -> p t n", t=LANES)
-        for t in PLANE_ORDER:
-            scalar_scatter(t, 0)
-        for t in PLANE_ORDER[:-1]:
-            scalar_scatter(t, 1)
-        vector_scatter(0, 1)
+        for c in (0, 1):
+            for t in PLANE_ORDER:
+                scalar_scatter(t, c)
         for c in (2, 3):
             vector_scatter(2, c)
         for t, c in ((3, 2), (1, 2), (3, 3), (1, 3), (0, 2), (0, 3)):

@@ -93,9 +93,9 @@ def tile_attend_gdepth_sil_pl_kernel(tc, xT, dyT, w1, w2, cf, gt, tx, c1, offs, 
 
         nc.sync.dma_start(offsets[:], offs)
         nc.scalar.dma_start(out=tx_pool[LAST:, :], in_=tx[LAST:, :])
-        nc.scalar.dma_start(out=gt_pool[LAST:, :], in_=gt[LAST:, :])
         nc.scalar.dma_start(out=c1_col[:], in_=c1.rearrange("(m t) o -> m (t o)", t=LANES))
         nc.sync.dma_start(out=cf_col[:], in_=cf.rearrange("(m t) o -> m (t o)", t=LANES))
+        nc.sync.dma_start(out=gt_pool[LAST:, :], in_=gt[LAST:, :])
         nc.sync.dma_start(out=x_plane[0][:], in_=x_rows[:, 0, :])
         for s in range(2):
             nc.sync.dma_start(out=w1_raw[s][:], in_=w1.rearrange("(p j) f -> p j f", j=LANES)[:, 2 * s : 2 * s + 2, :])
@@ -154,41 +154,39 @@ def tile_attend_gdepth_sil_pl_kernel(tc, xT, dyT, w1, w2, cf, gt, tx, c1, offs, 
             scalar_gather(x_got[h][:, 0, :], x_plane[0], half(h))
         cf_row = held("cf_row", [P, F], F32, replaces="x_plane0")
         nc.scalar.copy(out=cf_row[:], in_=cf_turned[:])
-        w1_rounded = held("w1_rounded", [P, LANES, F], BF16)
+        w1_row = held("w1_rounded", [P, LANES * F], BF16)
+        w1_rounded = w1_row[:].rearrange("p (j f) -> p j f", j=LANES)
         for s in range(2):
             nc.vector.tensor_copy(
                 out=w1_rounded[:, 2 * s : 2 * s + 2, :].rearrange("p j (u m e) -> p j m u e", u=2, e=2),
                 in_=w1_raw[s][:].rearrange("p j (m u e) -> p j m u e", u=2, e=2),
             )
-        w1_grouped = interleave(nc.vector.tensor_copy, "w1_grouped", w1_rounded[:])
+        w1_grouped = interleave(nc.vector.tensor_copy, "w1_grouped", w1_rounded)
         w1_mx = quantize("w1", w1_grouped[:], E4M3)
-        w1_words = w1_rounded[:].rearrange("p j f -> p (j f)").bitcast(F32).rearrange("p (j u m) -> p j u m", j=LANES, u=2)
+        w1_words = w1_row[:].bitcast(F32).rearrange("p (j u m) -> p j u m", j=LANES, u=2)
+
+        w1t_grouped = held("w1t_grouped", [P, D * LANES], BF16)
+        w1t_words = w1t_grouped[:].bitcast(F32).rearrange("p (s n i u) -> p s n u i", s=2, u=2, i=RUN)
 
         def turn_w1(s, replaces=""):
-            turned = bank(f"w1_turned{s}")
+            turned = bank(f"w1_turned{s}", replaces)
             for u in range(2):
                 for b in range(2):
                     nc.tensor.transpose(turned[:, block(2 * u + b)], w1_words[:, 2 * s + b, u, :], ident[:])
-            grouped = held(f"w1t_grouped{s}", [P, 2 * P * LANES], BF16, replaces)
-            nc.scalar.copy(
-                out=grouped[:].bitcast(F32).rearrange("p (n i u) -> p n u i", u=2, i=RUN),
-                in_=turned[:].rearrange("p (u n i) -> p n u i", u=2, i=RUN),
-            )
-            return grouped
+            nc.scalar.copy(out=w1t_words[:, s], in_=turned[:].rearrange("p (u n i) -> p n u i", u=2, i=RUN))
 
-        w1t_grouped = [turn_w1(0)]
+        turn_w1(0)
         gt_cols = slot_columns("gt", gt_pool, vector_gather, "w1_turned0")
-        for h in range(2):
-            scalar_gather(x_got[h][:, 1, :], x_plane[1], half(h))
-        vector_gather(x_got[0][:, 2, :], x_plane[2], half(0))
-        scalar_gather(x_got[1][:, 2, :], x_plane[2], half(1))
+        for t in (1, 2):
+            for h in range(2):
+                scalar_gather(x_got[h][:, t, :], x_plane[t], half(h))
         for c in range(2):
             vector_gather(x_got[0][:, 3, block(c)], x_plane[3], block(c))
         scalar_gather(x_got[1][:, 3, :], x_plane[3], half(1))
+        turn_w1(1)
         x_grouped = [interleave(nc.vector.tensor_copy, f"x_grouped{c}", x_got[0][:, :, block(c)]) for c in range(2)]
         x_grouped.append(interleave(nc.scalar.copy, "x_grouped2", x_got[1][:]))
         x_mx = [quantize(f"x{n}", x_grouped[n][:], E4M3) for n in range(2)]
-        w1t_grouped.append(turn_w1(1, "x_got1"))
 
         scaled, tanh_half, silu_neg, lifted, slope, dh, da_turned, da_grouped, dx = ({} for n in range(9))
 
@@ -250,7 +248,7 @@ def tile_attend_gdepth_sil_pl_kernel(tc, xT, dyT, w1, w2, cf, gt, tx, c1, offs, 
             da_mx = quantize(f"da{c}", da_grouped[c][:], E5M2)
             dx[c] = bank(f"dx{c}", replaces)
             for t in range(LANES):
-                product(dx[c][:, block(t)], w1t_mx[t // 2], E4M3, block(t % 2), da_mx, E5M2)
+                product(dx[c][:, block(t)], w1t_mx, E4M3, block(t), da_mx, E5M2)
 
         new_cols = {}
 
@@ -271,19 +269,17 @@ def tile_attend_gdepth_sil_pl_kernel(tc, xT, dyT, w1, w2, cf, gt, tx, c1, offs, 
         def vector_scatter(t, c):
             nc.vector.tensor_copy(out=out_plane[t][:].indirect(entries(block(c))), in_=new_cols[t, c])
 
-        dy_got = [held("dy_got0", [P, LANES, HALF], F32, replaces="x_grouped0")]
-        vector_gather(dy_got[0][:, 0, :], dy_pool[0], half(0))
-        w1t_mx = [quantize("w1t0", w1t_grouped[0][:], E4M3, "x_grouped1")]
+        w1t_mx = quantize("w1t", w1t_grouped[:], E4M3, "x_grouped0")
         a = [first_product(c, "") for c in range(2)]
-        scale(0, a[0])
-        scale(1, a[1])
-        c_col = held("c_col", [P, LANES], F32, replaces="x1_scales")
+        c_col = held("c_col", [P, LANES], F32, replaces="x_grouped1")
         nc.vector.tensor_tensor(out=c_col[:], in0=cf_col[:], in1=c1_col[:], op=ALU.mult)
         c_row = unit_row("c_row", c_col)
-        slot_factor = held("slot_factor", [P, CHUNKS], F32, replaces="x0_scales")
+        slot_factor = held("slot_factor", [P, CHUNKS], F32, replaces="x_got0")
         nc.vector.scalar_tensor_tensor(
             out=slot_factor[:], in0=gt_cols, scalar=0.5, in1=tx_neg[:], op0=ALU.mult, op1=ALU.mult
         )
+        scale(0, a[0])
+        scale(1, a[1])
         x_mx.append(quantize("x2", x_grouped[2][:], E4M3, "x1_codes"))
         a += [first_product(c, replaces) for c, replaces in ((2, ""), (3, "tx_turned"))]
         w2_grouped = held("w2_grouped", [P, F * LANES], BF16, replaces="x0_codes")
@@ -292,66 +288,72 @@ def tile_attend_gdepth_sil_pl_kernel(tc, xT, dyT, w1, w2, cf, gt, tx, c1, offs, 
             in_=w2_raw[:].rearrange("p j (m u e) -> p m j u e", u=2, e=2),
         )
         activate(0)
-        for t in range(1, LANES - 1):
+        tanh(1, held("tanh_half1", [P, F], F32)[:])
+        dy_got = [held("dy_got0", [P, LANES, HALF], F32, replaces="scaled0")]
+        for t in range(LANES - 1):
             scalar_gather(dy_got[0][:, t, :], dy_pool[t], half(0))
         lift(0)
         w2_mx = quantize("w2", w2_grouped[:], E4M3)
+        lift(1)
         make_slope(0)
+        silu(1, held("silu_neg1", [P, F], F32, replaces="tanh_half1")[:])
         for c in range(2):
             vector_gather(dy_got[0][:, LANES - 1, block(c)], dy_pool[LANES - 1], block(c))
         dy_grouped = [
             interleave(nc.vector.tensor_copy, f"dy_grouped{c}", dy_got[0][:, :, block(c)], replaces)
-            for c, replaces in enumerate(("activated0", ""))
+            for c, replaces in enumerate(("", ""))
         ]
         dy_mx = [quantize(f"dy{c}", dy_grouped[c][:], E5M2) for c in range(2)]
-        activate(1, "w2_grouped")
         make_dh(0, dy_mx[0], block(0), "gt_turned")
         make_dh(1, dy_mx[1], block(0), "cf_turned")
+        make_slope(1, "dy_grouped0")
         make_da(0, "w1_turned1")
-        scale(2, a[2], "dy_grouped0")
-        scale(3, a[3], "dy_grouped1")
-        lift(1, "dy0_codes")
-        w1t_mx.append(quantize("w1t1", w1t_grouped[1][:], E4M3, "dy1_codes"))
-        fetch_da(0, nc.vector.tensor_copy)
-        make_dx(0, "a1")
-        add_dy(0)
-        make_slope(1)
-        make_da(1, "a0")
+        scale(2, a[2], "dy0_codes")
+        make_da(1, "a0", "slope0")
+        scale(3, a[3], "lifted1")
         dy_got.append(held("dy_got1", [P, LANES, HALF], F32, replaces="scaled1"))
         for t in range(LANES):
             scalar_gather(dy_got[1][:, t, :], dy_pool[t], half(1))
-        activate(2, "dy_pool2")
-        activate(3, "dy_pool3")
-        dy_grouped_late = interleave(nc.vector.tensor_copy, "dy_grouped_late", dy_got[1][:], "lifted1")
-        dy_late = quantize("dy_late", dy_grouped_late[:], E5M2)
+        dy_grouped_late = interleave(nc.scalar.copy, "dy_grouped_late", dy_got[1][:])
+        fetch_da(0, nc.scalar.copy)
         fetch_da(1, nc.scalar.copy)
+        activate(2, "dy_pool3")
+        activate(3, "dy_pool2")
+        make_dx(0, "a1")
+        dy_late = quantize("dy_late", dy_grouped_late[:], E5M2, "slope1")
         make_dx(1, "dh0")
+        add_dy(0, 1, LANES, "da1")
+        lift(2, "da_grouped0")
         make_dh(2, dy_late, block(0), "a2")
         make_dh(3, dy_late, block(1), "a3")
-        lift(2, "slope1")
         lift(3, "dy_grouped_late")
         make_slope(2)
         add_dy(1)
         make_da(2, "dh1")
-        fetch_da(2, nc.vector.tensor_copy)
         make_slope(3, "activated2")
+        fetch_da(2, nc.vector.tensor_copy)
         make_da(3, "da_turned0")
         make_dx(2, "da_turned1")
         fetch_da(3, nc.vector.tensor_copy)
         make_dx(3, "c_row")
+        add_dy(0, 0, 1, "slope3")
         add_dy(2)
-        add_dy(3)
+        add_dy(3, 2, LANES)
+        add_dy(3, 0, 2)
 
         out_rows = out_0.rearrange("(p t) n -> p t n", t=LANES)
         for c in (0, 1):
-            for t in PLANE_ORDER:
+            for t in PLANE_ORDER[:-1]:
                 scalar_scatter(t, c)
-        for c in (2, 3):
-            vector_scatter(2, c)
-        for t, c in ((3, 2), (1, 2), (3, 3), (1, 3), (0, 2), (0, 3)):
-            scalar_scatter(t, c)
+            vector_scatter(0, c)
         for t in PLANE_ORDER:
-            nc.sync.dma_start(out=out_rows[:, t, :], in_=out_plane[t][:])
+            scalar_scatter(t, 2)
+        for t in PLANE_ORDER[:-1]:
+            vector_scatter(t, 3)
+        scalar_scatter(0, 3)
+        for t in PLANE_ORDER:
+            queue = nc.scalar if t == PLANE_ORDER[-1] else nc.sync
+            queue.dma_start(out=out_rows[:, t, :], in_=out_plane[t][:])
 
         out_pairs = held("out_pairs", [P, 2, 2 * T], BF16)
         out_lane = [out_pairs[:, t // 2, :].rearrange("p (n e) -> p n e", e=2)[:, :, t % 2] for t in range(LANES)]
@@ -360,7 +362,7 @@ def tile_attend_gdepth_sil_pl_kernel(tc, xT, dyT, w1, w2, cf, gt, tx, c1, offs, 
         pair_words = out_pairs[:].bitcast(U32).rearrange("p u (n i) -> p n u i", i=RUN)
         quarters = [slice(n * T // 4, (n + 1) * T // 4) for n in range(4)]
         runs = [slice(cols.start // RUN, cols.stop // RUN) for cols in quarters]
-        split = 3 * T // 4
+        split = 5 * T // 8
         for t in PLANE_ORDER[:2]:
             nc.vector.tensor_copy(out=out_lane[t], in_=out_plane[t][:])
         for t, cuts in zip(PLANE_ORDER[2:], ((0, split), (0, T // 4, split))):

@@ -93,8 +93,8 @@ def tile_attend_gdepth_sil_pl_kernel(tc, xT, dyT, w1, w2, cf, gt, tx, c1, offs, 
 
         nc.sync.dma_start(offsets[:], offs)
         nc.scalar.dma_start(out=tx_pool[LAST:, :], in_=tx[LAST:, :])
-        nc.scalar.dma_start(out=c1_col[:], in_=c1.rearrange("(m t) o -> m (t o)", t=LANES))
         nc.sync.dma_start(out=cf_col[:], in_=cf.rearrange("(m t) o -> m (t o)", t=LANES))
+        nc.sync.dma_start(out=c1_col[:], in_=c1.rearrange("(m t) o -> m (t o)", t=LANES))
         nc.sync.dma_start(out=gt_pool[LAST:, :], in_=gt[LAST:, :])
         nc.sync.dma_start(out=x_plane[0][:], in_=x_rows[:, 0, :])
         for s in range(2):
@@ -154,6 +154,9 @@ def tile_attend_gdepth_sil_pl_kernel(tc, xT, dyT, w1, w2, cf, gt, tx, c1, offs, 
             scalar_gather(x_got[h][:, 0, :], x_plane[0], half(h))
         cf_row = held("cf_row", [P, F], F32, replaces="x_plane0")
         nc.scalar.copy(out=cf_row[:], in_=cf_turned[:])
+        c_col = held("c_col", [P, LANES], F32)
+        nc.vector.tensor_tensor(out=c_col[:], in0=cf_col[:], in1=c1_col[:], op=ALU.mult)
+        c_row = unit_row("c_row", c_col)
         w1_row = held("w1_rounded", [P, LANES * F], BF16)
         w1_rounded = w1_row[:].rearrange("p (j f) -> p j f", j=LANES)
         for s in range(2):
@@ -165,17 +168,21 @@ def tile_attend_gdepth_sil_pl_kernel(tc, xT, dyT, w1, w2, cf, gt, tx, c1, offs, 
         w1_mx = quantize("w1", w1_grouped[:], E4M3)
         w1_words = w1_row[:].bitcast(F32).rearrange("p (j u m) -> p j u m", j=LANES, u=2)
 
-        w1t_grouped = held("w1t_grouped", [P, D * LANES], BF16)
-        w1t_words = w1t_grouped[:].bitcast(F32).rearrange("p (s n i u) -> p s n u i", s=2, u=2, i=RUN)
 
-        def turn_w1(s, replaces=""):
-            turned = bank(f"w1_turned{s}", replaces)
+        def turn_w1(s):
+            turned = bank(f"w1_turned{s}")
             for u in range(2):
                 for b in range(2):
                     nc.tensor.transpose(turned[:, block(2 * u + b)], w1_words[:, 2 * s + b, u, :], ident[:])
-            nc.scalar.copy(out=w1t_words[:, s], in_=turned[:].rearrange("p (u n i) -> p n u i", u=2, i=RUN))
+            grouped = held(f"w1t_grouped{s}", [P, 2 * P * LANES], BF16)
+            nc.scalar.copy(
+                out=grouped[:].bitcast(F32).rearrange("p (n i u) -> p n u i", u=2, i=RUN),
+                in_=turned[:].rearrange("p (u n i) -> p n u i", u=2, i=RUN),
+            )
+            return grouped
 
-        turn_w1(0)
+        w1t_grouped = [turn_w1(0)]
+        w1t_mx = [quantize("w1t0", w1t_grouped[0][:], E4M3)]
         gt_cols = slot_columns("gt", gt_pool, vector_gather, "w1_turned0")
         for t in (1, 2):
             for h in range(2):
@@ -183,10 +190,10 @@ def tile_attend_gdepth_sil_pl_kernel(tc, xT, dyT, w1, w2, cf, gt, tx, c1, offs, 
         for c in range(2):
             vector_gather(x_got[0][:, 3, block(c)], x_plane[3], block(c))
         scalar_gather(x_got[1][:, 3, :], x_plane[3], half(1))
-        turn_w1(1)
+        w1t_grouped.append(turn_w1(1))
         x_grouped = [interleave(nc.vector.tensor_copy, f"x_grouped{c}", x_got[0][:, :, block(c)]) for c in range(2)]
-        x_grouped.append(interleave(nc.scalar.copy, "x_grouped2", x_got[1][:]))
         x_mx = [quantize(f"x{n}", x_grouped[n][:], E4M3) for n in range(2)]
+        x_grouped.append(interleave(nc.vector.tensor_copy, "x_grouped2", x_got[1][:], "x_grouped0"))
 
         scaled, tanh_half, silu_neg, lifted, slope, dh, da_turned, da_grouped, dx = ({} for n in range(9))
 
@@ -195,17 +202,17 @@ def tile_attend_gdepth_sil_pl_kernel(tc, xT, dyT, w1, w2, cf, gt, tx, c1, offs, 
             product(a[:], x_mx[min(c, 2)], E4M3, block(max(c - 2, 0)), w1_mx, E4M3)
             return a
 
-        def scale(c, a, replaces=""):
-            scaled[c] = held(f"scaled{c}", [P, F], F32, replaces)
-            nc.vector.tensor_tensor(out=scaled[c][:], in0=a[:], in1=cf_row[:], op=ALU.mult)
+        def scale(c, a, out):
+            scaled[c] = out
+            nc.vector.tensor_tensor(out=out, in0=a[:], in1=cf_row[:], op=ALU.mult)
 
         def tanh(c, out):
             tanh_half[c] = out
-            nc.scalar.activation(out=out, in_=scaled[c][:], func=ACT.Tanh, scale=tx_half[:, c : c + 1])
+            nc.scalar.activation(out=out, in_=scaled[c], func=ACT.Tanh, scale=tx_half[:, c : c + 1])
 
         def silu(c, out):
             silu_neg[c] = out
-            nc.scalar.activation(out=out, in_=scaled[c][:], func=ACT.Silu, scale=tx_neg[:, c : c + 1])
+            nc.scalar.activation(out=out, in_=scaled[c], func=ACT.Silu, scale=tx_neg[:, c : c + 1])
 
         def activate(c, replaces=""):
             both = held(f"activated{c}", [P, 2, F], F32, replaces)
@@ -248,7 +255,7 @@ def tile_attend_gdepth_sil_pl_kernel(tc, xT, dyT, w1, w2, cf, gt, tx, c1, offs, 
             da_mx = quantize(f"da{c}", da_grouped[c][:], E5M2)
             dx[c] = bank(f"dx{c}", replaces)
             for t in range(LANES):
-                product(dx[c][:, block(t)], w1t_mx, E4M3, block(t), da_mx, E5M2)
+                product(dx[c][:, block(t)], w1t_mx[t // 2], E4M3, block(t % 2), da_mx, E5M2)
 
         new_cols = {}
 
@@ -269,84 +276,89 @@ def tile_attend_gdepth_sil_pl_kernel(tc, xT, dyT, w1, w2, cf, gt, tx, c1, offs, 
         def vector_scatter(t, c):
             nc.vector.tensor_copy(out=out_plane[t][:].indirect(entries(block(c))), in_=new_cols[t, c])
 
-        w1t_mx = quantize("w1t", w1t_grouped[:], E4M3, "x_grouped0")
-        a = [first_product(c, "") for c in range(2)]
-        c_col = held("c_col", [P, LANES], F32, replaces="x_grouped1")
-        nc.vector.tensor_tensor(out=c_col[:], in0=cf_col[:], in1=c1_col[:], op=ALU.mult)
-        c_row = unit_row("c_row", c_col)
         slot_factor = held("slot_factor", [P, CHUNKS], F32, replaces="x_got0")
         nc.vector.scalar_tensor_tensor(
             out=slot_factor[:], in0=gt_cols, scalar=0.5, in1=tx_neg[:], op0=ALU.mult, op1=ALU.mult
         )
-        scale(0, a[0])
-        scale(1, a[1])
-        x_mx.append(quantize("x2", x_grouped[2][:], E4M3, "x1_codes"))
-        a += [first_product(c, replaces) for c, replaces in ((2, ""), (3, "tx_turned"))]
-        w2_grouped = held("w2_grouped", [P, F * LANES], BF16, replaces="x0_codes")
-        nc.vector.tensor_copy(
-            out=w2_grouped[:].rearrange("p (u m e j) -> p m j u e", u=2, e=2, j=LANES),
-            in_=w2_raw[:].rearrange("p j (m u e) -> p m j u e", u=2, e=2),
+        x_mx.append(quantize("x2", x_grouped[2][:], E4M3))
+        a = [first_product(c, replaces) for c, replaces in enumerate(("", "gt_turned", "", "tx_turned"))]
+        dy_late_row = held("dy_got1", [P, LANES * HALF], F32)
+        scale(0, a[0], held("scaled0", [P, F], F32, replaces="x_got1")[:])
+        scale(1, a[1], dy_late_row[:, HALF : HALF + F])
+        for c in (2, 3):
+            scale(c, a[c], held(f"scaled{c}", [P, F], F32)[:])
+        w2_grouped = held("w2_grouped", [P, F * LANES], BF16, replaces="x_grouped2")
+        nc.gpsimd.tensor_scalar(
+            out=w2_grouped[:].rearrange("p (u m e j) -> p m u e j", u=2, e=2, j=LANES),
+            in0=w2_raw[:].rearrange("p j (m u e) -> p m u e j", u=2, e=2),
+            scalar1=1.0,
+            scalar2=0.0,
+            op0=ALU.mult,
+            op1=ALU.add,
         )
         activate(0)
         tanh(1, held("tanh_half1", [P, F], F32)[:])
-        dy_got = [held("dy_got0", [P, LANES, HALF], F32, replaces="scaled0")]
+        dy_got = [held("dy_got0", [P, LANES, HALF], F32, replaces="x_plane3")]
         for t in range(LANES - 1):
             scalar_gather(dy_got[0][:, t, :], dy_pool[t], half(0))
+        silu(1, held("silu_neg1", [P, F], F32)[:])
         lift(0)
-        w2_mx = quantize("w2", w2_grouped[:], E4M3)
         lift(1)
-        make_slope(0)
-        silu(1, held("silu_neg1", [P, F], F32, replaces="tanh_half1")[:])
         for c in range(2):
             vector_gather(dy_got[0][:, LANES - 1, block(c)], dy_pool[LANES - 1], block(c))
-        dy_grouped = [
-            interleave(nc.vector.tensor_copy, f"dy_grouped{c}", dy_got[0][:, :, block(c)], replaces)
-            for c, replaces in enumerate(("", ""))
-        ]
+        w2_mx = quantize("w2", w2_grouped[:], E4M3)
+        dy_grouped = [interleave(nc.vector.tensor_copy, f"dy_grouped{c}", dy_got[0][:, :, block(c)]) for c in range(2)]
         dy_mx = [quantize(f"dy{c}", dy_grouped[c][:], E5M2) for c in range(2)]
-        make_dh(0, dy_mx[0], block(0), "gt_turned")
+        w1t_mx.append(quantize("w1t1", w1t_grouped[1][:], E4M3, "w2_raw"))
+        make_dh(0, dy_mx[0], block(0), "")
         make_dh(1, dy_mx[1], block(0), "cf_turned")
-        make_slope(1, "dy_grouped0")
+        make_slope(0, "dy_grouped0")
+        make_slope(1, "dy_grouped1")
         make_da(0, "w1_turned1")
-        scale(2, a[2], "dy0_codes")
-        make_da(1, "a0", "slope0")
-        scale(3, a[3], "lifted1")
-        dy_got.append(held("dy_got1", [P, LANES, HALF], F32, replaces="scaled1"))
+        make_da(1, "a0")
+        dy_got.append(dy_late_row[:].rearrange("p (t i) -> p t i", t=LANES))
         for t in range(LANES):
             scalar_gather(dy_got[1][:, t, :], dy_pool[t], half(1))
-        dy_grouped_late = interleave(nc.scalar.copy, "dy_grouped_late", dy_got[1][:])
+        dy_grouped_late = held("dy_grouped_late", [P, HALF * LANES], BF16, replaces="lifted1")
+        nc.gpsimd.tensor_scalar(
+            out=dy_grouped_late[:].rearrange("p (i t) -> p i t", t=LANES),
+            in0=dy_got[1].rearrange("p t i -> p i t"),
+            scalar1=1.0,
+            scalar2=0.0,
+            op0=ALU.mult,
+            op1=ALU.add,
+        )
         fetch_da(0, nc.scalar.copy)
         fetch_da(1, nc.scalar.copy)
         activate(2, "dy_pool3")
-        activate(3, "dy_pool2")
+        activate(3, "da0")
+        lift(2, "slope1")
         make_dx(0, "a1")
-        dy_late = quantize("dy_late", dy_grouped_late[:], E5M2, "slope1")
+        dy_late = quantize("dy_late", dy_grouped_late[:], E5M2)
         make_dx(1, "dh0")
-        add_dy(0, 1, LANES, "da1")
-        lift(2, "da_grouped0")
+        add_dy(0, replaces="da1")
         make_dh(2, dy_late, block(0), "a2")
         make_dh(3, dy_late, block(1), "a3")
+        make_slope(2, "da_grouped0")
         lift(3, "dy_grouped_late")
-        make_slope(2)
-        add_dy(1)
         make_da(2, "dh1")
         make_slope(3, "activated2")
-        fetch_da(2, nc.vector.tensor_copy)
+        add_dy(1, replaces="slope2")
         make_da(3, "da_turned0")
+        for c in (2, 3):
+            fetch_da(c, nc.vector.tensor_copy)
         make_dx(2, "da_turned1")
-        fetch_da(3, nc.vector.tensor_copy)
         make_dx(3, "c_row")
-        add_dy(0, 0, 1, "slope3")
         add_dy(2)
         add_dy(3, 2, LANES)
-        add_dy(3, 0, 2)
 
         out_rows = out_0.rearrange("(p t) n -> p t n", t=LANES)
         for c in (0, 1):
-            for t in PLANE_ORDER[:-1]:
+            for t in PLANE_ORDER:
                 scalar_scatter(t, c)
-            vector_scatter(0, c)
-        for t in PLANE_ORDER:
+        vector_scatter(2, 2)
+        add_dy(3, 0, 2)
+        for t in PLANE_ORDER[1:]:
             scalar_scatter(t, 2)
         for t in PLANE_ORDER[:-1]:
             vector_scatter(t, 3)

@@ -296,7 +296,8 @@ def tile_attend_gdepth_sil_pl_kernel(tc, xT, dyT, w1, w2, cf, gt, tx, c1, offs, 
             op0=ALU.mult,
             op1=ALU.add,
         )
-        activate(0)
+        tanh(0, held("tanh_half0", [P, F], F32)[:])
+        silu(0, held("silu_neg0", [P, F], F32)[:])
         tanh(1, held("tanh_half1", [P, F], F32)[:])
         dy_got = [held("dy_got0", [P, LANES, HALF], F32, replaces="x_plane3")]
         for t in range(LANES - 1):
@@ -309,60 +310,58 @@ def tile_attend_gdepth_sil_pl_kernel(tc, xT, dyT, w1, w2, cf, gt, tx, c1, offs, 
         w2_mx = quantize("w2", w2_grouped[:], E4M3)
         dy_grouped = [interleave(nc.vector.tensor_copy, f"dy_grouped{c}", dy_got[0][:, :, block(c)]) for c in range(2)]
         dy_mx = [quantize(f"dy{c}", dy_grouped[c][:], E5M2) for c in range(2)]
-        w1t_mx.append(quantize("w1t1", w1t_grouped[1][:], E4M3, "w2_raw"))
         make_dh(0, dy_mx[0], block(0), "")
         make_dh(1, dy_mx[1], block(0), "cf_turned")
         make_slope(0, "dy_grouped0")
-        make_slope(1, "dy_grouped1")
+        w1t_mx.append(quantize("w1t1", w1t_grouped[1][:], E4M3, "dy_grouped1"))
         make_da(0, "w1_turned1")
-        make_da(1, "a0")
+        make_slope(1, "w1t_grouped1")
         dy_got.append(dy_late_row[:].rearrange("p (t i) -> p t i", t=LANES))
         for t in range(LANES):
             scalar_gather(dy_got[1][:, t, :], dy_pool[t], half(1))
-        dy_grouped_late = held("dy_grouped_late", [P, HALF * LANES], BF16, replaces="lifted1")
-        nc.gpsimd.tensor_scalar(
-            out=dy_grouped_late[:].rearrange("p (i t) -> p i t", t=LANES),
-            in0=dy_got[1].rearrange("p t i -> p i t"),
-            scalar1=1.0,
-            scalar2=0.0,
-            op0=ALU.mult,
-            op1=ALU.add,
-        )
+        tanh(2, held("tanh_half2", [P, F], F32, replaces="dy_pool3")[:])
+        dy_grouped_late = interleave(nc.scalar.copy, "dy_grouped_late", dy_got[1], "dy_pool2")
         fetch_da(0, nc.scalar.copy)
+        silu(2, held("silu_neg2", [P, F], F32, replaces="silu_neg0")[:])
+        lift(2, "slope0")
+        make_da(1, "a0")
         fetch_da(1, nc.scalar.copy)
-        activate(2, "dy_pool3")
         activate(3, "da0")
-        lift(2, "slope1")
         make_dx(0, "a1")
-        dy_late = quantize("dy_late", dy_grouped_late[:], E5M2)
+        dy_late = quantize("dy_late", dy_grouped_late[:], E5M2, "slope1")
+        add_dy(0, 2, LANES, "da1")
         make_dx(1, "dh0")
-        add_dy(0, replaces="da1")
         make_dh(2, dy_late, block(0), "a2")
         make_dh(3, dy_late, block(1), "a3")
         make_slope(2, "da_grouped0")
         lift(3, "dy_grouped_late")
         make_da(2, "dh1")
-        make_slope(3, "activated2")
+        add_dy(0, 0, 2, "lifted2")
+        make_slope(3, "silu_neg2")
         add_dy(1, replaces="slope2")
+        fetch_da(2, nc.vector.tensor_copy)
         make_da(3, "da_turned0")
-        for c in (2, 3):
-            fetch_da(c, nc.vector.tensor_copy)
         make_dx(2, "da_turned1")
+        fetch_da(3, nc.vector.tensor_copy)
         make_dx(3, "c_row")
-        add_dy(2)
+        add_dy(2, 2, LANES)
         add_dy(3, 2, LANES)
 
         out_rows = out_0.rearrange("(p t) n -> p t n", t=LANES)
-        for c in (0, 1):
-            for t in PLANE_ORDER:
-                scalar_scatter(t, c)
+        for t in (2, 3, 0, 1):
+            scalar_scatter(t, 0)
+        for t in PLANE_ORDER[:-1]:
+            scalar_scatter(t, 1)
+        vector_scatter(0, 1)
         vector_scatter(2, 2)
+        add_dy(2, 0, 2)
         add_dy(3, 0, 2)
         for t in PLANE_ORDER[1:]:
             scalar_scatter(t, 2)
-        for t in PLANE_ORDER[:-1]:
+        for t in PLANE_ORDER[:2]:
             vector_scatter(t, 3)
-        scalar_scatter(0, 3)
+        for t in PLANE_ORDER[2:]:
+            scalar_scatter(t, 3)
         for t in PLANE_ORDER:
             queue = nc.scalar if t == PLANE_ORDER[-1] else nc.sync
             queue.dma_start(out=out_rows[:, t, :], in_=out_plane[t][:])

@@ -93,10 +93,10 @@ def tile_attend_gdepth_sil_pl_kernel(tc, xT, dyT, w1, w2, cf, gt, tx, c1, offs, 
 
         nc.sync.dma_start(offsets[:], offs)
         nc.scalar.dma_start(out=tx_pool[LAST:, :], in_=tx[LAST:, :])
+        nc.sync.dma_start(out=x_plane[0][:], in_=x_rows[:, 0, :])
+        nc.sync.dma_start(out=gt_pool[LAST:, :], in_=gt[LAST:, :])
         nc.sync.dma_start(out=cf_col[:], in_=cf.rearrange("(m t) o -> m (t o)", t=LANES))
         nc.sync.dma_start(out=c1_col[:], in_=c1.rearrange("(m t) o -> m (t o)", t=LANES))
-        nc.sync.dma_start(out=gt_pool[LAST:, :], in_=gt[LAST:, :])
-        nc.sync.dma_start(out=x_plane[0][:], in_=x_rows[:, 0, :])
         for s in range(2):
             nc.sync.dma_start(out=w1_raw[s][:], in_=w1.rearrange("(p j) f -> p j f", j=LANES)[:, 2 * s : 2 * s + 2, :])
         for t in range(1, LANES):
@@ -154,9 +154,6 @@ def tile_attend_gdepth_sil_pl_kernel(tc, xT, dyT, w1, w2, cf, gt, tx, c1, offs, 
             scalar_gather(x_got[h][:, 0, :], x_plane[0], half(h))
         cf_row = held("cf_row", [P, F], F32, replaces="x_plane0")
         nc.scalar.copy(out=cf_row[:], in_=cf_turned[:])
-        c_col = held("c_col", [P, LANES], F32)
-        nc.vector.tensor_tensor(out=c_col[:], in0=cf_col[:], in1=c1_col[:], op=ALU.mult)
-        c_row = unit_row("c_row", c_col)
         w1_row = held("w1_rounded", [P, LANES * F], BF16)
         w1_rounded = w1_row[:].rearrange("p (j f) -> p j f", j=LANES)
         for s in range(2):
@@ -164,6 +161,9 @@ def tile_attend_gdepth_sil_pl_kernel(tc, xT, dyT, w1, w2, cf, gt, tx, c1, offs, 
                 out=w1_rounded[:, 2 * s : 2 * s + 2, :].rearrange("p j (u m e) -> p j m u e", u=2, e=2),
                 in_=w1_raw[s][:].rearrange("p j (m u e) -> p j m u e", u=2, e=2),
             )
+        c_col = held("c_col", [P, LANES], F32, replaces="w1_raw1")
+        nc.vector.tensor_tensor(out=c_col[:], in0=cf_col[:], in1=c1_col[:], op=ALU.mult)
+        c_row = unit_row("c_row", c_col)
         w1_grouped = interleave(nc.vector.tensor_copy, "w1_grouped", w1_rounded)
         w1_mx = quantize("w1", w1_grouped[:], E4M3)
         w1_words = w1_row[:].bitcast(F32).rearrange("p (j u m) -> p j u m", j=LANES, u=2)

@@ -169,12 +169,12 @@ def tile_attend_gdepth_sil_pl_kernel(tc, xT, dyT, w1, w2, cf, gt, tx, c1, offs, 
         w1_words = w1_row[:].bitcast(F32).rearrange("p (j u m) -> p j u m", j=LANES, u=2)
 
 
-        def turn_w1(s):
+        def turn_w1(s, replaces=""):
             turned = bank(f"w1_turned{s}")
             for u in range(2):
                 for b in range(2):
                     nc.tensor.transpose(turned[:, block(2 * u + b)], w1_words[:, 2 * s + b, u, :], ident[:])
-            grouped = held(f"w1t_grouped{s}", [P, 2 * P * LANES], BF16)
+            grouped = held(f"w1t_grouped{s}", [P, 2 * P * LANES], BF16, replaces)
             nc.scalar.copy(
                 out=grouped[:].bitcast(F32).rearrange("p (n i u) -> p n u i", u=2, i=RUN),
                 in_=turned[:].rearrange("p (u n i) -> p n u i", u=2, i=RUN),
@@ -187,13 +187,13 @@ def tile_attend_gdepth_sil_pl_kernel(tc, xT, dyT, w1, w2, cf, gt, tx, c1, offs, 
         for t in (1, 2):
             for h in range(2):
                 scalar_gather(x_got[h][:, t, :], x_plane[t], half(h))
-        for c in range(2):
-            vector_gather(x_got[0][:, 3, block(c)], x_plane[3], block(c))
+        vector_gather(x_got[0][:, 3, block(0)], x_plane[3], block(0))
+        scalar_gather(x_got[0][:, 3, block(1)], x_plane[3], block(1))
         scalar_gather(x_got[1][:, 3, :], x_plane[3], half(1))
-        w1t_grouped.append(turn_w1(1))
         x_grouped = [interleave(nc.vector.tensor_copy, f"x_grouped{c}", x_got[0][:, :, block(c)]) for c in range(2)]
         x_mx = [quantize(f"x{n}", x_grouped[n][:], E4M3) for n in range(2)]
-        x_grouped.append(interleave(nc.vector.tensor_copy, "x_grouped2", x_got[1][:], "x_grouped0"))
+        x_grouped.append(interleave(nc.vector.tensor_copy, "x_grouped2", x_got[1][:]))
+        w1t_grouped.append(turn_w1(1, "x_grouped1"))
 
         scaled, tanh_half, silu_neg, lifted, slope, dh, da_turned, da_grouped, dx = ({} for n in range(9))
 

from contextlib import ExitStack

import concourse.mybir as mybir
from concourse.masks import make_identity

F32 = mybir.dt.float32
BF16 = mybir.dt.bfloat16
I32 = mybir.dt.int32
U32 = mybir.dt.uint32
U16 = mybir.dt.uint16
U8 = mybir.dt.uint8
E4M3 = mybir.dt.float8_e4m3fn_x4
E5M2 = mybir.dt.float8_e5m2_x4
ALU = mybir.AluOpType
ACT = mybir.ActivationFunctionType

P = 128
LANES = 4
D = 512
F = 512
T = 1024
N = 512
CHUNKS = N // P
HALF = N // 2
BAND = 16
QUAD = 32
RUN = 4
LAST = P - 1
PLANE_ORDER = (2, 3, 1, 0)
FLOPS = 3 * 2 * D * F * N


def tile_attend_gdepth_sil_pl_kernel(tc, xT, dyT, w1, w2, cf, gt, tx, c1, offs, out_0, out_1, out_2):
    nc = tc.nc
    with ExitStack() as ctx:
        keep = ctx.enter_context(tc.tile_pool(name="keep", bufs=1))
        psum = ctx.enter_context(tc.psum_pool(name="psum", bufs=1))
        place = {}

        def held(name, shape, dtype, replaces=""):
            place[name] = place.get(replaces, name)
            return keep.tile(shape, dtype, name=name, tag=place[name], align_bytes=64)

        def bank(name, replaces=""):
            place[name] = place.get(replaces, name)
            return psum.tile([P, 512], F32, name=name, tag=place[name])

        def block(n):
            return slice(n * P, (n + 1) * P)

        def half(h):
            return slice(h * HALF, (h + 1) * HALF)

        def entries(slots):
            return offsets[:, slots.start // BAND : slots.stop // BAND]

        def quantize(name, values, fmt, replaces=""):
            width = values.shape[1] // LANES
            codes = held(name + "_codes", [P, width], U32, replaces)
            scales = held(name + "_scales", [P, width], U8)
            nc.vector.quantize_mx(out=codes[:].bitcast(fmt), scales=scales[:], in_=values)
            return codes, scales

        def product(out, still, still_fmt, cols, moving, moving_fmt):
            nc.tensor.matmul_mx(
                out=out,
                lhsT=still[0][:, cols].bitcast(still_fmt),
                lhsT_scale=still[1][:, cols],
                rhs=moving[0][:].bitcast(moving_fmt),
                rhs_scale=moving[1][:],
                start=True,
                stop=True,
            )

        def scalar_gather(out, window, slots):
            nc.scalar.activation(out=out, in_=window[:].indirect(entries(slots)), func=ACT.Copy)

        def vector_gather(out, window, slots):
            nc.vector.tensor_copy(out=out, in_=window[:].indirect(entries(slots)))

        offsets = keep.tile([P, N // BAND], U16, name="offsets")
        tx_pool = held("tx_pool", [P, T], F32)
        gt_pool = held("gt_pool", [P, T], F32)
        cf_col = held("cf_col", [P, LANES], F32)
        c1_col = held("c1_col", [P, LANES], F32)
        x_plane = [held(f"x_plane{t}", [P, T], F32) for t in range(LANES)]
        w1_raw = [held(f"w1_raw{s}", [P, 2, F], F32) for s in range(2)]
        w2_raw = held("w2_raw", [P, LANES, F], F32)
        dy_pool = [held(f"dy_pool{t}", [P, T], F32) for t in range(LANES)]
        out_plane = [held(f"out_plane{t}", [P, T], F32) for t in range(LANES)]
        x_rows = xT.rearrange("(p t) n -> p t n", t=LANES)
        dy_rows = dyT.rearrange("(p t) n -> p t n", t=LANES)

        nc.sync.dma_start(offsets[:], offs)
        nc.scalar.dma_start(out=tx_pool[LAST:, :], in_=tx[LAST:, :])
        nc.sync.dma_start(out=x_plane[0][:], in_=x_rows[:, 0, :])
        nc.sync.dma_start(out=gt_pool[LAST:, :], in_=gt[LAST:, :])
        nc.sync.dma_start(out=cf_col[:], in_=cf.rearrange("(m t) o -> m (t o)", t=LANES))
        nc.sync.dma_start(out=c1_col[:], in_=c1.rearrange("(m t) o -> m (t o)", t=LANES))
        for s in range(2):
            nc.sync.dma_start(out=w1_raw[s][:], in_=w1.rearrange("(p j) f -> p j f", j=LANES)[:, 2 * s : 2 * s + 2, :])
        for t in range(1, LANES):
            nc.sync.dma_start(out=x_plane[t][:], in_=x_rows[:, t, :])
        nc.sync.dma_start(out=dy_pool[0][:], in_=dy_rows[:, 0, :])
        nc.sync.dma_start(out=w2_raw[:], in_=w2.rearrange("(p j) f -> p j f", j=LANES))
        for t in range(1, LANES):
            nc.sync.dma_start(out=dy_pool[t][:], in_=dy_rows[:, t, :])
        for t in PLANE_ORDER:
            nc.sync.dma_start(out=out_plane[t][:], in_=dy_rows[:, t, :])

        ident = held("ident", [P, P], F32)
        seed = held("seed", [P, 1], F32)
        zeros = held("zeros", [P, 1], F32)
        nc.vector.memset(seed[:], 0.0)
        nc.scalar.activation(out=zeros[:], in_=seed[:], func=ACT.Silu)
        nc.vector.memset(ident[:], 0.0)
        make_identity(nc, ident[:], nomemset=True)
        nc.vector.memset(tx_pool[:LAST, :], 0.0)
        nc.vector.memset(gt_pool[:LAST, :], 0.0)

        def slot_columns(name, pool_tile, gather, replaces=""):
            got = held(name + "_got", [P, N], F32)
            gather(got[:], pool_tile, slice(0, N))
            turned = bank(name + "_turned", replaces)
            for c in range(CHUNKS):
                nc.tensor.transpose(turned[:, block(c)], got[:, block(c)], ident[:])
            return turned[:].rearrange("p (c r) -> p c r", r=P)[:, :, LAST]

        tx_cols = slot_columns("tx", tx_pool, vector_gather)

        def unit_row(name, column):
            row = bank(name)
            places = row[:].rearrange("p (u m e) -> p u e m", u=2, e=2)
            for t in range(LANES):
                nc.tensor.transpose(places[:, t // 2, t % 2, :], column[:, t : t + 1].to_broadcast([P, P]), ident[:])
            return row

        cf_turned = unit_row("cf_turned", cf_col)
        tx_neg = held("tx_neg", [P, CHUNKS], F32)
        tx_half = held("tx_half", [P, CHUNKS], F32)
        nc.vector.tensor_scalar(out=tx_neg[:], in0=tx_cols, scalar1=-1.0, scalar2=zeros[:], op0=ALU.mult, op1=ALU.add)
        nc.vector.tensor_scalar(out=tx_half[:], in0=tx_cols, scalar1=0.5, scalar2=None, op0=ALU.mult)

        def interleave(copy, name, planes, replaces=""):
            grouped = held(name, [P, planes.shape[2] * LANES], BF16, replaces)
            copy(
                out=grouped[:].rearrange("p (n i t) -> p n t i", i=RUN, t=LANES),
                in_=planes.rearrange("p t (n i) -> p n t i", i=RUN),
            )
            return grouped

        x_got = [held(f"x_got{h}", [P, LANES, HALF], BF16) for h in range(2)]
        for h in range(2):
            scalar_gather(x_got[h][:, 0, :], x_plane[0], half(h))
        cf_row = held("cf_row", [P, F], F32, replaces="x_plane0")
        nc.scalar.copy(out=cf_row[:], in_=cf_turned[:])
        w1_row = held("w1_rounded", [P, LANES * F], BF16)
        w1_rounded = w1_row[:].rearrange("p (j f) -> p j f", j=LANES)
        for s in range(2):
            nc.vector.tensor_copy(
                out=w1_rounded[:, 2 * s : 2 * s + 2, :].rearrange("p j (u m e) -> p j m u e", u=2, e=2),
                in_=w1_raw[s][:].rearrange("p j (m u e) -> p j m u e", u=2, e=2),
            )
        c_col = held("c_col", [P, LANES], F32, replaces="w1_raw1")
        nc.vector.tensor_tensor(out=c_col[:], in0=cf_col[:], in1=c1_col[:], op=ALU.mult)
        c_row = unit_row("c_row", c_col)
        w1_grouped = interleave(nc.vector.tensor_copy, "w1_grouped", w1_rounded)
        w1_mx = quantize("w1", w1_grouped[:], E4M3)
        w1_words = w1_row[:].bitcast(F32).rearrange("p (j u m) -> p j u m", j=LANES, u=2)


        def turn_w1(s, replaces=""):
            turned = bank(f"w1_turned{s}")
            for u in range(2):
                for b in range(2):
                    nc.tensor.transpose(turned[:, block(2 * u + b)], w1_words[:, 2 * s + b, u, :], ident[:])
            grouped = held(f"w1t_grouped{s}", [P, 2 * P * LANES], BF16, replaces)
            nc.scalar.copy(
                out=grouped[:].bitcast(F32).rearrange("p (n i u) -> p n u i", u=2, i=RUN),
                in_=turned[:].rearrange("p (u n i) -> p n u i", u=2, i=RUN),
            )
            return grouped

        w1t_grouped = [turn_w1(0)]
        w1t_mx = [quantize("w1t0", w1t_grouped[0][:], E4M3)]
        gt_cols = slot_columns("gt", gt_pool, vector_gather, "w1_turned0")
        for t in (1, 2):
            for h in range(2):
                scalar_gather(x_got[h][:, t, :], x_plane[t], half(h))
        vector_gather(x_got[0][:, 3, block(0)], x_plane[3], block(0))
        scalar_gather(x_got[0][:, 3, block(1)], x_plane[3], block(1))
        scalar_gather(x_got[1][:, 3, :], x_plane[3], half(1))
        x_grouped = [interleave(nc.vector.tensor_copy, f"x_grouped{c}", x_got[0][:, :, block(c)]) for c in range(2)]
        x_mx = [quantize(f"x{n}", x_grouped[n][:], E4M3) for n in range(2)]
        x_grouped.append(interleave(nc.vector.tensor_copy, "x_grouped2", x_got[1][:]))
        w1t_grouped.append(turn_w1(1, "x_grouped1"))

        scaled, tanh_half, silu_neg, lifted, slope, dh, da_turned, da_grouped, dx = ({} for n in range(9))

        def first_product(c, replaces):
            a = bank(f"a{c}", replaces)
            product(a[:], x_mx[min(c, 2)], E4M3, block(max(c - 2, 0)), w1_mx, E4M3)
            return a

        def scale(c, a, out):
            scaled[c] = out
            nc.vector.tensor_tensor(out=out, in0=a[:], in1=cf_row[:], op=ALU.mult)

        def tanh(c, out):
            tanh_half[c] = out
            nc.scalar.activation(out=out, in_=scaled[c], func=ACT.Tanh, scale=tx_half[:, c : c + 1])

        def silu(c, out):
            silu_neg[c] = out
            nc.scalar.activation(out=out, in_=scaled[c], func=ACT.Silu, scale=tx_neg[:, c : c + 1])

        def activate(c, replaces=""):
            both = held(f"activated{c}", [P, 2, F], F32, replaces)
            tanh(c, both[:, 0, :])
            silu(c, both[:, 1, :])

        def lift(c, replaces=""):
            lifted[c] = held(f"lifted{c}", [P, F], F32, replaces)
            nc.vector.scalar_tensor_tensor(
                out=lifted[c][:], in0=tanh_half[c], scalar=1.0, in1=c_row[:], op0=ALU.add, op1=ALU.mult
            )

        def make_slope(c, replaces=""):
            slope[c] = held(f"slope{c}", [P, F], F32, replaces)
            nc.vector.scalar_tensor_tensor(
                out=slope[c][:], in0=silu_neg[c], scalar=-1.0, in1=lifted[c][:], op0=ALU.add, op1=ALU.mult
            )

        def make_dh(c, dy_mx, cols, replaces):
            dh[c] = bank(f"dh{c}", replaces)
            product(dh[c][:], dy_mx, E5M2, cols, w2_mx, E4M3)

        def make_da(c, replaces, after=""):
            da = held(f"da{c}", [P, F], BF16, after)
            nc.vector.scalar_tensor_tensor(
                out=da[:], in0=dh[c][:], scalar=slot_factor[:, c : c + 1], in1=slope[c][:], op0=ALU.mult, op1=ALU.mult
            )
            da_turned[c] = bank(f"da_turned{c}", replaces)
            for u in range(2):
                nc.tensor.transpose(da_turned[c][:, block(u)], da[:].bitcast(F32)[:, block(u)], ident[:])

        def fetch_da(c, copy, replaces=""):
            da_grouped[c] = held(f"da_grouped{c}", [P, P * LANES], BF16, replaces)
            copy(
                out=da_grouped[c][:].bitcast(F32).rearrange("p (n i u) -> p n u i", u=2, i=RUN),
                in_=da_turned[c][:, half(0)].rearrange("p (u n i) -> p n u i", u=2, i=RUN),
            )

        def make_dx(c, replaces):
            da_mx = quantize(f"da{c}", da_grouped[c][:], E5M2)
            dx[c] = bank(f"dx{c}", replaces)
            for t in range(LANES):
                product(dx[c][:, block(t)], w1t_mx[t // 2], E4M3, block(t % 2), da_mx, E5M2)

        new_cols = {}

        def add_dy(c, first=0, last=LANES, replaces=""):
            sums = held(f"new_cols{c}{first}", [P, last - first, P], F32, replaces)
            nc.vector.tensor_tensor(
                out=sums[:],
                in0=dx[c][:].rearrange("p (t i) -> p t i", t=LANES)[:, first:last, :],
                in1=dy_got[c // 2][:, first:last, block(c % 2)],
                op=ALU.add,
            )
            for t in range(first, last):
                new_cols[t, c] = sums[:, t - first, :]

        def scalar_scatter(t, c):
            nc.scalar.activation(out=out_plane[t][:].indirect(entries(block(c))), in_=new_cols[t, c], func=ACT.Copy)

        def vector_scatter(t, c):
            nc.vector.tensor_copy(out=out_plane[t][:].indirect(entries(block(c))), in_=new_cols[t, c])

        slot_factor = held("slot_factor", [P, CHUNKS], F32, replaces="x_got0")
        nc.vector.scalar_tensor_tensor(
            out=slot_factor[:], in0=gt_cols, scalar=0.5, in1=tx_neg[:], op0=ALU.mult, op1=ALU.mult
        )
        x_mx.append(quantize("x2", x_grouped[2][:], E4M3))
        a = [first_product(c, replaces) for c, replaces in enumerate(("", "gt_turned", "", "tx_turned"))]
        dy_late_row = held("dy_got1", [P, LANES * HALF], F32)
        scale(0, a[0], held("scaled0", [P, F], F32, replaces="x_got1")[:])
        scale(1, a[1], dy_late_row[:, HALF : HALF + F])
        for c in (2, 3):
            scale(c, a[c], held(f"scaled{c}", [P, F], F32)[:])
        w2_grouped = held("w2_grouped", [P, F * LANES], BF16, replaces="x_grouped2")
        nc.gpsimd.tensor_scalar(
            out=w2_grouped[:].rearrange("p (u m e j) -> p m u e j", u=2, e=2, j=LANES),
            in0=w2_raw[:].rearrange("p j (m u e) -> p m u e j", u=2, e=2),
            scalar1=1.0,
            scalar2=0.0,
            op0=ALU.mult,
            op1=ALU.add,
        )
        tanh(0, held("tanh_half0", [P, F], F32)[:])
        silu(0, held("silu_neg0", [P, F], F32)[:])
        tanh(1, held("tanh_half1", [P, F], F32)[:])
        dy_got = [held("dy_got0", [P, LANES, HALF], F32, replaces="x_plane3")]
        for t in range(LANES - 1):
            scalar_gather(dy_got[0][:, t, :], dy_pool[t], half(0))
        silu(1, held("silu_neg1", [P, F], F32)[:])
        lift(0)
        lift(1)
        for c in range(2):
            vector_gather(dy_got[0][:, LANES - 1, block(c)], dy_pool[LANES - 1], block(c))
        w2_mx = quantize("w2", w2_grouped[:], E4M3)
        dy_grouped = [interleave(nc.vector.tensor_copy, f"dy_grouped{c}", dy_got[0][:, :, block(c)]) for c in range(2)]
        dy_mx = [quantize(f"dy{c}", dy_grouped[c][:], E5M2) for c in range(2)]
        make_dh(0, dy_mx[0], block(0), "")
        make_dh(1, dy_mx[1], block(0), "cf_turned")
        make_slope(0, "dy_grouped0")
        w1t_mx.append(quantize("w1t1", w1t_grouped[1][:], E4M3, "dy_grouped1"))
        make_da(0, "w1_turned1")
        make_slope(1, "w1t_grouped1")
        dy_got.append(dy_late_row[:].rearrange("p (t i) -> p t i", t=LANES))
        for t in range(LANES):
            scalar_gather(dy_got[1][:, t, :], dy_pool[t], half(1))
        tanh(2, held("tanh_half2", [P, F], F32, replaces="dy_pool3")[:])
        dy_grouped_late = interleave(nc.scalar.copy, "dy_grouped_late", dy_got[1], "dy_pool2")
        fetch_da(0, nc.scalar.copy)
        silu(2, held("silu_neg2", [P, F], F32, replaces="silu_neg0")[:])
        lift(2, "slope0")
        make_da(1, "a0")
        fetch_da(1, nc.scalar.copy)
        activate(3, "da0")
        make_dx(0, "a1")
        dy_late = quantize("dy_late", dy_grouped_late[:], E5M2, "slope1")
        add_dy(0, 2, LANES, "da1")
        make_dx(1, "dh0")
        make_dh(2, dy_late, block(0), "a2")
        make_dh(3, dy_late, block(1), "a3")
        make_slope(2, "da_grouped0")
        lift(3, "dy_grouped_late")
        make_da(2, "dh1")
        add_dy(0, 0, 2, "lifted2")
        make_slope(3, "silu_neg2")
        add_dy(1, replaces="slope2")
        fetch_da(2, nc.vector.tensor_copy)
        make_da(3, "da_turned0")
        make_dx(2, "da_turned1")
        fetch_da(3, nc.vector.tensor_copy)
        make_dx(3, "c_row")
        add_dy(2, 2, LANES)
        add_dy(3, 2, LANES)

        out_rows = out_0.rearrange("(p t) n -> p t n", t=LANES)
        for t in (2, 3, 0, 1):
            scalar_scatter(t, 0)
        for t in PLANE_ORDER[:-1]:
            scalar_scatter(t, 1)
        vector_scatter(0, 1)
        vector_scatter(2, 2)
        add_dy(2, 0, 2)
        add_dy(3, 0, 2)
        for t in PLANE_ORDER[1:]:
            scalar_scatter(t, 2)
        for t in PLANE_ORDER[:2]:
            vector_scatter(t, 3)
        for t in PLANE_ORDER[2:]:
            scalar_scatter(t, 3)
        for t in PLANE_ORDER:
            queue = nc.scalar if t == PLANE_ORDER[-1] else nc.sync
            queue.dma_start(out=out_rows[:, t, :], in_=out_plane[t][:])

        out_pairs = held("out_pairs", [P, 2, 2 * T], BF16)
        out_lane = [out_pairs[:, t // 2, :].rearrange("p (n e) -> p n e", e=2)[:, :, t % 2] for t in range(LANES)]
        out_grouped = held("out_grouped", [P, T * LANES], BF16)
        woven = out_grouped[:].bitcast(U32).rearrange("p (n i u) -> p n u i", u=2, i=RUN)
        pair_words = out_pairs[:].bitcast(U32).rearrange("p u (n i) -> p n u i", i=RUN)
        quarters = [slice(n * T // 4, (n + 1) * T // 4) for n in range(4)]
        runs = [slice(cols.start // RUN, cols.stop // RUN) for cols in quarters]
        split = 5 * T // 8
        for t in PLANE_ORDER[:2]:
            nc.vector.tensor_copy(out=out_lane[t], in_=out_plane[t][:])
        for t, cuts in zip(PLANE_ORDER[2:], ((0, split), (0, T // 4, split))):
            for first, last in zip(cuts, cuts[1:]):
                nc.vector.tensor_copy(out=out_lane[t][:, first:last], in_=out_plane[t][:, first:last])
            nc.scalar.copy(out=out_lane[t][:, split:], in_=out_plane[t][:, split:])
        for part in runs[:2]:
            nc.vector.tensor_copy(out=woven[:, part].bitcast(I32), in_=pair_words[:, part].bitcast(I32))
        for part in runs[:1:-1]:
            nc.scalar.copy(out=woven[:, part], in_=pair_words[:, part])

        out_codes = held("out_codes", [P, T], U32)
        out_scales = held("out_scales", [P, T], U8)
        words_hbm = out_1[0].rearrange("p n l -> p (n l)").bitcast(I32)
        for cols in quarters[:2] + quarters[:1:-1]:
            nc.vector.quantize_mx(
                out=out_codes[:, cols].bitcast(E4M3),
                scales=out_scales[:, cols],
                in_=out_grouped[:, cols.start * LANES : cols.stop * LANES],
            )
            nc.sync.dma_start(out=words_hbm[:, cols], in_=out_codes[:, cols].bitcast(I32))
        scales_hbm = out_2[0].bitcast(I32)
        for q in range(P // QUAD):
            queue = (nc.scalar, nc.sync)[q % 2]
            queue.dma_start(out=scales_hbm[4 * q : 4 * q + 4, :], in_=out_scales[QUAD * q : QUAD * q + 4, :].bitcast(I32))
